import numpy as np, ml_dtypes
CORES = [16,17,18,19,32,33,34,35]
N = 8
import mx_ref
BF = ml_dtypes.bfloat16
def gentries(a):
    return np.ascontiguousarray(a.reshape(8, 16, -1).transpose(0, 2, 1)).reshape(8, -1)
def gtable(e):
    e = np.asarray(e); return np.ascontiguousarray(e.reshape(8, -1, 16).transpose(0, 2, 1)).reshape(128, -1).astype(np.int32)
def gcols(t, e):
    v = np.concatenate([t.reshape(8, 16, -1, 4), np.zeros((8, 16, 1, 4), BF)], axis=2)
    return np.ascontiguousarray(np.stack([v[g][:, e[g]] for g in range(8)])).reshape(128, -1)
def tile(rs):
    return np.stack(rs, axis=2).reshape(128, -1).astype(BF)
def pick(q, e):
    c = np.concatenate([q[0].reshape(128, -1, 4), np.zeros((128, 1, 4), np.uint8)], axis=1); s = np.concatenate([q[1], np.ones((16, 1), np.uint8)], axis=1)
    return (np.ascontiguousarray(c[:, e].reshape(128, -1)), np.ascontiguousarray(s[:, e]))
def join(*qs):
    return (np.concatenate([q[0] for q in qs], axis=1), np.concatenate([q[1] for q in qs], axis=1))
def put(q, e, v):
    c, s = q[0].reshape(128, -1, 4).copy(), q[1].copy(); c[:, e] = v[0].reshape(128, -1, 4); s[:, e] = v[1]
    return (c.reshape(128, -1), s)
def pk(c, s):
    return (np.ascontiguousarray(c), mx_ref.live(s))
def emit(q):
    return q[0], q[1]
def packed(v, rng):
    q = [mx_ref.quantize(np.ascontiguousarray(v[r])) for r in range(N)]
    return np.stack([a for a, b in q]), np.stack([mx_ref.plane(b, rng) for a, b in q])
def values_of_codes():
    e, c = np.zeros((128, 128, 4), np.float32), np.zeros((128, 2, 4), np.uint8)
    e[np.arange(128), np.arange(128), 0] = 1
    c[:127, :, 0] = np.arange(256).reshape(2, 128).T[:127]
    return mx_ref.matmul(mx_ref.quantize(e.reshape(128, 512).astype(BF)), (c.reshape(128, 8), np.full((16, 2), 127, np.uint8))).T.reshape(-1).astype(np.float64)
CODE_VALUE, SCALE_VALUE = values_of_codes(), 2.0 ** (np.arange(256) - 127.0)
def decode(q):
    return (CODE_VALUE[q[0]].reshape(16, 8, -1, 4) * SCALE_VALUE[q[1]][:, None, :, None] + 0.0).reshape(128, -1).astype(np.float32)
def f(rng, *shape):
    return mx_ref.flush((rng.standard_normal(shape, dtype=np.float32) * np.exp2(rng.integers(-2, 3, shape[:-1] + (1,)))).astype(BF))
def wide(rng, *shape, cols=0):
    v = rng.standard_normal(shape, dtype=np.float32) * np.exp2(rng.integers(-12, 13, shape)).astype(np.float32)
    if cols: v *= np.repeat(np.exp2(rng.integers(-cols, cols + 1, shape[:-2] + (1, shape[-1] // 4))) * (rng.random(shape[:-2] + (1, shape[-1] // 4)) > 0.0625), 4, axis=-1).astype(np.float32)
    return mx_ref.flush(v.astype(BF))
C = 320
STEP = [1, 2, 4]
GAPS = [[2, 4, 5, 6, 7, 8], [3, 4, 5, 6, 7, 8]]
def numbers_of(rng):
    return {"x": np.array(f(rng, N, 128, 4 * C)), "u": np.array(f(rng, N, 128, 512)), "v": np.array(f(rng, N, 128, 512))}
def full(rng, k):
    h = 128 + rng.permutation(128)[:k]
    low = rng.permutation(np.concatenate([2 * h, 2 * h + 1]))[:C - 127 - k]
    return np.sort(np.concatenate([np.arange(1, 128), h, low]))
def below(h):
    return np.concatenate([np.arange(h << n, (h + 1) << n) for n in range(10 - h.bit_length())])
def lean(side, slot):
    c = 3 - side
    return np.sort(np.concatenate([[1], below(2 + side), np.concatenate([[c], below(2 * c + slot)])[:C - 256]]))
def ragged(rng, first):
    cuts, left = [], 511 - C
    for n, most in [(n, 1) for n in first] + [(n, 9) for n in range(3, 9)]:
        size = 2 ** (9 - n) - 1
        k = min(most, left // size)
        cuts += [n] * k
        left -= k * size
    keep = np.arange(512) > 0
    for n in sorted(cuts):
        h = np.arange(2 ** n, 2 ** (n + 1))
        h = int(rng.choice(h[keep[h] & keep[h ^ 1]]))
        keep[below(h)] = False
    return np.flatnonzero(keep)
def grown(h, places):
    at = np.zeros(512, np.int64)
    at[h] = places
    e = np.zeros(C, np.int64)
    e[places[1:]] = 2 * at[h[1:] >> 1] + (h[1:] & 1)
    return e
def shuffled(rng):
    return np.concatenate([[0], 1 + rng.permutation(C - 1)])
def trees(rng):
    t = np.stack([np.stack([grown(full(rng, int(rng.integers(112, 129))), shuffled(rng)) for g in range(8)]) for r in range(N)])
    o = rng.permutation(8)
    for r in range(N):
        for n in range(2): t[r, o[(r + 4 * n) % 8]] = grown(ragged(rng, GAPS[n]), shuffled(rng))
    return t
def stored(t):
    return {"se": np.stack([gtable(t[r]) for r in range(N)])}
def weights(rng, w):
    c, s = packed(np.ascontiguousarray(w).reshape(N, 128, 2048), rng)
    return {"wc": c, "ws": s}
def layers(rng, still=[], pairs=False):
    w = np.array(f(rng, N, 128, 2048)).reshape(N, 8, 16, 4, 8, 16, 4)
    for i in still:
        w[:, :, i] = 0
        w[:, :, :, :, :, i] = 0
    if pairs:
        w[:, :, :, :, :, 8:] = 0
        for g in range(8):
            w[:, g, 8, 0, g, 8, 0] = -28.0
            for b in range(4): w[:, g, 10, b, g, 9, 0] = -2.0 ** (b - 5)
    return weights(rng, w)
def setup_inputs(rng):
    return {**numbers_of(rng), **stored(trees(rng)), **layers(rng)}
def setup_inputs_ties(rng):
    d = numbers_of(rng)
    o = rng.permutation(N)
    k = rng.integers(-1, 2, (N, 8, C)).astype(np.float32)
    k[o[1]] = -1
    x = d["x"].reshape(N, 8, 16, C, 4)
    x[:, :, 0] = 0
    x[:, :, 0, :, 0] = k.astype(BF)
    a = np.exp2(rng.integers(-3, 4, (1, 8, 1)).astype(np.float32))
    x[:, :, 8:] = 0
    x[:, :, 8, :, 0] = (-1.125 * a).astype(BF)
    x[:, :, 10, :, 0] = (-0.0703125 * a).astype(BF)
    c = np.ones(N, np.float32)
    c[o[0]] = 0
    c[o[2]] = -1
    u = d["u"].reshape(N, 128, 128, 4)
    u[:, :, ::16] = 0
    for h in range(0, 128, 16): u[:, h, h, 0] = c.astype(BF)
    return {"x": x.reshape(N, 128, 4 * C), "u": u.reshape(N, 128, 512), "v": d["v"], **stored(trees(rng)), **layers(rng, [0], True)}
def setup_inputs_near(rng):
    d = numbers_of(rng)
    o = rng.permutation(N) % 2
    k = np.where(o == 0, 2.0 ** -30, 1.0).astype(np.float32)
    x = np.zeros((N, 8, 16, C, 4), np.float32)
    s = rng.integers(-1, 2, (N, 8, C)) * k[:, None, None]
    x[:, :, 0, :, 0] = 1.125 * s
    x[:, :, 1, :, 0] = -1.25 * s
    s = rng.choice([-1.0, 1.0], (N, 8, C)) * 2.0 ** -30
    x[:, :, 8, :, 0] = 1.125 * s
    x[:, :, 9, :, 0] = -1.25 * s
    x[:, :, 2, :, 0] = 2.0 ** -28
    x[:, :, 10, :, 0] = 2.0 ** -28
    for r in range(N):
        at = [0, C - 1, int(rng.integers(C)), int(rng.integers(C))]
        for g, j in zip(rng.permutation(8)[:4], at): x[r, g, 0, j, 0] = 2.0 ** 30 * rng.choice([-1.0, 1.0])
    u = d["u"].astype(np.float32).reshape(N, 128, 128, 4)
    u[:, :, ::16] = 0
    w = np.zeros((N, 128, 4, 128, 4), np.float32)
    for h in range(0, 128, 16):
        u[:, h, h, 0] = 1.125 * k
        u[:, h + 1, h, 0] = k
        w[:, h + 8, 0, h, 0] = 0.5
        w[:, h + 9, 0, h + 1, 0] = 0.5
        w[:, h + 10, 0, h + 2, 0] = 32.0
        w[:, h + 10, 0, h + 10, 0] = 32.0
    return {"x": x.reshape(N, 128, 4 * C).astype(BF), "u": u.reshape(N, 128, 512).astype(BF), "v": d["v"], **stored(trees(rng)), **weights(rng, w.astype(BF))}
def setup_inputs_odd(rng):
    d = numbers_of(rng)
    x = (1.0 + (2 * rng.integers(0, 64, (N, 16, 8, C, 4)) + 1) * 2.0 ** -7) * np.exp2(-rng.integers(0, 7, (N, 16, 8, C, 4)).astype(np.float64)) * rng.choice([-1.0, 1.0], (N, 16, 8, C, 4))
    x[:, :, 0, :, 0] = 1.96875 * 2.0 ** 8 * rng.choice([-1.0, 1.0], (N, 16, C))
    e = rng.choice([-1.0, 1.0], (N, 8, C)) * 2.0 ** -5
    x[:, ::2, 1, :, 0] = 1.125 * e
    x[:, ::2, 2, :, 0] = -e
    u = d["u"].reshape(N, 128, 128, 4)
    u[:, :, ::16] = 0
    for h in range(0, 128, 16): u[:, h + 1:h + 3, h, 0] = 1
    return {"x": x.astype(np.float32).reshape(N, 128, 4 * C).astype(BF), "u": u.reshape(N, 128, 512), "v": d["v"], **stored(trees(rng)), **layers(rng, [0, 8])}
def setup_inputs_ends(rng):
    d = numbers_of(rng)
    o, e = rng.permutation(N) % 4, rng.permutation(N) % 4
    x = np.zeros((N, 128, C, 4))
    u = d["u"].astype(np.float32).reshape(N, 128, 128, 4)
    v = d["v"].astype(np.float32)
    w = np.zeros((N, 128, 4, 128, 4), np.float32)
    t = np.zeros((N, 8, C), np.int64)
    i = np.arange(128)
    last = i % 16 == 15
    for r in range(N):
        h = rng.permutation(8)
        c = np.where(h < 2, 0.0, h % 2 * 2.0 - 1.0)[None, :, None]
        a = -(0.9 + 0.1 * rng.random((128, C, 4))) * 2.0 ** 30
        if o[r] == 1: a = a * rng.choice([-1.0, 1.0], (C, 1))
        if o[r] == 2: a = -(1.0 + 0.125 * rng.integers(0, 8, (128, C, 4))) * 2.0 ** -30
        if o[r] == 3: a = d["x"][r].astype(np.float32).reshape(128, C, 4)[:, :1]
        x[r] = a
        if o[r] < 2:
            x[r, last] = 2.0 ** -30
            u[r, :, ::16] = c * (0.9 + 0.1 * rng.random((128, 8, 4))) * 2.0 ** 30
            v[r] = rng.choice([-1.0, 1.0], (128, 512)) * (0.9 + 0.1 * rng.random((128, 512))) * 2.0 ** 30
        if o[r] == 2:
            u[r, :, ::16] = c * (1.0 + 0.125 * rng.integers(0, 8, (128, 8, 4))) * 2.0 ** -30
            v[r] = rng.choice([-1.0, 1.0], (128, 512)) * (1.0 + 0.125 * rng.integers(0, 8, (128, 512))) * 2.0 ** -30
        if o[r] == 3: u[r, :, ::16] *= np.abs(c).astype(np.float32)
        k = np.where(last, [32.0, 32.0, 256.0, 2.0 ** -8][o[r]], 32.0)
        for b in range(4): w[r, i, b, i, b] = k
        for g in range(8):
            if e[r] == 0: t[r, g] = grown(lean(0, g % 2), np.arange(C))
            if e[r] == 1: t[r, g] = grown(lean(1, g % 2), np.concatenate([[0], np.arange(C - 1, 0, -1)]))
            if e[r] >= 2: t[r, g] = grown(ragged(rng, GAPS[g - 6]) if g >= 6 else full(rng, 128 if e[r] == 2 else (C - 125) // 3), shuffled(rng))
    return {"x": x.astype(np.float32).reshape(N, 128, 4 * C).astype(BF), "u": u.reshape(N, 128, 512).astype(BF), "v": v.astype(BF), **stored(t), **weights(rng, w.astype(BF))}
def setup_inputs_spread(rng):
    d = setup_inputs(rng)
    d["x"] = wide(rng, N, 128, 4 * C, cols=6)
    return d
def check_inputs(d):
    b = []
    for k in ("x", "u", "v"):
        a = np.abs(d[k].astype(np.float32))
        if not (np.isfinite(a).all() and ((a == 0) | (a >= 2.0 ** -30) & (a <= 2.0 ** 30)).all()): b.append("a value of " + k)
    e = np.stack([gentries(d["se"][r]) for r in range(N)])
    if not ((e >= 0) & (e < 2 * C)).all(): b.append("an entry of se")
    else:
        if e[:, :, 0].any(): b.append("se: entry 0")
        if (np.diff(np.sort(e[:, :, 1:], axis=2), axis=2) == 0).any(): b.append("se: equal seats")
        a = e >> 1
        for n in range(7): a = np.take_along_axis(e >> 1, a, 2)
        if a.any(): b.append("se: a place from which eight steps don't lead to place 0")
    none, least, most = [emit(mx_ref.quantize(np.full((128, 16), k, np.float32).astype(BF)))[1][0, 0] for k in (0.0, 2.0 ** -8, 2.0 ** 8)]
    for r in range(N):
        if ((d["wc"][r] == 0x7F) | (d["wc"][r] == 0xFF)).any(): b.append("wc: a code that is no number")
        s = mx_ref.live(d["ws"][r])
        if ((s != none) & ((s < least) | (s > most))).any(): b.append("ws: a scale out of range")
        if (((d["wc"][r].reshape(16, 8, 512, 4) & 0x7F) != 0) & (s == none)[:, None, :, None]).any(): b.append("wc: a code other than zero under the scale of zeros")
    return b
def reference(x, u, v, se, wc, ws):
    qu = [mx_ref.quantize(u[r]) for r in range(N)]
    lay = [pk(wc[r], ws[r]) for r in range(N)]
    seat = [gentries(se[r]).astype(np.int64) for r in range(N)]
    par = [seat[r] >> 1 for r in range(N)]
    now = [x[r] for r in range(N)]
    y, im = np.zeros((N, 128, C), np.float32), np.zeros((N, 8, C), np.float32)
    oc, osc = np.zeros((N, 128, 4 * C), np.uint8), np.zeros((N, 16, C), np.uint8)
    for step in STEP:
        q = [mx_ref.quantize(now[r]) for r in range(N)]
        layered, child = [], []
        for r in range(N):
            layered.append(tile([mx_ref.matmul(pick(lay[r], np.arange(128 * b, 128 * b + 128)), q[r]) * np.float32(0.03125) for b in range(4)]))
            turn = (mx_ref.matmul(qu[r], q[r])[::16] < 0).astype(np.int64)
            seat[r] = seat[r] ^ np.take_along_axis(turn, par[r], 1)
            c = np.full((8, 2 * C), -1, np.int64)
            np.put_along_axis(c, seat[r][:, 1:], np.tile(np.arange(1, C), (8, 1)), 1)
            child.append(c)
        for r in range(N):
            p = r ^ step
            m = np.zeros((8, C), np.int64)
            for depth in range(8):
                at = np.take_along_axis(m, par[r], 1)
                c = np.take_along_axis(child[p], 2 * at + (seat[r] & 1), 1)
                m = np.where(c < 0, at, c)
                m[:, 0] = 0
            e = mx_ref.quantize(gcols(layered[p], m))
            above = gcols(decode(q[r]).astype(BF), par[r]).astype(np.float32)
            now[r] = ((decode(e) + above) * np.float32(0.5)).astype(BF)
            im[r] = m
    for r in range(N):
        z = mx_ref.quantize(now[r])
        y[r] = mx_ref.matmul(mx_ref.quantize(v[r]), z)
        oc[r], osc[r] = emit(z)
    return {"y": y, "im": im, "oc": oc, "osc": osc}

@@ -1,0 +1,454 @@
+import numpy as np
+from concourse.mybir import dt, AluOpType, AxisListType, ActivationFunctionType
+
+C = 320
+STEP = [1, 2, 4]
+PARTS = [(0, 192), (192, 320)]
+A = AluOpType
+F = ActivationFunctionType
+
+SCRATCH = {"ps": ("psum", [128, 4096], "float32")}
+for _n, _w, _d in (
+        ("x0", 1280, "bfloat16"), ("ub", 512, "bfloat16"), ("vb", 512, "bfloat16"), ("sei", 20, "int32"),
+        ("uq", 128, "float8_e4m3fn_x4"), ("us", 128, "uint8"), ("ur", 128, "float8_e4m3fn_x4"), ("urs", 128, "uint8"),
+        ("vq", 128, "float8_e4m3fn_x4"), ("vs", 128, "uint8"), ("wq", 512, "float8_e4m3fn_x4"), ("wqs", 512, "uint8"),
+        ("idt", 128, "bfloat16"), ("eb", 2048, "bfloat16"), ("eq", 512, "float8_e4m3fn_x4"), ("es", 512, "uint8"),
+        ("pi", 1, "int32"), ("li", 1, "int32"), ("lf", 1, "float32"), ("i16", 320, "float32"), ("i512", 512, "float32"),
+        ("ma1", 320, "bfloat16"), ("ma2", 320, "bfloat16"), ("d0r", 320, "bfloat16"), ("d0l", 320, "float32"),
+        ("subl", 1, "float32"), ("i8", 32, "float32"), ("d0t", 32, "float32"), ("x4", 4, "int32"), ("bo", 4, "float32"),
+        ("m4", 4, "float32"), ("oh", 4, "float32"), ("fl0", 1, "float32"), ("ini", 1, "float32"), ("tr", 1, "float32"),
+        ("zz", 16, "float32"), ("nd", 16, "float32"), ("ad", 16, "float32"), ("sg", 16, "float32"), ("an", 16, "float32"),
+        ("w1", 16, "float32"), ("w2", 16, "float32"), ("zl", 16, "float32"), ("zr", 1, "float32"), ("tm", 16, "float32"),
+        ("wt0", 16, "float32"), ("wt1", 16, "float32"), ("wm0", 16, "float32"), ("wm1", 16, "float32"), ("ba", 1, "float32"), ("bt", 1, "float32"),
+        ("ji", 32, "float32"), ("fc", 64, "float32"), ("fm", 64, "float32"), ("fs", 64, "float32"), ("tl", 4, "uint16"), ("tls", 2, "uint16"),
+        ("ull", 8, "uint16"),
+        ("ai", 20, "int32"), ("ofl", 20, "uint16"), ("parl", 20, "uint16"), ("dd", 656, "float32"), ("wo", 8, "uint16"), ("wv", 32, "uint16"),
+        ("g16", 64, "float32"), ("yt", 8, "float32"), ("yo", 8, "float32"), ("gg", 512, "float32"), ("gs", 512, "float32"),
+        ("ls", 32, "uint16"), ("yf", 32, "float32"), ("lab", 32, "float32"), ("eqv", 32, "float32"), ("eqr", 8, "float32"),
+        ("eqp", 4, "float32"), ("eqm", 4, "float32"), ("cb", 1, "float32"), ("ct", 1, "float32"), ("cs", 42, "float32"), ("z32", 32, "float32"), ("y32", 32, "float32"), ("zy", 32, "float32"), ("o32", 32, "float32"), ("ol", 32, "uint16"),
+        ("at", 960, "float32"), ("als", 320, "float32"), ("al", 20, "uint16"),
+        ("tb", 320, "bfloat16"), ("mg", 256, "bfloat16"), ("sc", 240, "bfloat16"), ("e0", 32, "float32"), ("e1", 32, "float32"),
+        ("pp", 42, "float32"), ("prep", 512, "float32"), ("brep", 320, "float32"), ("bsc", 320, "float32"), ("bl", 20, "uint16"),
+        ("zt", 512, "float32"), ("msc", 320, "float32"), ("ml", 20, "uint16"), ("mr", 320, "float32"), ("ysb", 320, "float32"),
+        ("fw", 1280, "bfloat16"), ("fg", 1280, "bfloat16"), ("aw", 1280, "bfloat16"),
+        ("pl", 96, "uint16"), ("pa", 96, "uint16"), ("ll", 96, "uint16"), ("lr", 1536, "float32")):
+    SCRATCH[_n] = ("sbuf", [128, _w], _d)
+for _r in range(2):
+    SCRATCH["q%d" % _r] = ("sbuf", [128, 320], "float8_e4m3fn_x4")
+    SCRATCH["qs%d" % _r] = ("sbuf", [128, 320], "uint8")
+SCRATCH["xr"] = SCRATCH["hb"] = ("sbuf", [128, 1280], "bfloat16")
+for _r in range(3):
+    SCRATCH["hq%d" % _r] = ("sbuf", [128, 320], "float8_e4m3fn_x4")
+    SCRATCH["hs%d" % _r] = ("sbuf", [128, 320], "uint8")
+    SCRATCH["lq%d" % _r] = ("sbuf", [128, 320], "float8_e4m3fn_x4")
+    SCRATCH["lqs%d" % _r] = ("sbuf", [128, 320], "uint8")
+
+SEMAPHORES = ["cV", "cS", "cT", "cG", "sent", "stored", "hand", "handed", "sra", "lse", "lx", "lu", "lv", "lwc", "lws"]
+for _r in range(3):
+    SEMAPHORES += ["pr%d" % _r, "lb%d" % _r, "cr%d" % _r, "sr%d" % _r]
+
+
+def relay_of(T, topo, rank, s):
+    core, dst = T.cores[rank], T.cores[rank ^ s]
+    if topo.chip(core) == topo.chip(dst): return None
+    mine = [c for c in topo.cores_of(core) if T.rank_of(c) is not None]
+    free = [c for c in topo.cores_of(core) if T.rank_of(c) is None and topo.die(c) != topo.die(core) and topo.may_write(c, dst)]
+    return free[mine.index(core) % len(free)]
+
+
+def hand_on(g, core, T, topo):
+    for rank in range(len(T.cores)):
+        for k, s in enumerate(STEP):
+            if relay_of(T, topo, rank, s) != core: continue
+            src, dst = T.cores[rank], T.cores[rank ^ s]
+            rid, pid, _s = topo.addr(dst)
+            m, n, got = topo.mask(core, dst), len(topo.engines(core, dst)), len(topo.engines(src, core))
+            c0, c1 = PARTS[0]
+            ll, hq, lq = T.ll[:, 32 * k:32 * k + 32], T["hq%d" % k][:, c0:c1].bitcast(dt.uint8), T["lq%d" % k][:, c0:c1].bitcast(dt.uint8)
+            g.wait_ge(T.sem["lb%d" % k], got)
+            g.remote_dma(ll, ll, T.sem["lb%d" % k], T.sem.sent, pid, rid, m)
+            g.wait_ge(T.sem.hand, got)
+            g.remote_dma(lq, hq, T.sem.handed, T.sem.sent, pid, rid, m)
+            g.wait_ge(T.sem.sent, 2 * n)
+
+
+def rank_program(g, core, T, topo):
+    rank = T.rank_of(core)
+    if rank is None:
+        hand_on(g, core, T, topo)
+        return
+    eng = {"V": g.vector, "S": g.scalar, "T": g.tensor, "G": g, "Y": g.sync}
+    cnt = {"V": 0, "S": 0, "T": 0, "G": 0}
+    known = {q: {} for q in eng}
+    lastw, readers = {}, {}
+
+    def wait(q, stamp):
+        sem, val = stamp
+        if known[q].get(sem, 0) < val:
+            eng[q].wait_ge(T.sem[sem], val)
+            known[q][sem] = val
+
+    def order(q, r, w):
+        need = {}
+        for t in r:
+            if t in lastw: need[lastw[t][0]] = max(need.get(lastw[t][0], 0), lastw[t][1])
+        for t in w:
+            if t in lastw: need[lastw[t][0]] = max(need.get(lastw[t][0], 0), lastw[t][1])
+            for s, v in readers.get(t, []): need[s] = max(need.get(s, 0), v)
+        for s in sorted(need): wait(q, (s, need[s]))
+
+    def mark(r, w, stamp):
+        for t in r: readers.setdefault(t, []).append(stamp)
+        for t in w:
+            lastw[t] = stamp
+            readers[t] = []
+
+    def op(q, call, r, w):
+        bank = [t for t in r if t.startswith("bank")]
+        r, w = [t for t in r if t not in bank], list(w) + bank
+        order(q, r, w)
+        cnt[q] += 1
+        call(eng[q]).then_inc(T.sem["c" + q], 1)
+        mark(r, w, ("c" + q, cnt[q]))
+
+    def load(q, out, in_, w, sem):
+        eng[q].dma_start(out, in_).then_inc(T.sem[sem], 16)
+        mark([], [w], (sem, 16))
+
+    stores = [0]
+
+    def store(q, out, in_, r):
+        order(q, r, [])
+        eng[q].dma_start(out, in_).then_inc(T.sem.stored, 16)
+        stores[0] += 16
+
+    def vts(out, in0, s1, s2, op0, op1, r, w):
+        if op1 is None: op("V", lambda e: e.tensor_scalar(out, in0, s1, s2, op0), r, w)
+        else: op("V", lambda e: e.tensor_scalar(out, in0, s1, s2, op0, op1), r, w)
+
+    def vtt(out, a, b, o, r, w): op("V", lambda e: e.tensor_tensor(out, a, b, o), r, w)
+    def vcp(out, in_, r, w): op("V", lambda e: e.tensor_copy(out, in_), r, w)
+    def vset(ap, c, w): op("V", lambda e: e.memset(ap, c), [], w)
+    def vred(out, in_, r, w): op("V", lambda e: e.tensor_reduce(out, in_, AxisListType.X, A.add), r, w)
+    def vscan(out, d0, d1, ini, o0, o1, r, w): op("V", lambda e: e.tensor_tensor_scan(out, d0, d1, ini, o0, o1), r, w)
+    def iota(ap, pat, base, cm, w): op("G", lambda e: e.iota(ap, pat, base, cm, allow_small_or_imprecise_dtypes=True), [], w)
+    def act(out, in_, r, w, f=F.Copy, **k): op("S", lambda e: e.activation(out, in_, f, **k), r, w)
+    def quant(c, s, t, r, w): op("V", lambda e: e.quantize_mx(c, s, t), r, w)
+
+    def mm(bank, lc, lsc, rc, rsc, r, n=C):
+        out = T.ps[:, 512 * bank:512 * bank + n]
+        op("T", lambda e: e.matmul_mx(out, lc, lsc, rc, rsc, True, True), r, ["bank%d" % bank])
+
+    def bank(b): return T.ps[:, 512 * b:512 * b + C]
+
+    sent = [0]
+
+    def send(out, in_, rsem, dst, r):
+        order("G", r, [])
+        rid, pid, _s = topo.addr(dst)
+        g.remote_dma(out, in_, T.sem[rsem], T.sem.sent, pid, rid, topo.mask(core, dst))
+        sent[0] += len(topo.engines(core, dst))
+
+    spare = []
+
+    def later(f, *a, **k): spare.append(lambda: f(*a, **k))
+
+    def fill(n=1):
+        for _i in range(n):
+            if spare: spare.pop(0)()
+
+    partner = [T.cores[rank ^ s] for s in STEP]
+    relay = [relay_of(T, topo, rank, s) for s in STEP]
+    theirs = [relay_of(T, topo, rank ^ s, s) for s in STEP]
+
+    load("Y", T.sei[:, :], T.se[:, :], "sei", "lse")
+    load("S", T.ub[:, :], T.u[:, :], "ub", "lu")
+    load("Y", T.x0[:, :], T.x[:, :], "x0", "lx")
+    load("S", T.wq[:, :].bitcast(dt.uint8), T.wc[:, :], "wq", "lwc")
+    load("Y", T.wqs[:, :], T.ws[:, :], "wqs", "lws")
+    load("S", T.vb[:, :], T.v[:, :], "vb", "lv")
+
+    LS = ["ls31", "ls8", "ls7", "ls6", "ls5", "ls4"]
+    E0 = ["e0.%d" % j for j in range(4)]
+    FC = ["fc%d" % j for j in range(10)]
+    ZZ = ["zz%d" % j for j in range(5)]
+    op("G", lambda e: e.iota(T.pi[:, :], [[0, 1]], 0, 1), [], ["pi"])
+    iota(T.i512[:, 0:C], [[1, C]], 0, 0, ["i512"])
+    iota(T.i16[:, :], [[0, 20], [1, 16]], 0, 0, ["i16"])
+    iota(T.i512[:, C:512], [[1, 512 - C]], C, 0, ["i512b"])
+    vset(T.idt[:, :], 0.5, ["idt"])
+    vset(T.yt[:, :], 0.0, ["yt0"])
+    vset(T.ls[:, :], 0, LS)
+    vts(T.li[:, :], T.pi[:, :], 15, None, A.bitwise_and, None, ["pi"], ["li"])
+    vset(T.m4[:, :], 0.0, ["m0", "m1", "m2", "m3"])
+    vcp(T.lf[:, :], T.li[:, :], ["li"], ["lf"])
+    for j in range(4):
+        vts(T.x4[:, j:j + 1], T.li[:, :], 8 >> j, None, A.bitwise_and, None, ["li"], ["x4%d" % j])
+    vts(T.tr[:, :], T.lf[:, :], 0.0, 640.0, A.is_equal, A.mult, ["lf"], ["tr"])
+    for j in range(4):
+        vts(T.bo[:, j:j + 1], T.x4[:, j:j + 1], 1.0 / (8 >> j), None, A.mult, None, ["x4%d" % j], ["bo%d" % j])
+    vset(T.ma2[:, 240:256], 2.0, ["ma2b"])
+    vcp(T.wo[:, 0:1], T.bo[:, 0:1], ["bo0"], ["wo0"])
+    vset(T.pp[:, 40:41], 0.0, ["pp0"])
+    vset(T.cs[:, 40:41], 0.0, ["cs0"])
+    vts(T.fl0[:, :], T.lf[:, :], 0.0, None, A.is_equal, None, ["lf"], ["fl0"])
+    vts(T.nd[:, :], T.i16[:, 0:16], T.lf[:, 0:1], None, A.subtract, None, ["i16", "lf"], ["nd"])
+    vts(T.ma1[:, :], T.i16[:, :], T.lf[:, 0:1], None, A.is_equal, None, ["i16", "lf"], ["ma1"])
+    act(T.dd[:, 0:640:2], T.i512[:, 0:C], ["i512"], ["dd"])
+    act(T.dd[:, 1:640:2], T.i512[:, 0:C], ["i512"], ["dd1"])
+    act(T.d0r[:, :], T.i16[:, :], ["i16"], ["d0r"], F.Sign)
+    for b in range(4):
+        act(T.eb[:, 512 * b:512 * b + 512], T.i512[:, :], ["i512", "i512b"], ["eb%d" % b], scale=0.0)
+    op("G", lambda e: e.affine_select(T.idt[:, :], T.idt[:, :], [[-1, 128]], A.is_equal, 0.0, 0, 1), ["idt"], ["idt"])
+    iota(T.zz[:, 1:16:2], [[0, 8]], 1, 0, ["zz0"])
+    iota(T.zz[:, 2:16:4], [[0, 4]], 2, 0, ["zz1"])
+    iota(T.zz[:, 4:16:8], [[0, 2]], 4, 0, ["zz2"])
+    iota(T.zz[:, 8:9], [[0, 1]], 8, 0, ["zz3"])
+    iota(T.zz[:, 0:1], [[0, 1]], 16, 0, ["zz4"])
+    iota(T.i8[:, :], [[0, 8], [1, 4]], 0, 0, ["i8"])
+    iota(T.fc[:, 0:32:4], [[0, 8]], 239, 0, ["fc0"])
+    iota(T.fc[:, 1:32:4], [[0, 4], [16, 2]], 207, 0, ["fc1"])
+    iota(T.fc[:, 2:32:4], [[0, 2], [16, 4]], 143, 0, ["fc2"])
+    iota(T.fc[:, 3:32:4], [[16, 8]], 15, 0, ["fc3"])
+    iota(T.fc[:, 32:40], [[4, 8]], 3, 0, ["fc4"])
+    iota(T.fc[:, 40:48], [[1, 8]], 32, 0, ["fc5"])
+    iota(T.fc[:, 48:56], [[4, 8]], 2, 0, ["fc6"])
+    iota(T.fc[:, 56:60], [[4, 4]], 1, 0, ["fc7"])
+    iota(T.fc[:, 60:62], [[4, 2]], 0, 0, ["fc8"])
+    iota(T.fc[:, 62:64], [[1, 2]], 40, 0, ["fc9"])
+    iota(T.e0[:, 0:32:4], [[0, 4], [16, 2]], -8, 0, ["e0.0"])
+    iota(T.e0[:, 1:32:4], [[0, 2], [8, 2], [0, 2]], -4, 0, ["e0.1"])
+    iota(T.e0[:, 2:32:4], [[4, 2], [0, 4]], -2, 0, ["e0.2"])
+    iota(T.e0[:, 3:32:4], [[0, 8]], -1, 0, ["e0.3"])
+    iota(T.ji[:, :], [[16, 32]], 320, 1, ["ji"])
+    act(T.m4[:, 2:3], T.bo[:, 3:4], ["bo3"], ["m2"])
+    act(T.m4[:, 1:2], T.bo[:, 2:3], ["bo2", "bo3"], ["m1"], F.Sign, bias=T.bo[:, 3:4])
+    act(T.ini[:, :], T.fl0[:, :], ["fl0"], ["ini"], scale=-256.0)
+    act(T.m4[:, 0:1], T.bo[:, 1:2], ["bo1", "m1"], ["m0"], F.Sign, bias=T.m4[:, 1:2])
+    act(T.subl[:, :], T.lf[:, :], ["lf"], ["subl"], F.Identity, bias=15360.0, scale=-1024.0)
+    act(T.ad[:, :], T.nd[:, :], ["nd"], ["ad"], F.Abs, bias=0.5, scale=-1.0)
+    act(T.ma2[:, 0:240], T.ma1[:, 0:240], ["ma1"], ["ma2"], scale=2.0)
+    act(T.d0l[:, :], T.ma1[:, :], ["ma1"], ["d0l"], F.Identity, bias=1024.0, scale=-66560.0)
+    act(T.d0t[:, :], T.i8[:, :], ["i8"], ["d0t"], F.Sign)
+    for b in range(4):
+        act(T.eb[:, 512 * b + b:512 * b + 512:4], T.idt[:, :], ["idt"], ["eb%d" % b])
+
+    vts(T.ofl[:, 0:1], T.sei[:, 0:1], T.tr[:, 0:1], None, A.add, None, ["sei", "tr"], ["ofl0"])
+    vcp(T.ofl[:, 1:20], T.sei[:, 1:20], ["sei"], ["ofl"])
+    vcp(T.dd[:, 0:656].indirect(T.ofl[:, 0:20]), T.i512[:, 0:C], ["ofl", "ofl0", "i512"], ["dd", "dd1"])
+    later(vcp, T.ull[:, :], T.i512[:, 0:128:16], ["i512"], ["ull"])
+    later(vts, T.ai[:, :], T.sei[:, :], 1, None, A.arith_shift_right, None, ["sei"], ["ai"])
+    later(vts, T.sg[:, :], T.nd[:, :], 0.0, 0.5, A.is_le, A.subtract, ["nd"], ["sg"])
+    later(vcp, T.parl[:, :], T.ai[:, :], ["ai"], ["parl"])
+    later(vtt, T.an[:, :], T.ad[:, :], T.zz[:, :], A.is_lt, ["ad"] + ZZ, ["an"])
+    later(vtt, T.oh[:, 0:3], T.m4[:, 0:3], T.m4[:, 1:4], A.subtract, ["m0", "m1", "m2", "m3"], ["oh"])
+    later(vtt, T.w1[:, :], T.sg[:, :], T.zz[:, :], A.mult, ["sg"] + ZZ, ["w1"])
+    later(vset, T.an[:, 0:1], 0.0, ["an"])
+    later(vtt, T.zl[:, :], T.zz[:, :], T.ma1[:, 0:16], A.mult, ZZ + ["ma1"], ["zl"])
+    later(vtt, T.w2[:, :], T.w1[:, :], T.an[:, :], A.mult, ["w1", "an"], ["w2"])
+    later(vred, T.zr[:, :], T.zl[:, :], ["zl"], ["zr"])
+    later(act, T.wt0[:, :], T.w2[:, :], ["w2"], ["wt0"], scale=32.0)
+    later(vts, T.tm[:, :], T.zz[:, :], T.zr[:, 0:1], None, A.is_gt, None, ZZ + ["zr"], ["tm"])
+    later(vtt, T.fm[:, :], T.fc[:, :], T.ma1[:, 0:64], A.mult, FC + ["ma1"], ["fm"])
+    later(vtt, T.yo[:, 0:3], T.yt[:, 1:4], T.oh[:, 0:3], A.mult, ["oh", "yt1", "yt2", "yt3"], ["yo"])
+    later(vscan, T.fs[:, :], T.d0r[:, 0:64], T.fm[:, :], 0.0, A.mult, A.add, ["fm", "d0r"], ["fs"])
+    later(vred, T.yo[:, 4:5], T.yo[:, 0:3], ["yo"], ["yo4"])
+    later(vcp, T.tl[:, 0:4], T.fs[:, 15:64:16], ["fs"], ["tl"])
+    later(vcp, T.ls[:, 31:32], T.yo[:, 4:5], ["yo4"], ["ls31"])
+    later(vtt, T.wm0[:, :], T.wt0[:, :], T.tm[:, :], A.mult, ["wt0", "tm"], ["wm0"])
+
+    for j in range(4):
+        vtt(T.g16[:, 16 * j:16 * j + 16], T.dd[:, 0:640].indirect(T.wo[:, 2 * j:2 * j + 1]), T.ma1[:, 0:16], A.mult,
+            ["dd", "dd1", "wo%d" % j, "ma1"], ["g16%d" % j])
+        fill()
+        vred(T.yt[:, j + 1:j + 2], T.g16[:, 16 * j:16 * j + 16], ["g16%d" % j], ["yt%d" % (j + 1)])
+        fill()
+        y = T.yt[:, j + 1:j + 2]
+        if j < 3:
+            vts(T.wo[:, 2 * j + 2:2 * j + 3], y, 2.0, T.bo[:, j + 1:j + 2], A.mult, A.add, ["yt%d" % (j + 1), "bo%d" % (j + 1)], ["wo%d" % (j + 1)])
+        else:
+            vts(T.wv[:, 0:1], y, 2.0, None, A.mult, None, ["yt4"], ["wv0"])
+            vts(T.wv[:, 1:2], y, 2.0, 1.0, A.mult, A.add, ["yt4"], ["wv1"])
+            vcp(T.ls[:, 30:31], y, ["yt4"], ["ls4"])
+        fill()
+
+    for n, s1, b, o, o1 in ((1, 28, "ls5", 0, 2), (2, 24, "ls6", 2, 6), (4, 16, "ls7", 6, 14), (8, 0, "ls8", 14, 0)):
+        k, h = 32 * n, 32 * (n - 1)
+        vtt(T.gg[:, h:h + k], T.dd[:, 0:640].indirect(T.wv[:, o:o + 2 * n]), T.ma1[:, 0:k], A.mult, ["dd", "dd1", "wv0", "wv1", "ma1"], [b + "g"])
+        if n == 1:
+            quant(T.uq[:, :], T.us[:, :], T.ub[:, :], ["ub"], ["uq"])
+        else: fill()
+        vscan(T.gs[:, h:h + k], T.d0r[:, 0:k], T.gg[:, h:h + k], 0.0, A.mult, A.add, [b + "g", "d0r"], [b + "s"])
+        if n == 1:
+            vcp(T.ur[:, 0:128].bitcast(dt.uint32), T.uq[:, 0:128].bitcast(dt.uint32).indirect(T.ull[:, 0:8]), ["uq", "ull"], ["ur"])
+            act(T.urs[:, 0:128], T.us[:, 0:128].indirect(T.ull[:, 0:8]), ["uq", "ull"], ["urs"])
+        elif n == 2:
+            quant(T.q0[:, 0:C], T.qs0[:, 0:C], T.x0[:, 0:1280], ["x0"], ["q0.0"])
+        else: fill()
+        y = T.gs[:, h + 15:h + k:16]
+        if n < 8:
+            vts(T.wv[:, o1:o1 + 2 * n], y, 2.0, None, A.mult, None, [b + "s"], ["wv0"])
+            vts(T.wv[:, o1 + 2 * n:o1 + 4 * n], y, 2.0, 1.0, A.mult, A.add, [b + "s"], ["wv1"])
+        vcp(T.ls[:, s1:s1 + 2 * n], y, [b + "s"], [b])
+        fill()
+    fill(len(spare))
+
+    def labels(k):
+        send(T.ll[:, 32 * k:32 * k + 32], T.ls[:, 0:32], "lb%d" % k, relay[k] or partner[k], LS)
+
+    labels(0)
+
+    later(vcp, T.yf[:, :], T.ls[:, :], LS, ["yf"])
+    later(vts, T.tls[:, 0:2], T.fs[:, 15:32:16], 0.0625, 15.0625, A.mult, A.add, ["fs"], ["tls"])
+    later(vtt, T.eqp[:, :], T.yt[:, 0:4], T.yt[:, 1:5], A.is_equal, ["yt0", "yt1", "yt2", "yt3", "yt4"], ["eqp"])
+    later(vtt, T.y32[:, :], T.yf[:, :], T.ji[:, :], A.subtract, ["yf", "ji"], ["y32"])
+    later(vcp, T.lab[:, :], T.yf[:, :].indirect(T.tls[:, 0:2]), ["yf", "tls"], ["lab"])
+    later(vtt, T.eqm[:, :], T.eqp[:, :], T.m4[:, :], A.mult, ["eqp", "m0", "m1", "m2", "m3"], ["eqm"])
+    later(vred, T.cb[:, :], T.eqp[:, :], ["eqp"], ["cb"])
+    later(vtt, T.eqv[:, 0:31], T.lab[:, 1:32], T.lab[:, 0:31], A.is_equal, ["lab"], ["eqv"])
+    later(vred, T.ct[:, :], T.eqm[:, :], ["eqm"], ["ct"])
+    later(vtt, T.eqr[:, :], T.lab[:, 3:32:4], T.yf[:, 8:16], A.is_equal, ["lab", "yf"], ["eqr"])
+    later(vtt, T.eqv[:, 3:32:4], T.lab[:, 3:32:4], T.yf[:, 0:8], A.is_equal, ["lab", "yf"], ["eqv"])
+    later(vts, T.cs[:, 41:42], T.ct[:, :], T.cb[:, 0:1], T.fl0[:, 0:1], A.subtract, A.add, ["ct", "cb", "fl0"], ["cst"])
+    later(vscan, T.cs[:, 0:32], T.d0t[:, :], T.eqv[:, :], 0.0, A.mult, A.add, ["eqv", "d0t"], ["cs"])
+    later(vtt, T.cs[:, 32:40], T.cs[:, 2:32:4], T.eqr[:, :], A.add, ["cs", "eqr"], ["csr"])
+    later(vts, T.z32[:, :], T.cs[:, 0:42].indirect(T.tl[:, 2:4]), T.cb[:, 0:1], 0.0, A.add, A.is_equal, ["cs", "csr", "cst", "cs0", "cb", "tl"], ["z32"])
+    later(vtt, T.zy[:, :], T.z32[:, :], T.y32[:, :], A.mult, ["z32", "y32"], ["zy"])
+    later(vtt, T.o32[:, :], T.zy[:, :], T.ji[:, :], A.add, ["zy", "ji"], ["o32"])
+    later(vcp, T.ol[:, :], T.o32[:, :], ["o32"], ["ol"])
+
+    for r in range(3):
+        q, qs, qt = T["q%d" % (r % 2)], T["qs%d" % (r % 2)], "q%d" % (r % 2)
+        Q, QS = q[:, 0:C], qs[:, 0:C]
+        parts = PARTS if r else [(0, C)]
+        qp = ["%s.%d" % (qt, i) for i in range(len(parts))]
+        wb, fb, ab = [[1, 2, 3, 4], [6, 7, 0, 5]], [[6, 7, 0, 5], [1, 2, 3, 4]][len(parts) - 1], [[1, 2, 3, 4], [6, 7, 0, 5]][len(parts) - 1]
+        far = relay[r] is not None
+        hq, hs, lq, lqs = T["hq%d" % r], T["hs%d" % r], T["lq%d" % r], T["lqs%d" % r]
+
+        def scores(i):
+            c0, c1 = parts[i]
+            mm(5 * i, T.ur[:, 0:128], T.urs[:, 0:128], q[:, c0:c1], qs[:, c0:c1], [qp[i], "ur", "urs"], c1 - c0)
+
+        def layer(i):
+            c0, c1 = parts[i]
+            for b in range(4):
+                mm(wb[i][b], T.wq[:, 128 * b:128 * b + 128], T.wqs[:, 128 * b:128 * b + 128], q[:, c0:c1], qs[:, c0:c1], [qp[i], "wq", "wqs"], c1 - c0)
+            for b in range(4):
+                k = wb[i][b]
+                act(T.hb[:, 4 * c0 + b:4 * c1:4], T.ps[:, 512 * k:512 * k + c1 - c0], ["bank%d" % k], ["hb%d.%d" % (i, b)], scale=0.03125)
+
+        def pack(c0, c1, ii, t):
+            quant(hq[:, c0:c1], hs[:, c0:c1], T.hb[:, 4 * c0:4 * c1], ["hb%d.%d" % (i, b) for i in ii for b in range(4)], [t])
+
+        def signs(i):
+            c0, c1 = parts[i]
+            vts(T.tb[:, c0:c1], T.ps[:, 2560 * i:2560 * i + c1 - c0], 0.0, 0.5, A.is_ge, A.subtract, ["bank%d" % (5 * i)], ["tb%d" % i])
+
+        if far:
+            c0, c1 = parts[0]
+            layer(0)
+            scores(0)
+            scores(1)
+            pack(c0, c1, [0], "hqa")
+            send(hq[:, c0:c1].bitcast(dt.uint8), hq[:, c0:c1].bitcast(dt.uint8), "hand", relay[r], ["hqa"])
+            send(lqs[:, c0:c1], hs[:, c0:c1], "sra", partner[r], ["hqa"])
+        else:
+            scores(0)
+            layer(0)
+            if r: scores(1)
+        for i in range(len(parts)): signs(i)
+        if r: layer(1)
+        fill()
+        vtt(T.mg[:, :], T.tb[:, 0:C].indirect(T.ls[:, 16:32]), T.ma2[:, 0:256], A.mult, ["tb0", "tb1", "ma2", "ma2b"] + LS, ["mg"])
+        fill()
+        vscan(T.sc[:, :], T.d0r[:, 0:240], T.mg[:, 0:240], 0.0, A.mult, A.add, ["mg", "d0r"], ["sc"])
+        o, n = r % 2, 1 - r % 2
+        vtt(T["wt%d" % n][:, :], T.mg[:, 240:256], T["wt%d" % o][:, :], A.mult, ["mg", "wt%d" % o], ["wt%d" % n])
+        eo, en, te, tn = (T.e0, T.e1, E0, ["e1"]) if r % 2 == 0 else (T.e1, T.e0, ["e1"], E0)
+        vtt(en[:, :], T.sc[:, 0:240].indirect(T.tl[:, 0:2]), eo[:, :], A.mult, ["sc", "tl"] + te, tn)
+        vtt(T["wm%d" % n][:, :], T.mg[:, 240:256], T["wm%d" % o][:, :], A.mult, ["mg", "wm%d" % o], ["wm%d" % n])
+        vred(T.ba[:, :], T["wt%d" % n][:, :], ["wt%d" % n], ["ba"])
+        vscan(T.pp[:, 0:32], T.d0t[:, :], en[:, :], 0.0, A.mult, A.add, tn + ["d0t"], ["pp"])
+        vred(T.bt[:, :], T["wm%d" % n][:, :], ["wm%d" % n], ["bt"])
+        vtt(T.pp[:, 32:40], T.pp[:, 2:32:4], en[:, 3:32:4], A.subtract, ["pp"] + tn, ["ppr"])
+        vts(T.pp[:, 41:42], T.bt[:, :], T.ba[:, 0:1], T.ini[:, 0:1], A.subtract, A.add, ["bt", "ba", "ini"], ["ppt"])
+        pl, pa = T.pl[:, 32 * r:32 * r + 32], T.pa[:, 32 * r:32 * r + 32]
+        vts(pl, T.pp[:, 0:42].indirect(T.tl[:, 2:4]), T.ba[:, 0:1], 256.0, A.add, A.add, ["pp", "ppr", "ppt", "pp0", "ba", "tl"], ["pl%d" % r])
+        send(pa, pl, "pr%d" % r, partner[r], ["pl%d" % r])
+        fill()
+        c0, c1 = parts[1] if far else (0, C)
+        pack(c0, c1, [1] if far else range(len(parts)), "hq%d" % r)
+        send(lq[:, c0:c1].bitcast(dt.uint8), hq[:, c0:c1].bitcast(dt.uint8), "cr%d" % r, partner[r], ["hq%d" % r])
+        send(lqs[:, c0:c1], hs[:, c0:c1], "sr%d" % r, partner[r], ["hq%d" % r])
+        fill()
+        if r == 0:
+            labels(1)
+            labels(2)
+            quant(T.eq[:, :], T.es[:, :], T.eb[:, :], ["eb0", "eb1", "eb2", "eb3"], ["eq"])
+        for b in range(4):
+            mm(fb[b], T.eq[:, 128 * b:128 * b + 128], T.es[:, 128 * b:128 * b + 128], Q, QS, qp + ["eq"])
+        act(T.prep[:, :], T.i512[:, :].indirect(pl), ["i512", "i512b", "pl%d" % r], ["prep"])
+        if r == 0:
+            for b in range(4):
+                act(T.fw[:, C * b:C * b + C], bank(fb[b]), ["bank%d" % fb[b]], ["fw%d" % b])
+            fill(len(spare))
+            vcp(T.at[:, 0:960].indirect(T.ol[:, 0:32]), T.i512[:, :], ["ol", "i512", "i512b"], ["at"])
+            vscan(T.als[:, :], T.d0l[:, :], T.at[:, 0:C], 0.0, A.add, A.max, ["at", "d0l"], ["als"])
+            vts(T.al[:, :], T.als[:, 15:C:16], T.subl[:, 0:1], None, A.subtract, None, ["als", "subl"], ["al"])
+            lastw["ll0"] = ("lb0", len(topo.engines(core, partner[0])))
+            act(T.lr[:, 0:512], T.i512[:, 0:C].indirect(T.ll[:, 0:32]), ["i512", "ll0"], ["lr0"])
+            for b in range(2):
+                act(T.fg[:, C * b:C * b + C], T.fw[:, C * b:C * b + C].indirect(T.parl[:, 0:20]), ["fw%d" % b, "parl"], ["fg%d" % b])
+        act(T.brep[:, :], T.prep[:, :].indirect(T.al[:, 0:20]), ["prep", "al"], ["brep"])
+        if r:
+            for b in range(4):
+                vcp(T.fw[:, C * b:C * b + C], bank(fb[b]), ["bank%d" % fb[b]], ["fw%d" % b])
+        if r == 1:
+            quant(T.vq[:, :], T.vs[:, :], T.vb[:, :], ["vb"], ["vq"])
+        for b in range(0 if r else 2, 4):
+            act(T.fg[:, C * b:C * b + C], T.fw[:, C * b:C * b + C].indirect(T.parl[:, 0:20]), ["fw%d" % b, "parl"], ["fg%d" % b])
+        k = len(topo.engines(core, partner[r]))
+        lastw["pa%d" % r], lastw["lq%d" % r], lastw["lqs%d" % r] = ("pr%d" % r, k), ("cr%d" % r, k), ("sr%d" % r, k)
+        zt = (T.zt[:, :].indirect(pa), T.lr[:, 512 * r:512 * r + 512], ["pa%d" % r, "lr%d" % r], ["zt"])
+        if r == 0: vcp(*zt)
+        vscan(T.bsc[:, :], T.d0l[:, :], T.brep[:, :], 0.0, A.add, A.max, ["brep", "d0l"], ["bsc"])
+        vts(T.bl[:, :], T.bsc[:, 15:C:16], T.subl[:, 0:1], None, A.subtract, None, ["bsc", "subl"], ["bl"])
+        if r: vcp(*zt)
+        vcp(T.mr[:, :], T.zt[:, :].indirect(T.bl[:, 0:20]), ["zt", "bl"], ["mr"])
+        vscan(T.msc[:, :], T.d0l[:, :], T.mr[:, :], 0.0, A.add, A.max, ["mr", "d0l"], ["msc"])
+        vts(T.ml[:, :], T.msc[:, 15:C:16], T.subl[:, 0:1], None, A.subtract, None, ["msc", "subl"], ["ml"])
+        if r == 2:
+            store("Y", T.im[:, :], T.mr[0:128:16, :], ["mr"])
+        runs = [(0, C, ab, ["lq%d" % r, "lqs%d" % r])]
+        if far:
+            lastw["lqa"], lastw["lqsa"] = ("handed", len(topo.engines(theirs[r], core))), ("sra", k)
+            runs = [parts[0] + ([1, 2, 3, 4], ["lqa", "lqsa"]), parts[1] + (ab, ["lq%d" % r, "lqs%d" % r])]
+        for c0, c1, bb, tt in runs:
+            for b in range(4):
+                mm(bb[b], T.eq[:, 128 * b:128 * b + 128], T.es[:, 128 * b:128 * b + 128], lq[:, c0:c1], lqs[:, c0:c1], tt + ["eq"], c1 - c0)
+        for j, (c0, c1, bb, tt) in enumerate(runs):
+            for b in range(4):
+                act(T.aw[:, C * b + c0:C * b + c1], T.ps[:, 512 * bb[b]:512 * bb[b] + c1 - c0], ["bank%d" % bb[b]], ["aw%d.%d" % (j, b)])
+        n = r + 1
+        for i, (c0, c1) in enumerate(PARTS):
+            for b in range(4):
+                vtt(T.xr[:, 4 * c0 + b:4 * c1:4], T.aw[:, C * b:C * b + C].indirect(T.ml[:, c0 // 16:c1 // 16]), T.fg[:, C * b + c0:C * b + c1], A.add,
+                    ["aw0.%d" % b, "aw1.%d" % b, "ml", "fg%d" % b], ["xr%d.%d" % (i, b)])
+            quant(T["q%d" % (n % 2)][:, c0:c1], T["qs%d" % (n % 2)][:, c0:c1], T.xr[:, 4 * c0:4 * c1], ["xr%d.%d" % (i, b) for b in range(4)], ["q%d.%d" % (n % 2, i)])
+        if r < 2:
+            lastw["ll%d" % n] = ("lb%d" % n, len(topo.engines(theirs[n] or partner[n], core)))
+            act(T.lr[:, 512 * n:512 * n + 512], T.i512[:, 0:C].indirect(T.ll[:, 32 * n:32 * n + 32]), ["i512", "ll%d" % n], ["lr%d" % n])
+
+    for i, (c0, c1) in enumerate(PARTS):
+        t = "q1.%d" % i
+        mm(5 * i, T.vq[:, 0:128], T.vs[:, 0:128], T.q1[:, c0:c1], T.qs1[:, c0:c1], [t, "vq"], c1 - c0)
+        vcp(T.ysb[:, c0:c1], T.ps[:, 2560 * i:2560 * i + c1 - c0], ["bank%d" % (5 * i)], ["ysb%d" % i])
+        store("Y", T.oc[:, 4 * c0:4 * c1], T.q1[:, c0:c1].bitcast(dt.uint8), [t])
+        for k in range(4):
+            store("S", T.osc[4 * k:4 * k + 4, c0:c1], T.qs1[32 * k:32 * k + 4, c0:c1], [t])
+        store("Y", T.y[:, c0:c1], T.ysb[:, c0:c1], ["ysb%d" % i])
+    for k in ("V", "S", "T", "G"):
+        wait("G", ("c" + k, cnt[k]))
+    g.wait_ge(T.sem.stored, stores[0])
+    g.wait_ge(T.sem.sent, sent[0])

@@ -1,9 +1,9 @@
-import numpy as np
 from concourse.mybir import dt, AluOpType, AxisListType, ActivationFunctionType
 
 C = 320
 STEP = [1, 2, 4]
 PARTS = [(0, 192), (192, 320)]
+OWN = 512
 A = AluOpType
 F = ActivationFunctionType
 
@@ -12,24 +12,20 @@ for _n, _w, _d in (
         ("x0", 1280, "bfloat16"), ("ub", 512, "bfloat16"), ("vb", 512, "bfloat16"), ("sei", 20, "int32"),
         ("uq", 128, "float8_e4m3fn_x4"), ("us", 128, "uint8"), ("ur", 128, "float8_e4m3fn_x4"), ("urs", 128, "uint8"),
         ("vq", 128, "float8_e4m3fn_x4"), ("vs", 128, "uint8"), ("wq", 512, "float8_e4m3fn_x4"), ("wqs", 512, "uint8"),
-        ("idt", 128, "bfloat16"), ("eb", 2048, "bfloat16"), ("eq", 512, "float8_e4m3fn_x4"), ("es", 512, "uint8"),
-        ("pi", 1, "int32"), ("li", 1, "int32"), ("lf", 1, "float32"), ("i16", 320, "float32"), ("i512", 512, "float32"),
-        ("ma1", 320, "bfloat16"), ("ma2", 320, "bfloat16"), ("d0r", 320, "bfloat16"), ("d0l", 320, "float32"),
-        ("subl", 1, "float32"), ("i8", 32, "float32"), ("d0t", 32, "float32"), ("x4", 4, "int32"), ("bo", 4, "float32"),
-        ("m4", 4, "float32"), ("oh", 4, "float32"), ("fl0", 1, "float32"), ("ini", 1, "float32"), ("tr", 1, "float32"),
-        ("zz", 16, "float32"), ("nd", 16, "float32"), ("ad", 16, "float32"), ("sg", 16, "float32"), ("an", 16, "float32"),
-        ("w1", 16, "float32"), ("w2", 16, "float32"), ("zl", 16, "float32"), ("zr", 1, "float32"), ("tm", 16, "float32"),
-        ("wt0", 16, "float32"), ("wt1", 16, "float32"), ("wm0", 16, "float32"), ("wm1", 16, "float32"), ("ba", 1, "float32"), ("bt", 1, "float32"),
-        ("ji", 32, "float32"), ("fc", 64, "float32"), ("fm", 64, "float32"), ("fs", 64, "float32"), ("tl", 4, "uint16"), ("tls", 2, "uint16"),
-        ("ull", 8, "uint16"),
-        ("ai", 20, "int32"), ("ofl", 20, "uint16"), ("parl", 20, "uint16"), ("dd", 656, "float32"), ("wo", 8, "uint16"), ("wv", 32, "uint16"),
-        ("g16", 64, "float32"), ("yt", 8, "float32"), ("yo", 8, "float32"), ("gg", 512, "float32"), ("gs", 512, "float32"),
-        ("ls", 32, "uint16"), ("yf", 32, "float32"), ("lab", 32, "float32"), ("eqv", 32, "float32"), ("eqr", 8, "float32"),
-        ("eqp", 4, "float32"), ("eqm", 4, "float32"), ("cb", 1, "float32"), ("ct", 1, "float32"), ("cs", 42, "float32"), ("z32", 32, "float32"), ("y32", 32, "float32"), ("zy", 32, "float32"), ("o32", 32, "float32"), ("ol", 32, "uint16"),
-        ("at", 960, "float32"), ("als", 320, "float32"), ("al", 20, "uint16"),
-        ("tb", 320, "bfloat16"), ("mg", 256, "bfloat16"), ("sc", 240, "bfloat16"), ("e0", 32, "float32"), ("e1", 32, "float32"),
-        ("pp", 42, "float32"), ("prep", 512, "float32"), ("brep", 320, "float32"), ("bsc", 320, "float32"), ("bl", 20, "uint16"),
-        ("zt", 512, "float32"), ("msc", 320, "float32"), ("ml", 20, "uint16"), ("mr", 320, "float32"), ("ysb", 320, "float32"),
+        ("ea", 520, "bfloat16"), ("eb", 2048, "bfloat16"), ("eq", 512, "float8_e4m3fn_x4"), ("es", 512, "uint8"),
+        ("pi", 1, "int32"), ("p4", 1, "float32"), ("xi", 8, "int32"), ("ln", 16, "float32"),
+        ("i16", 320, "float32"), ("it", OWN + C, "float32"), ("sv", 320, "float32"),
+        ("mk", 336, "bfloat16"), ("d0r", 256, "bfloat16"), ("d0l", 320, "float32"), ("d0t", 80, "float32"), ("subl", 1, "float32"),
+        ("zz", 16, "float32"), ("ad", 16, "float32"), ("sg", 16, "float32"), ("an", 16, "float32"),
+        ("w1", 16, "float32"), ("zl", 16, "float32"), ("zr", 1, "float32"), ("tm", 16, "float32"),
+        ("ji", 32, "float32"), ("j4", 32, "float32"), ("fc", 128, "float32"), ("fs", 128, "float32"), ("tl", 8, "uint16"), ("ull", 8, "uint16"),
+        ("ai", 20, "int32"), ("ofl", 20, "uint16"), ("parl", 20, "uint16"), ("kid", 2 * OWN + 2 * C + 16, "int32"), ("wo", 8, "uint16"), ("wv", 32, "uint16"),
+        ("g16", 48, "float32"), ("yt", 8, "float32"), ("tp", 4, "float32"), ("gg", 512, "float32"), ("gs", 512, "float32"),
+        ("cl", 32, "uint16"), ("ci", 16, "int32"), ("cj", 16, "int32"), ("ls", 16, "uint16"), ("yf", 16, "float32"), ("o32", 32, "float32"), ("ol", 32, "uint16"),
+        ("at", 4 * (OWN + C), "float32"), ("als", 320, "float32"), ("al", 20, "uint16"),
+        ("tb", OWN + C, "bfloat16"), ("sm", 496, "bfloat16"), ("e0", 80, "float32"), ("e1", 80, "float32"),
+        ("pp", 80, "float32"), ("prep", 512, "float32"), ("brep", 320, "float32"), ("bsc", 320, "float32"), ("bl", 20, "uint16"),
+        ("zt", 520, "float32"), ("msc", 320, "float32"), ("ml", 20, "uint16"), ("mr", 320, "float32"), ("ysb", 320, "float32"),
         ("fw", 1280, "bfloat16"), ("fg", 1280, "bfloat16"), ("aw", 1280, "bfloat16"),
         ("pl", 96, "uint16"), ("pa", 96, "uint16"), ("ll", 96, "uint16"), ("lr", 1536, "float32")):
     SCRATCH[_n] = ("sbuf", [128, _w], _d)
@@ -43,9 +39,9 @@ for _r in range(3):
     SCRATCH["lq%d" % _r] = ("sbuf", [128, 320], "float8_e4m3fn_x4")
     SCRATCH["lqs%d" % _r] = ("sbuf", [128, 320], "uint8")
 
-SEMAPHORES = ["cV", "cS", "cT", "cG", "sent", "stored", "hand", "handed", "sra", "lse", "lx", "lu", "lv", "lwc", "lws"]
+SEMAPHORES = ["cV", "cS", "cT", "cG", "sent", "stored", "hand", "lse", "lx", "lu", "lv", "lwc", "lws"]
 for _r in range(3):
-    SEMAPHORES += ["pr%d" % _r, "lb%d" % _r, "cr%d" % _r, "sr%d" % _r]
+    SEMAPHORES += ["pr%d" % _r, "lb%d" % _r, "h%d_0" % _r, "h%d_1" % _r]
 
 
 def relay_of(T, topo, rank, s):
@@ -68,7 +64,7 @@ def hand_on(g, core, T, topo):
             g.wait_ge(T.sem["lb%d" % k], got)
             g.remote_dma(ll, ll, T.sem["lb%d" % k], T.sem.sent, pid, rid, m)
             g.wait_ge(T.sem.hand, got)
-            g.remote_dma(lq, hq, T.sem.handed, T.sem.sent, pid, rid, m)
+            g.remote_dma(lq, hq, T.sem["h%d_0" % k], T.sem.sent, pid, rid, m)
             g.wait_ge(T.sem.sent, 2 * n)
 
 
@@ -134,12 +130,19 @@ def rank_program(g, core, T, topo):
     def iota(ap, pat, base, cm, w): op("G", lambda e: e.iota(ap, pat, base, cm, allow_small_or_imprecise_dtypes=True), [], w)
     def act(out, in_, r, w, f=F.Copy, **k): op("S", lambda e: e.activation(out, in_, f, **k), r, w)
     def quant(c, s, t, r, w): op("V", lambda e: e.quantize_mx(c, s, t), r, w)
+    def copy(q, *a): (vcp if q == "V" else act)(*a)
 
     def mm(bank, lc, lsc, rc, rsc, r, n=C):
         out = T.ps[:, 512 * bank:512 * bank + n]
         op("T", lambda e: e.matmul_mx(out, lc, lsc, rc, rsc, True, True), r, ["bank%d" % bank])
 
-    def bank(b): return T.ps[:, 512 * b:512 * b + C]
+    def bank(b, n=C): return T.ps[:, 512 * b:512 * b + n]
+
+    def latch(out, row, n, r, w):
+        vscan(out, T.d0l[:, 0:n], row, 0.0, A.add, A.max, r + ["d0l"], w)
+
+    def listed(out, latched, r, w):
+        vts(out, latched, T.subl[:, 0:1], None, A.subtract, None, r + ["subl"], w)
 
     sent = [0]
 
@@ -161,293 +164,307 @@ def rank_program(g, core, T, topo):
     relay = [relay_of(T, topo, rank, s) for s in STEP]
     theirs = [relay_of(T, topo, rank ^ s, s) for s in STEP]
 
+    def codes(r): return T["q%d" % (r % 2)], T["qs%d" % (r % 2)]
+    def runs(r): return PARTS if r else [(0, C)]
+    def qtags(r): return ["q%d.%d" % (r % 2, i) for i in range(len(runs(r)))]
+    LAYER = [[1, 2, 3, 4], [6, 7, 0, 5]]
+
+    def scores(r, i):
+        (q, qs), (c0, c1) = codes(r), runs(r)[i]
+        mm(5 * i, T.ur[:, 0:128], T.urs[:, 0:128], q[:, c0:c1], qs[:, c0:c1], [qtags(r)[i], "ur", "urs"], c1 - c0)
+        act(T.tb[:, c0:c1], bank(5 * i, c1 - c0), ["bank%d" % (5 * i)], ["tb%d" % i], F.Sign, bias=2.0 ** -100)
+        if r == 0: act(T.tb[:, OWN:OWN + C], bank(0), ["bank0"], ["tb1"], F.Sign, bias=2.0 ** -100)
+
+    def layer(r, i):
+        (q, qs), (c0, c1) = codes(r), runs(r)[i]
+        for b, k in enumerate(LAYER[i]):
+            mm(k, T.wq[:, 128 * b:128 * b + 128], T.wqs[:, 128 * b:128 * b + 128], q[:, c0:c1], qs[:, c0:c1], [qtags(r)[i], "wq", "wqs"], c1 - c0)
+        for b, k in enumerate(LAYER[i]):
+            act(T.hb[:, 4 * c0 + b:4 * c1:4], bank(k, c1 - c0), ["bank%d" % k], ["hb%d.%d" % (i, b)], scale=0.03125)
+
+    def pack(r, i):
+        (c0, c1), hq, hs, t = runs(r)[i], T["hq%d" % r], T["hs%d" % r], "hq%d.%d" % (r, i)
+        quant(hq[:, c0:c1], hs[:, c0:c1], T.hb[:, 4 * c0:4 * c1], ["hb%d.%d" % (i, b) for b in range(4)], [t])
+        sem, k = "h%d_%d" % (r, i), len(topo.engines(core, partner[r]))
+        if i == 0 and relay[r] is not None:
+            send(hq[:, c0:c1].bitcast(dt.uint8), hq[:, c0:c1].bitcast(dt.uint8), "hand", relay[r], [t])
+            lastw["lq%d.%d" % (r, i)] = (sem, k + len(topo.engines(theirs[r], core)))
+        else:
+            send(T["lq%d" % r][:, c0:c1].bitcast(dt.uint8), hq[:, c0:c1].bitcast(dt.uint8), sem, partner[r], [t])
+            lastw["lq%d.%d" % (r, i)] = (sem, 2 * k)
+        send(T["lqs%d" % r][:, c0:c1], hs[:, c0:c1], sem, partner[r], [t])
+
+    def unpack(banks, q, qs, r, n):
+        for b, k in enumerate(banks):
+            mm(k, T.eq[:, 128 * b:128 * b + 128], T.es[:, 128 * b:128 * b + 128], q, qs, r + ["eq%d" % b], n)
+
+    def own(r, banks):
+        q, qs = codes(r)
+        unpack(banks, q[:, 0:C], qs[:, 0:C], qtags(r), C)
+
+    def fw(e, b, k): copy(e, T.fw[:, C * b:C * b + C], bank(k), ["bank%d" % k], ["fw%d" % b])
+    def fg(e, b): copy(e, T.fg[:, C * b:C * b + C], T.fw[:, C * b:C * b + C].indirect(T.parl[:, 0:20]), ["fw%d" % b, "parl"], ["fg%d" % b])
+
+    def arrived(r, i, banks):
+        c0, c1 = runs(r)[i]
+        unpack(banks, T["lq%d" % r][:, c0:c1], T["lqs%d" % r][:, c0:c1], ["lq%d.%d" % (r, i)], c1 - c0)
+        for b, k in enumerate(banks):
+            act(T.aw[:, C * b + c0:C * b + c1], bank(k, c1 - c0), ["bank%d" % k], ["aw%d.%d" % (i, b)])
+
+    E0 = ["e0.%d" % j for j in range(10)]
+
+    def positions(r):
+        eo, en, te, tn = (T.e0, T.e1, E0, ["e1"]) if r % 2 == 0 else (T.e1, T.e0, ["e1"], E0)
+        signs = T.tb[:, 0:C].indirect(T.ls[:, 0:16]) if r else T.tb[:, 0:OWN + C].indirect(T.cl[:, 0:16])
+        pl = T.pl[:, 32 * r:32 * r + 32]
+        yield vtt(T.sm[:, 240:496], signs, T.mk[:, 0:256], A.mult, ["tb0", "tb1", "mk", "mk1", "ls" if r else "cl0", "cl1", "cl8"], ["mg"])
+        yield vscan(T.sm[:, 0:240], T.d0r[:, 0:240], T.sm[:, 256:496], 0.0, A.mult, A.add, ["mg", "d0r"], ["sc"])
+        yield vtt(en[:, :], T.sm[:, 0:256].indirect(T.tl[:, 0:5]), eo[:, :], A.mult, ["sc", "mg", "tl"] + te, tn)
+        yield vscan(T.pp[:, :], T.d0t[:, :], en[:, :], 0.0, A.mult, A.add, tn + ["d0t", "d0t1"], ["pp"])
+        vts(pl, T.pp[:, 16:80].indirect(T.tl[:, 6:8]), T.pp[:, 15:16], 256.0, A.add, A.add, ["pp", "tl"], ["pl%d" % r])
+        send(T.pa[:, 32 * r:32 * r + 32], pl, "pr%d" % r, partner[r], ["pl%d" % r])
+        lastw["pa%d" % r] = ("pr%d" % r, len(topo.engines(core, partner[r])))
+        yield
+
+    def labels(k):
+        send(T.ll[:, 32 * k:32 * k + 32], T.cl[:, 0:32], "lb%d" % k, relay[k] or partner[k], ["cl0", "cl1", "cl8", "cl16"])
+        lastw["ll%d" % k] = ("lb%d" % k, len(topo.engines(theirs[k] or partner[k], core)))
+
+    def spread(k):
+        act(T.lr[:, 512 * k:512 * k + 512], T.it[:, :].indirect(T.ll[:, 32 * k:32 * k + 32]), ["it0", "it1", "it2", "ll%d" % k], ["lr%d" % k])
+
+    def prep(r): act(T.prep[:, :], T.it[:, 0:520].indirect(T.pl[:, 32 * r:32 * r + 32]), ["it0", "it1", "it2", "pl%d" % r], ["prep"])
+    def brep(): act(T.brep[:, :], T.prep[:, :].indirect(T.al[:, 0:20]), ["prep", "al"], ["brep"])
+    def zt(r): vcp(T.zt[:, :].indirect(T.pa[:, 32 * r:32 * r + 32]), T.lr[:, 512 * r:512 * r + 512], ["pa%d" % r, "lr%d" % r], ["zt", "zt1"])
+
+    def placed():
+        latch(T.bsc[:, :], T.brep[:, :], C, ["brep"], ["bsc"])
+        fill()
+        listed(T.bl[:, :], T.bsc[:, 15:C:16], ["bsc"], ["bl"])
+
+    def mapped(r):
+        for e, (i, (c0, c1)) in zip("VS", enumerate(PARTS)):
+            copy(e, T.mr[:, c0:c1], T.zt[:, :].indirect(T.bl[:, c0 // 16:c1 // 16]), ["zt", "bl"], ["mr%d" % i])
+        for i, (c0, c1) in enumerate(PARTS):
+            latch(T.msc[:, c0:c1], T.mr[:, c0:c1], c1 - c0, ["mr%d" % i], ["msc%d" % i])
+        for i, (c0, c1) in enumerate(PARTS):
+            listed(T.ml[:, c0 // 16:c1 // 16], T.msc[:, c0 + 15:c1:16], ["msc%d" % i], ["ml%d" % i])
+
+    def state(r, i):
+        for j, b in ([(0, 0), (0, 1), (0, 2), (0, 3), (1, 0)], [(1, 1), (1, 2), (1, 3)])[i]:
+            c0, c1 = PARTS[j]
+            vtt(T.xr[:, 4 * c0 + b:4 * c1:4], T.aw[:, C * b:C * b + C].indirect(T.ml[:, c0 // 16:c1 // 16]), T.fg[:, C * b + c0:C * b + c1], A.add,
+                ["aw0.%d" % b, "aw1.%d" % b, "ml%d" % j, "fg%d" % b], ["xr%d.%d" % (j, b)])
+        (q, qs), (c0, c1) = codes(r + 1), PARTS[i]
+        quant(q[:, c0:c1], qs[:, c0:c1], T.xr[:, 4 * c0:4 * c1], ["xr%d.%d" % (i, b) for b in range(4)], [qtags(r + 1)[i]])
+
     load("Y", T.sei[:, :], T.se[:, :], "sei", "lse")
     load("S", T.ub[:, :], T.u[:, :], "ub", "lu")
     load("Y", T.x0[:, :], T.x[:, :], "x0", "lx")
     load("S", T.wq[:, :].bitcast(dt.uint8), T.wc[:, :], "wq", "lwc")
     load("Y", T.wqs[:, :], T.ws[:, :], "wqs", "lws")
-    load("S", T.vb[:, :], T.v[:, :], "vb", "lv")
+    load("Y", T.vb[:, :], T.v[:, :], "vb", "lv")
 
-    LS = ["ls31", "ls8", "ls7", "ls6", "ls5", "ls4"]
-    E0 = ["e0.%d" % j for j in range(4)]
-    FC = ["fc%d" % j for j in range(10)]
-    ZZ = ["zz%d" % j for j in range(5)]
     op("G", lambda e: e.iota(T.pi[:, :], [[0, 1]], 0, 1), [], ["pi"])
-    iota(T.i512[:, 0:C], [[1, C]], 0, 0, ["i512"])
+    iota(T.it[:, 0:C], [[1, C]], 0, 0, ["it0"])
     iota(T.i16[:, :], [[0, 20], [1, 16]], 0, 0, ["i16"])
-    iota(T.i512[:, C:512], [[1, 512 - C]], C, 0, ["i512b"])
-    vset(T.idt[:, :], 0.5, ["idt"])
-    vset(T.yt[:, :], 0.0, ["yt0"])
-    vset(T.ls[:, :], 0, LS)
-    vts(T.li[:, :], T.pi[:, :], 15, None, A.bitwise_and, None, ["pi"], ["li"])
-    vset(T.m4[:, :], 0.0, ["m0", "m1", "m2", "m3"])
-    vcp(T.lf[:, :], T.li[:, :], ["li"], ["lf"])
+    iota(T.p4[:, :], [[0, 1]], -3, -4, ["p4"])
+    iota(T.it[:, C:512], [[1, 512 - C]], C, 0, ["it1"])
+    ZZ = ["zz%d" % j for j in range(4)]
     for j in range(4):
-        vts(T.x4[:, j:j + 1], T.li[:, :], 8 >> j, None, A.bitwise_and, None, ["li"], ["x4%d" % j])
-    vts(T.tr[:, :], T.lf[:, :], 0.0, 640.0, A.is_equal, A.mult, ["lf"], ["tr"])
-    for j in range(4):
-        vts(T.bo[:, j:j + 1], T.x4[:, j:j + 1], 1.0 / (8 >> j), None, A.mult, None, ["x4%d" % j], ["bo%d" % j])
-    vset(T.ma2[:, 240:256], 2.0, ["ma2b"])
-    vcp(T.wo[:, 0:1], T.bo[:, 0:1], ["bo0"], ["wo0"])
-    vset(T.pp[:, 40:41], 0.0, ["pp0"])
-    vset(T.cs[:, 40:41], 0.0, ["cs0"])
-    vts(T.fl0[:, :], T.lf[:, :], 0.0, None, A.is_equal, None, ["lf"], ["fl0"])
-    vts(T.nd[:, :], T.i16[:, 0:16], T.lf[:, 0:1], None, A.subtract, None, ["i16", "lf"], ["nd"])
-    vts(T.ma1[:, :], T.i16[:, :], T.lf[:, 0:1], None, A.is_equal, None, ["i16", "lf"], ["ma1"])
-    act(T.dd[:, 0:640:2], T.i512[:, 0:C], ["i512"], ["dd"])
-    act(T.dd[:, 1:640:2], T.i512[:, 0:C], ["i512"], ["dd1"])
-    act(T.d0r[:, :], T.i16[:, :], ["i16"], ["d0r"], F.Sign)
-    for b in range(4):
-        act(T.eb[:, 512 * b:512 * b + 512], T.i512[:, :], ["i512", "i512b"], ["eb%d" % b], scale=0.0)
-    op("G", lambda e: e.affine_select(T.idt[:, :], T.idt[:, :], [[-1, 128]], A.is_equal, 0.0, 0, 1), ["idt"], ["idt"])
-    iota(T.zz[:, 1:16:2], [[0, 8]], 1, 0, ["zz0"])
-    iota(T.zz[:, 2:16:4], [[0, 4]], 2, 0, ["zz1"])
-    iota(T.zz[:, 4:16:8], [[0, 2]], 4, 0, ["zz2"])
-    iota(T.zz[:, 8:9], [[0, 1]], 8, 0, ["zz3"])
-    iota(T.zz[:, 0:1], [[0, 1]], 16, 0, ["zz4"])
-    iota(T.i8[:, :], [[0, 8], [1, 4]], 0, 0, ["i8"])
-    iota(T.fc[:, 0:32:4], [[0, 8]], 239, 0, ["fc0"])
-    iota(T.fc[:, 1:32:4], [[0, 4], [16, 2]], 207, 0, ["fc1"])
-    iota(T.fc[:, 2:32:4], [[0, 2], [16, 4]], 143, 0, ["fc2"])
-    iota(T.fc[:, 3:32:4], [[16, 8]], 15, 0, ["fc3"])
-    iota(T.fc[:, 32:40], [[4, 8]], 3, 0, ["fc4"])
-    iota(T.fc[:, 40:48], [[1, 8]], 32, 0, ["fc5"])
-    iota(T.fc[:, 48:56], [[4, 8]], 2, 0, ["fc6"])
-    iota(T.fc[:, 56:60], [[4, 4]], 1, 0, ["fc7"])
-    iota(T.fc[:, 60:62], [[4, 2]], 0, 0, ["fc8"])
-    iota(T.fc[:, 62:64], [[1, 2]], 40, 0, ["fc9"])
-    iota(T.e0[:, 0:32:4], [[0, 4], [16, 2]], -8, 0, ["e0.0"])
-    iota(T.e0[:, 1:32:4], [[0, 2], [8, 2], [0, 2]], -4, 0, ["e0.1"])
-    iota(T.e0[:, 2:32:4], [[4, 2], [0, 4]], -2, 0, ["e0.2"])
-    iota(T.e0[:, 3:32:4], [[0, 8]], -1, 0, ["e0.3"])
-    iota(T.ji[:, :], [[16, 32]], 320, 1, ["ji"])
-    act(T.m4[:, 2:3], T.bo[:, 3:4], ["bo3"], ["m2"])
-    act(T.m4[:, 1:2], T.bo[:, 2:3], ["bo2", "bo3"], ["m1"], F.Sign, bias=T.bo[:, 3:4])
-    act(T.ini[:, :], T.fl0[:, :], ["fl0"], ["ini"], scale=-256.0)
-    act(T.m4[:, 0:1], T.bo[:, 1:2], ["bo1", "m1"], ["m0"], F.Sign, bias=T.m4[:, 1:2])
-    act(T.subl[:, :], T.lf[:, :], ["lf"], ["subl"], F.Identity, bias=15360.0, scale=-1024.0)
-    act(T.ad[:, :], T.nd[:, :], ["nd"], ["ad"], F.Abs, bias=0.5, scale=-1.0)
-    act(T.ma2[:, 0:240], T.ma1[:, 0:240], ["ma1"], ["ma2"], scale=2.0)
-    act(T.d0l[:, :], T.ma1[:, :], ["ma1"], ["d0l"], F.Identity, bias=1024.0, scale=-66560.0)
-    act(T.d0t[:, :], T.i8[:, :], ["i8"], ["d0t"], F.Sign)
-    for b in range(4):
-        act(T.eb[:, 512 * b + b:512 * b + 512:4], T.idt[:, :], ["idt"], ["eb%d" % b])
+        iota(T.zz[:, (1 << j) % 8:16:min(2 << j, 8)], [[0, max(8 >> j, 2)]], 16 << j, 0, [ZZ[j]])
+    FC = ["fc%d" % j for j in range(12)]
+    for j, (ap, pat, base) in enumerate((
+            (T.fc[:, 32:72:5], [[0, 8]], 15), (T.fc[:, 33:72:5], [[16, 2], [0, 4]], 31), (T.fc[:, 34:72:5], [[16, 4], [0, 2]], 63),
+            (T.fc[:, 35:72:5], [[16, 8]], 127), (T.fc[:, 36:72:5], [[16, 8]], 127), (T.fc[:, 0:32], [[0, 2], [1, 16]], 240), (T.fc[:, 72:96], [[0, 24]], 0),
+            (T.fc[:, 96:98], [[41, 2]], 15), (T.fc[:, 98:100], [[20, 2]], 16), (T.fc[:, 100:104], [[10, 4]], 17), (T.fc[:, 104:112], [[5, 8]], 18),
+            (T.fc[:, 112:128], [[5, 8], [1, 2]], 19))):
+        iota(ap, pat, base, 0, [FC[j]])
+    for j, (ap, pat, base) in enumerate((
+            (T.e0[:, 32:72:5], [[16, 2], [0, 4]], -8), (T.e0[:, 33:72:5], [[0, 2], [8, 2], [0, 2]], -4), (T.e0[:, 34:72:5], [[0, 4], [4, 2]], -2),
+            (T.e0[:, 35:72:5], [[0, 8]], -1), (T.e0[:, 36:72:5], [[0, 8]], 2), (T.e0[:, 72:80], [[0, 8]], 0))):
+        iota(ap, pat, base, 0, [E0[j]])
+    iota(T.ji[:, :], [[16, 32]], 4 * C, 1, ["ji"])
 
-    vts(T.ofl[:, 0:1], T.sei[:, 0:1], T.tr[:, 0:1], None, A.add, None, ["sei", "tr"], ["ofl0"])
+    bits = {m: T.xi[:, j:j + 1] for j, m in enumerate((15, 8, 4, 2, 1, 3, 7))}
+    ln = {n: T.ln[:, j:j + 1] for j, n in enumerate(("trash", "right", "left", "b1", "b2", "b3", "lane", "at1", "at2", "root", "top", "mid", "none"))}
+    for m in bits:
+        vts(bits[m], T.pi[:, :], m, None, A.bitwise_and, None, ["pi"], ["x%d" % m])
+    vset(T.mk[:, 0:16], 1.0, ["mk1"])
+    vset(T.d0t[:, :], 1.0, ["d0t", "d0t1"])
+    for n, m, s1, s2, o0, o1 in (
+            ("trash", 15, 0.0, 2.0 * C, A.is_equal, A.mult), ("lane", 15, 1.0, None, A.mult, None), ("mid", 15, 16.0, 8.0, A.mult, A.add),
+            ("right", 8, 0.25, None, A.mult, None), ("left", 8, -0.25, 2.0, A.mult, A.add),
+            ("b1", 4, 0.25, None, A.mult, None), ("b2", 2, 0.5, None, A.mult, None), ("b3", 1, 1.0, None, A.mult, None),
+            ("at1", 7, 4.0, 0.5, A.is_equal, A.mult), ("at2", 3, 2.0, None, A.is_equal, None),
+            ("root", 15, 8.0, float(OWN), A.is_equal, A.mult), ("none", 15, 0.0, 256.0, A.is_equal, A.mult)):
+        vts(ln[n], bits[m], s1, s2, o0, o1, ["x%d" % m], [n])
+    vcp(T.kid[:, 2 * OWN:2 * OWN + 2 * C:2], T.it[:, 0:C], ["it0"], ["kid0"])
+    vcp(T.kid[:, 2 * OWN + 1:2 * OWN + 2 * C:2], T.it[:, 0:C], ["it0"], ["kid1"])
+    vset(T.d0t[:, 32:77:5], 0.0, ["d0t"])
+    vset(T.zt[:, 0:1], 0.0, ["zt"])
+    vset(T.zt[:, 512:520], 0.0, ["zt1"])
+    vset(T.d0t[:, 0:32:16], 0.0, ["d0t1"])
+    vts(T.mk[:, 16:336], T.i16[:, :], ln["lane"], None, A.is_equal, None, ["i16", "lane"], ["mk"])
+    act(T.sv[:, :], T.it[:, 0:C], ["it0"], ["sv"], F.Identity, bias=float(OWN))
+    act(T.it[:, OWN:OWN + C], T.it[:, 0:C], ["it0"], ["it2"])
+    act(ln["top"], ln["at1"], ["at1", "root"], ["top"], F.Identity, bias=ln["root"], scale=-1.0)
+    act(T.subl[:, :], ln["lane"], ["lane"], ["subl"], F.Identity, bias=15360.0, scale=-1024.0)
+    act(T.d0r[:, :], T.i16[:, 0:256], ["i16"], ["d0r"], F.Sign)
+    act(T.sg[:, :], T.i16[:, 0:16], ["i16", "mid"], ["sg"], F.Sign, bias=ln["mid"], scale=-16.0)
+    act(T.ad[:, :], T.i16[:, 0:16], ["i16", "mid"], ["ad"], F.Abs, bias=ln["mid"], scale=-16.0)
+    act(T.d0l[:, :], T.mk[:, 16:336], ["mk"], ["d0l"], F.Identity, bias=1024.0, scale=-66560.0)
+    act(T.ea[:, :], T.it[:, 0:520], ["it0", "it1", "it2", "p4"], ["ea"], F.Abs, bias=T.p4[:, 0:1])
+    for b in range(4):
+        act(T.eb[:, 512 * b:512 * b + 512], T.ea[:, 3 - b:515 - b], ["ea"], ["eb%d" % b], F.Relu, bias=0.5, scale=-1.0)
+    act(T.j4[:, :], T.ji[:, :], ["ji"], ["j4"], scale=0.25)
+
+    vts(T.ofl[:, 0:1], T.sei[:, 0:1], ln["trash"], None, A.add, None, ["sei", "trash"], ["ofl0"])
     vcp(T.ofl[:, 1:20], T.sei[:, 1:20], ["sei"], ["ofl"])
-    vcp(T.dd[:, 0:656].indirect(T.ofl[:, 0:20]), T.i512[:, 0:C], ["ofl", "ofl0", "i512"], ["dd", "dd1"])
-    later(vcp, T.ull[:, :], T.i512[:, 0:128:16], ["i512"], ["ull"])
-    later(vts, T.ai[:, :], T.sei[:, :], 1, None, A.arith_shift_right, None, ["sei"], ["ai"])
-    later(vts, T.sg[:, :], T.nd[:, :], 0.0, 0.5, A.is_le, A.subtract, ["nd"], ["sg"])
-    later(vcp, T.parl[:, :], T.ai[:, :], ["ai"], ["parl"])
-    later(vtt, T.an[:, :], T.ad[:, :], T.zz[:, :], A.is_lt, ["ad"] + ZZ, ["an"])
-    later(vtt, T.oh[:, 0:3], T.m4[:, 0:3], T.m4[:, 1:4], A.subtract, ["m0", "m1", "m2", "m3"], ["oh"])
-    later(vtt, T.w1[:, :], T.sg[:, :], T.zz[:, :], A.mult, ["sg"] + ZZ, ["w1"])
-    later(vset, T.an[:, 0:1], 0.0, ["an"])
-    later(vtt, T.zl[:, :], T.zz[:, :], T.ma1[:, 0:16], A.mult, ZZ + ["ma1"], ["zl"])
-    later(vtt, T.w2[:, :], T.w1[:, :], T.an[:, :], A.mult, ["w1", "an"], ["w2"])
-    later(vred, T.zr[:, :], T.zl[:, :], ["zl"], ["zr"])
-    later(act, T.wt0[:, :], T.w2[:, :], ["w2"], ["wt0"], scale=32.0)
-    later(vts, T.tm[:, :], T.zz[:, :], T.zr[:, 0:1], None, A.is_gt, None, ZZ + ["zr"], ["tm"])
-    later(vtt, T.fm[:, :], T.fc[:, :], T.ma1[:, 0:64], A.mult, FC + ["ma1"], ["fm"])
-    later(vtt, T.yo[:, 0:3], T.yt[:, 1:4], T.oh[:, 0:3], A.mult, ["oh", "yt1", "yt2", "yt3"], ["yo"])
-    later(vscan, T.fs[:, :], T.d0r[:, 0:64], T.fm[:, :], 0.0, A.mult, A.add, ["fm", "d0r"], ["fs"])
-    later(vred, T.yo[:, 4:5], T.yo[:, 0:3], ["yo"], ["yo4"])
-    later(vcp, T.tl[:, 0:4], T.fs[:, 15:64:16], ["fs"], ["tl"])
-    later(vcp, T.ls[:, 31:32], T.yo[:, 4:5], ["yo4"], ["ls31"])
-    later(vtt, T.wm0[:, :], T.wt0[:, :], T.tm[:, :], A.mult, ["wt0", "tm"], ["wm0"])
+    vcp(T.kid[:, 2 * OWN:2 * OWN + 2 * C + 16].indirect(T.ofl[:, 0:20]), T.sv[:, :], ["ofl", "ofl0", "sv"], ["kid0", "kid1"])
+    KID, kid = ["kid0", "kid1", "kid2"], T.kid[:, 0:2 * OWN + 2 * C]
 
-    for j in range(4):
-        vtt(T.g16[:, 16 * j:16 * j + 16], T.dd[:, 0:640].indirect(T.wo[:, 2 * j:2 * j + 1]), T.ma1[:, 0:16], A.mult,
-            ["dd", "dd1", "wo%d" % j, "ma1"], ["g16%d" % j])
+    def pick_u():
+        vcp(T.ur[:, 0:128].bitcast(dt.uint32), T.uq[:, 0:128].bitcast(dt.uint32).indirect(T.ull[:, 0:8]), ["uq", "ull"], ["ur"])
+        act(T.urs[:, 0:128], T.us[:, 0:128].indirect(T.ull[:, 0:8]), ["uq", "ull"], ["urs"])
+        scores(0, 0)
+
+    def first():
+        quant(T.q0[:, 0:C], T.qs0[:, 0:C], T.x0[:, 0:1280], ["x0"], ["q0.0"])
+        layer(0, 0)
+
+    def tiles(b):
+        quant(T.eq[:, 128 * b:128 * b + 128], T.es[:, 128 * b:128 * b + 128], T.eb[:, 512 * b:512 * b + 512], ["eb%d" % b], ["eq%d" % b])
+        if b < 3: return
+        own(0, LAYER[1])
+        for j in range(4): fw("S", j, LAYER[1][j])
+        for j in range(4): fg("S", j)
+
+    later(vcp, T.ull[:, :], T.it[:, 0:128:16], ["it0"], ["ull"])
+    later(quant, T.uq[:, :], T.us[:, :], T.ub[:, :], ["ub"], ["uq"])
+    later(vtt, T.an[:, :], T.ad[:, :], T.zz[:, :], A.is_lt, ["ad"] + ZZ, ["an"])
+    later(first)
+    later(vtt, T.w1[:, :], T.sg[:, :], T.zz[:, :], A.mult, ["sg"] + ZZ, ["w1"])
+    later(vts, T.tp[:, 1:2], T.wo[:, 2:3], ln["at1"], ln["top"], A.mult, A.add, ["wo1", "at1", "top"], ["tp1"])
+    later(pick_u)
+    later(vts, T.tp[:, 2:3], T.yt[:, 2:3], ln["at2"], T.tp[:, 1:2], A.mult, A.add, ["yt2", "at2", "tp1"], ["tp2"])
+    later(vtt, T.zl[:, :], T.zz[:, :], T.mk[:, 16:32], A.mult, ZZ + ["mk"], ["zl"])
+    later(vts, T.cl[:, 0:1], T.yt[:, 3:4], ln["b3"], T.tp[:, 2:3], A.mult, A.add, ["yt3", "b3", "tp2"], ["cl0"])
+    later(tiles, 0)
+    later(vtt, T.e0[:, 0:16], T.w1[:, :], T.an[:, :], A.mult, ["w1", "an"], [E0[6]])
+    later(vred, T.zr[:, :], T.zl[:, :], ["zl"], ["zr"])
+    later(vts, T.ai[:, :], T.sei[:, :], 1, None, A.arith_shift_right, None, ["sei"], ["ai"])
+    later(pack, 0, 0)
+    later(vcp, T.parl[:, :], T.ai[:, :], ["ai"], ["parl"])
+    later(tiles, 1)
+    later(vts, T.tm[:, :], T.zz[:, :], T.zr[:, 0:1], -1.0, A.is_le, A.mult, ZZ + ["zr"], ["tm"])
+    later(latch, T.fs[:, :], T.fc[:, :], 128, FC, ["fs"])
+    later(tiles, 2)
+    later(vtt, T.e0[:, 16:32], T.e0[:, 0:16], T.tm[:, :], A.mult, [E0[6], "tm"], [E0[7]])
+    later(listed, T.tl[:, :], T.fs[:, 15:128:16], ["fs"], ["tl"])
+    later(tiles, 3)
+    later(vset, T.e0[:, 0:1], 0.0, [E0[6]])
+    later(vcp, T.e0[:, 16:17], ln["none"], ["none"], [E0[7]])
+
+    vts(T.tp[:, 0:1], T.kid[:, 2 * OWN + 1:2 * OWN + 2], ln["right"], ln["b1"], A.mult, A.add, ["kid1", "right", "b1"], ["tp0"])
+    vts(T.kid[:, 0:2 * C], T.kid[:, 2 * OWN:2 * OWN + 2 * C], OWN - 1, None, A.bitwise_and, None, ["kid0", "kid1"], ["kid2"])
+    vts(T.wo[:, 2:3], T.kid[:, 2 * OWN:2 * OWN + 1], ln["left"], T.tp[:, 0:1], A.mult, A.add, ["kid0", "left", "tp0"], ["wo1"])
+    fill()
+    for j in range(1, 4):
+        vtt(T.g16[:, 16 * j - 16:16 * j], kid.indirect(T.wo[:, 2 * j:2 * j + 1]), T.mk[:, 16:32], A.mult, KID + ["wo%d" % j, "mk"], ["g16%d" % j])
         fill()
-        vred(T.yt[:, j + 1:j + 2], T.g16[:, 16 * j:16 * j + 16], ["g16%d" % j], ["yt%d" % (j + 1)])
+        vred(T.yt[:, j + 1:j + 2], T.g16[:, 16 * j - 16:16 * j], ["g16%d" % j], ["yt%d" % (j + 1)])
         fill()
         y = T.yt[:, j + 1:j + 2]
         if j < 3:
-            vts(T.wo[:, 2 * j + 2:2 * j + 3], y, 2.0, T.bo[:, j + 1:j + 2], A.mult, A.add, ["yt%d" % (j + 1), "bo%d" % (j + 1)], ["wo%d" % (j + 1)])
+            vts(T.wo[:, 2 * j + 2:2 * j + 3], y, 2.0, ln["b%d" % (j + 1)], A.mult, A.add, ["yt%d" % (j + 1), "b%d" % (j + 1)], ["wo%d" % (j + 1)])
         else:
-            vts(T.wv[:, 0:1], y, 2.0, None, A.mult, None, ["yt4"], ["wv0"])
-            vts(T.wv[:, 1:2], y, 2.0, 1.0, A.mult, A.add, ["yt4"], ["wv1"])
-            vcp(T.ls[:, 30:31], y, ["yt4"], ["ls4"])
+            vts(T.wv[:, 2:3], y, 2.0, None, A.mult, None, ["yt4"], ["wv1a"])
+            vts(T.wv[:, 3:4], y, 2.0, 1.0, A.mult, A.add, ["yt4"], ["wv1b"])
         fill()
 
-    for n, s1, b, o, o1 in ((1, 28, "ls5", 0, 2), (2, 24, "ls6", 2, 6), (4, 16, "ls7", 6, 14), (8, 0, "ls8", 14, 0)):
+    def below(n):
         k, h = 32 * n, 32 * (n - 1)
-        vtt(T.gg[:, h:h + k], T.dd[:, 0:640].indirect(T.wv[:, o:o + 2 * n]), T.ma1[:, 0:k], A.mult, ["dd", "dd1", "wv0", "wv1", "ma1"], [b + "g"])
-        if n == 1:
-            quant(T.uq[:, :], T.us[:, :], T.ub[:, :], ["ub"], ["uq"])
-        else: fill()
-        vscan(T.gs[:, h:h + k], T.d0r[:, 0:k], T.gg[:, h:h + k], 0.0, A.mult, A.add, [b + "g", "d0r"], [b + "s"])
-        if n == 1:
-            vcp(T.ur[:, 0:128].bitcast(dt.uint32), T.uq[:, 0:128].bitcast(dt.uint32).indirect(T.ull[:, 0:8]), ["uq", "ull"], ["ur"])
-            act(T.urs[:, 0:128], T.us[:, 0:128].indirect(T.ull[:, 0:8]), ["uq", "ull"], ["urs"])
-        elif n == 2:
-            quant(T.q0[:, 0:C], T.qs0[:, 0:C], T.x0[:, 0:1280], ["x0"], ["q0.0"])
-        else: fill()
+        yield vtt(T.gg[:, h:h + k], kid.indirect(T.wv[:, 2 * n:4 * n]), T.mk[:, 16:16 + k], A.mult, KID + ["wv%da" % n, "wv%db" % n, "mk"], ["gg%d" % n])
+        yield vscan(T.gs[:, h:h + k], T.d0r[:, 0:k], T.gg[:, h:h + k], 0.0, A.mult, A.add, ["gg%d" % n, "d0r"], ["gs%d" % n])
         y = T.gs[:, h + 15:h + k:16]
+        if n >= 4: vcp(T.cl[:, 2 * n:4 * n], y, ["gs%d" % n], ["cl%d" % (2 * n)])
         if n < 8:
-            vts(T.wv[:, o1:o1 + 2 * n], y, 2.0, None, A.mult, None, [b + "s"], ["wv0"])
-            vts(T.wv[:, o1 + 2 * n:o1 + 4 * n], y, 2.0, 1.0, A.mult, A.add, [b + "s"], ["wv1"])
-        vcp(T.ls[:, s1:s1 + 2 * n], y, [b + "s"], [b])
-        fill()
+            vts(T.wv[:, 4 * n:8 * n:2], y, 2.0, None, A.mult, None, ["gs%d" % n], ["wv%da" % (2 * n)])
+            vts(T.wv[:, 4 * n + 1:8 * n:2], y, 2.0, 1.0, A.mult, A.add, ["gs%d" % n], ["wv%db" % (2 * n)])
+        yield
+
+    for n in (1, 2, 4):
+        if n == 4: spare.insert(0, lambda: vts(T.cl[:, 1:8], T.wv[:, 2:16:2], 0.5, None, A.mult, None, ["wv1a", "wv2a", "wv4a"], ["cl1"]))
+        for _c in below(n): fill(2)
     fill(len(spare))
 
-    def labels(k):
-        send(T.ll[:, 32 * k:32 * k + 32], T.ls[:, 0:32], "lb%d" % k, relay[k] or partner[k], LS)
-
+    chain, leaves = positions(0), below(8)
+    next(chain)
+    next(leaves)
+    next(chain)
+    vcp(T.yf[:, :], T.cl[:, 0:16], ["cl0", "cl1", "cl8"], ["yf"])
+    next(leaves)
+    next(chain)
+    next(leaves)
     labels(0)
+    vtt(T.o32[:, 16:32], T.gs[:, 224 + 15:480:16], T.j4[:, 16:32], A.max, ["gs8", "j4"], ["o32b"])
+    next(chain)
+    vtt(T.o32[:, 0:16], T.yf[:, :], T.j4[:, 0:16], A.max, ["yf", "j4"], ["o32a"])
+    next(chain)
+    labels(1)
+    labels(2)
+    prep(0)
+    vts(T.ol[:, :], T.o32[:, :], 4.0, None, A.mult, None, ["o32a", "o32b"], ["ol"])
+    vcp(T.ci[:, :], T.cl[:, 0:16], ["cl0", "cl1", "cl8"], ["ci"])
+    vcp(T.at[:, :].indirect(T.ol[:, 0:32]), T.it[:, 0:512], ["ol", "it0", "it1"], ["at"])
+    vts(T.cj[:, :], T.ci[:, :], OWN - 1, None, A.bitwise_and, None, ["ci"], ["cj"])
+    latch(T.als[:, :], T.at[:, 4 * OWN:4 * (OWN + C):4], C, ["at"], ["als"])
+    vcp(T.ls[:, :], T.cj[:, :], ["cj"], ["ls"])
+    listed(T.al[:, :], T.als[:, 15:C:16], ["als"], ["al"])
+    spread(0)
+    brep()
+    arrived(0, 0, LAYER[0])
+    zt(0)
+    placed()
+    mapped(0)
 
-    later(vcp, T.yf[:, :], T.ls[:, :], LS, ["yf"])
-    later(vts, T.tls[:, 0:2], T.fs[:, 15:32:16], 0.0625, 15.0625, A.mult, A.add, ["fs"], ["tls"])
-    later(vtt, T.eqp[:, :], T.yt[:, 0:4], T.yt[:, 1:5], A.is_equal, ["yt0", "yt1", "yt2", "yt3", "yt4"], ["eqp"])
-    later(vtt, T.y32[:, :], T.yf[:, :], T.ji[:, :], A.subtract, ["yf", "ji"], ["y32"])
-    later(vcp, T.lab[:, :], T.yf[:, :].indirect(T.tls[:, 0:2]), ["yf", "tls"], ["lab"])
-    later(vtt, T.eqm[:, :], T.eqp[:, :], T.m4[:, :], A.mult, ["eqp", "m0", "m1", "m2", "m3"], ["eqm"])
-    later(vred, T.cb[:, :], T.eqp[:, :], ["eqp"], ["cb"])
-    later(vtt, T.eqv[:, 0:31], T.lab[:, 1:32], T.lab[:, 0:31], A.is_equal, ["lab"], ["eqv"])
-    later(vred, T.ct[:, :], T.eqm[:, :], ["eqm"], ["ct"])
-    later(vtt, T.eqr[:, :], T.lab[:, 3:32:4], T.yf[:, 8:16], A.is_equal, ["lab", "yf"], ["eqr"])
-    later(vtt, T.eqv[:, 3:32:4], T.lab[:, 3:32:4], T.yf[:, 0:8], A.is_equal, ["lab", "yf"], ["eqv"])
-    later(vts, T.cs[:, 41:42], T.ct[:, :], T.cb[:, 0:1], T.fl0[:, 0:1], A.subtract, A.add, ["ct", "cb", "fl0"], ["cst"])
-    later(vscan, T.cs[:, 0:32], T.d0t[:, :], T.eqv[:, :], 0.0, A.mult, A.add, ["eqv", "d0t"], ["cs"])
-    later(vtt, T.cs[:, 32:40], T.cs[:, 2:32:4], T.eqr[:, :], A.add, ["cs", "eqr"], ["csr"])
-    later(vts, T.z32[:, :], T.cs[:, 0:42].indirect(T.tl[:, 2:4]), T.cb[:, 0:1], 0.0, A.add, A.is_equal, ["cs", "csr", "cst", "cs0", "cb", "tl"], ["z32"])
-    later(vtt, T.zy[:, :], T.z32[:, :], T.y32[:, :], A.mult, ["z32", "y32"], ["zy"])
-    later(vtt, T.o32[:, :], T.zy[:, :], T.ji[:, :], A.add, ["zy", "ji"], ["o32"])
-    later(vcp, T.ol[:, :], T.o32[:, :], ["o32"], ["ol"])
-
-    for r in range(3):
-        q, qs, qt = T["q%d" % (r % 2)], T["qs%d" % (r % 2)], "q%d" % (r % 2)
-        Q, QS = q[:, 0:C], qs[:, 0:C]
-        parts = PARTS if r else [(0, C)]
-        qp = ["%s.%d" % (qt, i) for i in range(len(parts))]
-        wb, fb, ab = [[1, 2, 3, 4], [6, 7, 0, 5]], [[6, 7, 0, 5], [1, 2, 3, 4]][len(parts) - 1], [[1, 2, 3, 4], [6, 7, 0, 5]][len(parts) - 1]
-        far = relay[r] is not None
-        hq, hs, lq, lqs = T["hq%d" % r], T["hs%d" % r], T["lq%d" % r], T["lqs%d" % r]
-
-        def scores(i):
-            c0, c1 = parts[i]
-            mm(5 * i, T.ur[:, 0:128], T.urs[:, 0:128], q[:, c0:c1], qs[:, c0:c1], [qp[i], "ur", "urs"], c1 - c0)
-
-        def layer(i):
-            c0, c1 = parts[i]
-            for b in range(4):
-                mm(wb[i][b], T.wq[:, 128 * b:128 * b + 128], T.wqs[:, 128 * b:128 * b + 128], q[:, c0:c1], qs[:, c0:c1], [qp[i], "wq", "wqs"], c1 - c0)
-            for b in range(4):
-                k = wb[i][b]
-                act(T.hb[:, 4 * c0 + b:4 * c1:4], T.ps[:, 512 * k:512 * k + c1 - c0], ["bank%d" % k], ["hb%d.%d" % (i, b)], scale=0.03125)
-
-        def pack(c0, c1, ii, t):
-            quant(hq[:, c0:c1], hs[:, c0:c1], T.hb[:, 4 * c0:4 * c1], ["hb%d.%d" % (i, b) for i in ii for b in range(4)], [t])
-
-        def signs(i):
-            c0, c1 = parts[i]
-            vts(T.tb[:, c0:c1], T.ps[:, 2560 * i:2560 * i + c1 - c0], 0.0, 0.5, A.is_ge, A.subtract, ["bank%d" % (5 * i)], ["tb%d" % i])
-
-        if far:
-            c0, c1 = parts[0]
-            layer(0)
-            scores(0)
-            scores(1)
-            pack(c0, c1, [0], "hqa")
-            send(hq[:, c0:c1].bitcast(dt.uint8), hq[:, c0:c1].bitcast(dt.uint8), "hand", relay[r], ["hqa"])
-            send(lqs[:, c0:c1], hs[:, c0:c1], "sra", partner[r], ["hqa"])
-        else:
-            scores(0)
-            layer(0)
-            if r: scores(1)
-        for i in range(len(parts)): signs(i)
-        if r: layer(1)
-        fill()
-        vtt(T.mg[:, :], T.tb[:, 0:C].indirect(T.ls[:, 16:32]), T.ma2[:, 0:256], A.mult, ["tb0", "tb1", "ma2", "ma2b"] + LS, ["mg"])
-        fill()
-        vscan(T.sc[:, :], T.d0r[:, 0:240], T.mg[:, 0:240], 0.0, A.mult, A.add, ["mg", "d0r"], ["sc"])
-        o, n = r % 2, 1 - r % 2
-        vtt(T["wt%d" % n][:, :], T.mg[:, 240:256], T["wt%d" % o][:, :], A.mult, ["mg", "wt%d" % o], ["wt%d" % n])
-        eo, en, te, tn = (T.e0, T.e1, E0, ["e1"]) if r % 2 == 0 else (T.e1, T.e0, ["e1"], E0)
-        vtt(en[:, :], T.sc[:, 0:240].indirect(T.tl[:, 0:2]), eo[:, :], A.mult, ["sc", "tl"] + te, tn)
-        vtt(T["wm%d" % n][:, :], T.mg[:, 240:256], T["wm%d" % o][:, :], A.mult, ["mg", "wm%d" % o], ["wm%d" % n])
-        vred(T.ba[:, :], T["wt%d" % n][:, :], ["wt%d" % n], ["ba"])
-        vscan(T.pp[:, 0:32], T.d0t[:, :], en[:, :], 0.0, A.mult, A.add, tn + ["d0t"], ["pp"])
-        vred(T.bt[:, :], T["wm%d" % n][:, :], ["wm%d" % n], ["bt"])
-        vtt(T.pp[:, 32:40], T.pp[:, 2:32:4], en[:, 3:32:4], A.subtract, ["pp"] + tn, ["ppr"])
-        vts(T.pp[:, 41:42], T.bt[:, :], T.ba[:, 0:1], T.ini[:, 0:1], A.subtract, A.add, ["bt", "ba", "ini"], ["ppt"])
-        pl, pa = T.pl[:, 32 * r:32 * r + 32], T.pa[:, 32 * r:32 * r + 32]
-        vts(pl, T.pp[:, 0:42].indirect(T.tl[:, 2:4]), T.ba[:, 0:1], 256.0, A.add, A.add, ["pp", "ppr", "ppt", "pp0", "ba", "tl"], ["pl%d" % r])
-        send(pa, pl, "pr%d" % r, partner[r], ["pl%d" % r])
-        fill()
-        c0, c1 = parts[1] if far else (0, C)
-        pack(c0, c1, [1] if far else range(len(parts)), "hq%d" % r)
-        send(lq[:, c0:c1].bitcast(dt.uint8), hq[:, c0:c1].bitcast(dt.uint8), "cr%d" % r, partner[r], ["hq%d" % r])
-        send(lqs[:, c0:c1], hs[:, c0:c1], "sr%d" % r, partner[r], ["hq%d" % r])
-        fill()
-        if r == 0:
-            labels(1)
-            labels(2)
-            quant(T.eq[:, :], T.es[:, :], T.eb[:, :], ["eb0", "eb1", "eb2", "eb3"], ["eq"])
-        for b in range(4):
-            mm(fb[b], T.eq[:, 128 * b:128 * b + 128], T.es[:, 128 * b:128 * b + 128], Q, QS, qp + ["eq"])
-        act(T.prep[:, :], T.i512[:, :].indirect(pl), ["i512", "i512b", "pl%d" % r], ["prep"])
-        if r == 0:
-            for b in range(4):
-                act(T.fw[:, C * b:C * b + C], bank(fb[b]), ["bank%d" % fb[b]], ["fw%d" % b])
-            fill(len(spare))
-            vcp(T.at[:, 0:960].indirect(T.ol[:, 0:32]), T.i512[:, :], ["ol", "i512", "i512b"], ["at"])
-            vscan(T.als[:, :], T.d0l[:, :], T.at[:, 0:C], 0.0, A.add, A.max, ["at", "d0l"], ["als"])
-            vts(T.al[:, :], T.als[:, 15:C:16], T.subl[:, 0:1], None, A.subtract, None, ["als", "subl"], ["al"])
-            lastw["ll0"] = ("lb0", len(topo.engines(core, partner[0])))
-            act(T.lr[:, 0:512], T.i512[:, 0:C].indirect(T.ll[:, 0:32]), ["i512", "ll0"], ["lr0"])
-            for b in range(2):
-                act(T.fg[:, C * b:C * b + C], T.fw[:, C * b:C * b + C].indirect(T.parl[:, 0:20]), ["fw%d" % b, "parl"], ["fg%d" % b])
-        act(T.brep[:, :], T.prep[:, :].indirect(T.al[:, 0:20]), ["prep", "al"], ["brep"])
-        if r:
-            for b in range(4):
-                vcp(T.fw[:, C * b:C * b + C], bank(fb[b]), ["bank%d" % fb[b]], ["fw%d" % b])
-        if r == 1:
-            quant(T.vq[:, :], T.vs[:, :], T.vb[:, :], ["vb"], ["vq"])
-        for b in range(0 if r else 2, 4):
-            act(T.fg[:, C * b:C * b + C], T.fw[:, C * b:C * b + C].indirect(T.parl[:, 0:20]), ["fw%d" % b, "parl"], ["fg%d" % b])
-        k = len(topo.engines(core, partner[r]))
-        lastw["pa%d" % r], lastw["lq%d" % r], lastw["lqs%d" % r] = ("pr%d" % r, k), ("cr%d" % r, k), ("sr%d" % r, k)
-        zt = (T.zt[:, :].indirect(pa), T.lr[:, 512 * r:512 * r + 512], ["pa%d" % r, "lr%d" % r], ["zt"])
-        if r == 0: vcp(*zt)
-        vscan(T.bsc[:, :], T.d0l[:, :], T.brep[:, :], 0.0, A.add, A.max, ["brep", "d0l"], ["bsc"])
-        vts(T.bl[:, :], T.bsc[:, 15:C:16], T.subl[:, 0:1], None, A.subtract, None, ["bsc", "subl"], ["bl"])
-        if r: vcp(*zt)
-        vcp(T.mr[:, :], T.zt[:, :].indirect(T.bl[:, 0:20]), ["zt", "bl"], ["mr"])
-        vscan(T.msc[:, :], T.d0l[:, :], T.mr[:, :], 0.0, A.add, A.max, ["mr", "d0l"], ["msc"])
-        vts(T.ml[:, :], T.msc[:, 15:C:16], T.subl[:, 0:1], None, A.subtract, None, ["msc", "subl"], ["ml"])
-        if r == 2:
-            store("Y", T.im[:, :], T.mr[0:128:16, :], ["mr"])
-        runs = [(0, C, ab, ["lq%d" % r, "lqs%d" % r])]
-        if far:
-            lastw["lqa"], lastw["lqsa"] = ("handed", len(topo.engines(theirs[r], core))), ("sra", k)
-            runs = [parts[0] + ([1, 2, 3, 4], ["lqa", "lqsa"]), parts[1] + (ab, ["lq%d" % r, "lqs%d" % r])]
-        for c0, c1, bb, tt in runs:
-            for b in range(4):
-                mm(bb[b], T.eq[:, 128 * b:128 * b + 128], T.es[:, 128 * b:128 * b + 128], lq[:, c0:c1], lqs[:, c0:c1], tt + ["eq"], c1 - c0)
-        for j, (c0, c1, bb, tt) in enumerate(runs):
-            for b in range(4):
-                act(T.aw[:, C * b + c0:C * b + c1], T.ps[:, 512 * bb[b]:512 * bb[b] + c1 - c0], ["bank%d" % bb[b]], ["aw%d.%d" % (j, b)])
-        n = r + 1
-        for i, (c0, c1) in enumerate(PARTS):
-            for b in range(4):
-                vtt(T.xr[:, 4 * c0 + b:4 * c1:4], T.aw[:, C * b:C * b + C].indirect(T.ml[:, c0 // 16:c1 // 16]), T.fg[:, C * b + c0:C * b + c1], A.add,
-                    ["aw0.%d" % b, "aw1.%d" % b, "ml", "fg%d" % b], ["xr%d.%d" % (i, b)])
-            quant(T["q%d" % (n % 2)][:, c0:c1], T["qs%d" % (n % 2)][:, c0:c1], T.xr[:, 4 * c0:4 * c1], ["xr%d.%d" % (i, b) for b in range(4)], ["q%d.%d" % (n % 2, i)])
-        if r < 2:
-            lastw["ll%d" % n] = ("lb%d" % n, len(topo.engines(theirs[n] or partner[n], core)))
-            act(T.lr[:, 512 * n:512 * n + 512], T.i512[:, 0:C].indirect(T.ll[:, 32 * n:32 * n + 32]), ["i512", "ll%d" % n], ["lr%d" % n])
+    for r in (1, 2):
+        spread(r)
+        state(r - 1, 0)
+        layer(r, 0)
+        scores(r, 0)
+        state(r - 1, 1)
+        scores(r, 1)
+        layer(r, 1)
+        pack(r, 0)
+        own(r, LAYER[0])
+        for _c in positions(r): pass
+        pack(r, 1)
+        fw("S", 0, LAYER[0][0])
+        prep(r)
+        for b in (1, 2, 3): fw("V", b, LAYER[0][b])
+        brep()
+        if r == 1: quant(T.vq[:, :], T.vs[:, :], T.vb[:, :], ["vb"], ["vq"])
+        fg("V", 0)
+        placed()
+        for b in (1, 2, 3): fg("S", b)
+        if relay[r] is None: arrived(r, 0, LAYER[1])
+        zt(r)
+        mapped(r)
+        arrived(r, 1, LAYER[0])
+        if relay[r] is not None: arrived(r, 0, LAYER[1])
+    store("Y", T.im[:, :], T.mr[0:128:16, :], ["mr0", "mr1"])
 
     for i, (c0, c1) in enumerate(PARTS):
+        state(2, i)
         t = "q1.%d" % i
         mm(5 * i, T.vq[:, 0:128], T.vs[:, 0:128], T.q1[:, c0:c1], T.qs1[:, c0:c1], [t, "vq"], c1 - c0)
-        vcp(T.ysb[:, c0:c1], T.ps[:, 2560 * i:2560 * i + c1 - c0], ["bank%d" % (5 * i)], ["ysb%d" % i])
+        act(T.ysb[:, c0:c1], bank(5 * i, c1 - c0), ["bank%d" % (5 * i)], ["ysb%d" % i])
         store("Y", T.oc[:, 4 * c0:4 * c1], T.q1[:, c0:c1].bitcast(dt.uint8), [t])
+        store("S", T.y[:, c0:c1], T.ysb[:, c0:c1], ["ysb%d" % i])
         for k in range(4):
-            store("S", T.osc[4 * k:4 * k + 4, c0:c1], T.qs1[32 * k:32 * k + 4, c0:c1], [t])
-        store("Y", T.y[:, c0:c1], T.ysb[:, c0:c1], ["ysb%d" % i])
+            store("Y", T.osc[4 * k:4 * k + 4, c0:c1], T.qs1[32 * k:32 * k + 4, c0:c1], [t])
     for k in ("V", "S", "T", "G"):
         wait("G", ("c" + k, cnt[k]))
     g.wait_ge(T.sem.stored, stores[0])

@@ -1,9 +1,14 @@
 from concourse.mybir import dt, AluOpType, AxisListType, ActivationFunctionType
 
 C = 320
+MACHINE = 64
+MATE = False
 STEP = [1, 2, 4]
 PARTS = [(0, 192), (192, 320)]
+WAYS = {True: ([("q", 0, 144), ("s", 192, 320)], [("q", 144, 192), ("s", 0, 192), ("q", 192, 320)]), False: ([("q", 0, 192), ("s", 192, 320)], [("s", 0, 192), ("q", 192, 320)])}
+ASIDE = False
 OWN = 512
+BESIDE = "ull an w1|zl tp1 down|zr qu|pu|tp2 tm ai halves|first|t0 cl0|t1 parl|back d0 d1|fs z0|t2 z16|tl t3|t4|pack|t5|j4 t6|cl1 t7|t8||t9|t10|t11 sq|pair"
 A = AluOpType
 F = ActivationFunctionType
 
@@ -12,7 +17,9 @@ for _n, _w, _d in (
         ("x0", 1280, "bfloat16"), ("ub", 512, "bfloat16"), ("vb", 512, "bfloat16"), ("sei", 20, "int32"),
         ("uq", 128, "float8_e4m3fn_x4"), ("us", 128, "uint8"), ("ur", 128, "float8_e4m3fn_x4"), ("urs", 128, "uint8"),
         ("vq", 128, "float8_e4m3fn_x4"), ("vs", 128, "uint8"), ("wq", 512, "float8_e4m3fn_x4"), ("wqs", 512, "uint8"),
-        ("ea", 520, "bfloat16"), ("eb", 2048, "bfloat16"), ("eq", 512, "float8_e4m3fn_x4"), ("es", 512, "uint8"),
+        ("ea", 520, "bfloat16"), ("eb", 1560, "bfloat16"), ("eq", 1536, "float8_e4m3fn_x4"), ("es", 1536, "uint8"),
+        ("sp", 40, "int32"), ("sq", 40, "int32"), ("pair", 40, "uint16"), ("ag", 640, "bfloat16"),
+        ("pq1", 640, "float8_e4m3fn_x4"), ("pqs1", 640, "uint8"), ("pq2", 640, "float8_e4m3fn_x4"), ("pqs2", 640, "uint8"),
         ("pi", 1, "int32"), ("p4", 1, "float32"), ("xi", 8, "int32"), ("ln", 16, "float32"),
         ("i16", 320, "float32"), ("it", OWN + C, "float32"), ("sv", 320, "float32"),
         ("mk", 336, "bfloat16"), ("d0r", 256, "bfloat16"), ("d0l", 320, "float32"), ("d0t", 80, "float32"), ("subl", 1, "float32"),
@@ -37,9 +44,9 @@ for _r in range(3):
     SCRATCH["hq%d" % _r] = ("sbuf", [128, 320], "float8_e4m3fn_x4")
     SCRATCH["hs%d" % _r] = ("sbuf", [128, 320], "uint8")
     SCRATCH["lq%d" % _r] = ("sbuf", [128, 320], "float8_e4m3fn_x4")
-    SCRATCH["lqs%d" % _r] = ("sbuf", [128, 320], "uint8")
+    SCRATCH["ls%d" % _r] = ("sbuf", [128, 320], "uint8")
 
-SEMAPHORES = ["cV", "cS", "cT", "cG", "sent", "stored", "hand", "lse", "lx", "lu", "lv", "lwc", "lws"]
+SEMAPHORES = ["cV", "cS", "cT", "cG", "sent", "stored", "lse", "lsp", "lx", "lu", "lv", "lwc", "lws"] + ["hand%d" % _j for _j in range(4)]
 for _r in range(3):
     SEMAPHORES += ["pr%d" % _r, "lb%d" % _r, "h%d_0" % _r, "h%d_1" % _r]
 
@@ -48,8 +55,24 @@ def relay_of(T, topo, rank, s):
     core, dst = T.cores[rank], T.cores[rank ^ s]
     if topo.chip(core) == topo.chip(dst): return None
     mine = [c for c in topo.cores_of(core) if T.rank_of(c) is not None]
+    beside = [c for c in range(MACHINE) if topo.mates(topo.chip(c), topo.chip(dst)) and topo.die(c) == topo.die(core) and topo.may_write(c, dst)]
+    able = [c for c in mine if all(topo.may_write(c, b) for b in beside)]
+    if MATE and core in able: return beside[able.index(core) % len(beside)]
     free = [c for c in topo.cores_of(core) if T.rank_of(c) is None and topo.die(c) != topo.die(core) and topo.may_write(c, dst)]
     return free[mine.index(core) % len(free)]
+
+
+def ways(topo, core, relay):
+    return WAYS[topo.chip(core) == topo.chip(relay)]
+
+
+def aside(topo, core, relay, dst):
+    return [e for e in topo.engines(core, relay) if e not in topo.engines(core, dst) or not ASIDE] or topo.engines(core, relay)
+
+
+def piece(T, side, kind, r, a, b):
+    if kind == "q": return T["%sq%d" % (side, r)][:, a:b].bitcast(dt.uint8)
+    return T["%ss%d" % (side, r)][:, a:b]
 
 
 def hand_on(g, core, T, topo):
@@ -58,14 +81,14 @@ def hand_on(g, core, T, topo):
             if relay_of(T, topo, rank, s) != core: continue
             src, dst = T.cores[rank], T.cores[rank ^ s]
             rid, pid, _s = topo.addr(dst)
-            m, n, got = topo.mask(core, dst), len(topo.engines(core, dst)), len(topo.engines(src, core))
-            c0, c1 = PARTS[0]
-            ll, hq, lq = T.ll[:, 32 * k:32 * k + 32], T["hq%d" % k][:, c0:c1].bitcast(dt.uint8), T["lq%d" % k][:, c0:c1].bitcast(dt.uint8)
-            g.wait_ge(T.sem["lb%d" % k], got)
+            m, n, handed = topo.mask(core, dst), len(topo.engines(core, dst)), ways(topo, src, core)[0]
+            ll = T.ll[:, 32 * k:32 * k + 32]
+            g.wait_ge(T.sem["lb%d" % k], len(topo.engines(src, core)))
             g.remote_dma(ll, ll, T.sem["lb%d" % k], T.sem.sent, pid, rid, m)
-            g.wait_ge(T.sem.hand, got)
-            g.remote_dma(lq, hq, T.sem["h%d_0" % k], T.sem.sent, pid, rid, m)
-            g.wait_ge(T.sem.sent, 2 * n)
+            for j, (kind, a, b) in enumerate(handed):
+                g.wait_ge(T.sem["hand%d" % j], len(aside(topo, src, core, dst)))
+                g.remote_dma(piece(T, "l", kind, k, a, b), piece(T, "h", kind, k, a, b), T.sem["h%d_%d" % (k, a >= PARTS[1][0])], T.sem.sent, pid, rid, m)
+            g.wait_ge(T.sem.sent, (1 + len(handed)) * n)
 
 
 def rank_program(g, core, T, topo):
@@ -132,9 +155,9 @@ def rank_program(g, core, T, topo):
     def quant(c, s, t, r, w): op("V", lambda e: e.quantize_mx(c, s, t), r, w)
     def copy(q, *a): (vcp if q == "V" else act)(*a)
 
-    def mm(bank, lc, lsc, rc, rsc, r, n=C):
+    def mm(bank, lc, lsc, rc, rsc, r, n=C, start=True, stop=True):
         out = T.ps[:, 512 * bank:512 * bank + n]
-        op("T", lambda e: e.matmul_mx(out, lc, lsc, rc, rsc, True, True), r, ["bank%d" % bank])
+        op("T", lambda e: e.matmul_mx(out, lc, lsc, rc, rsc, start, stop), r, ["bank%d" % bank])
 
     def bank(b, n=C): return T.ps[:, 512 * b:512 * b + n]
 
@@ -146,11 +169,12 @@ def rank_program(g, core, T, topo):
 
     sent = [0]
 
-    def send(out, in_, rsem, dst, r):
+    def send(out, in_, rsem, dst, r, engines=None):
         order("G", r, [])
         rid, pid, _s = topo.addr(dst)
-        g.remote_dma(out, in_, T.sem[rsem], T.sem.sent, pid, rid, topo.mask(core, dst))
-        sent[0] += len(topo.engines(core, dst))
+        engines = engines or topo.engines(core, dst)
+        g.remote_dma(out, in_, T.sem[rsem], T.sem.sent, pid, rid, sum(1 << e for e in engines))
+        sent[0] += len(engines)
 
     spare = []
 
@@ -167,7 +191,8 @@ def rank_program(g, core, T, topo):
     def codes(r): return T["q%d" % (r % 2)], T["qs%d" % (r % 2)]
     def runs(r): return PARTS if r else [(0, C)]
     def qtags(r): return ["q%d.%d" % (r % 2, i) for i in range(len(runs(r)))]
-    LAYER = [[1, 2, 3, 4], [6, 7, 0, 5]]
+    def held(r): return [[3, 4], [6, 7]][r % 2]
+    def four(r, i): return [[1, 2] + held(r), held(r + 1) + [0, 5], [1, 2] + held(r + 1)][i]
 
     def scores(r, i):
         (q, qs), (c0, c1) = codes(r), runs(r)[i]
@@ -175,24 +200,32 @@ def rank_program(g, core, T, topo):
         act(T.tb[:, c0:c1], bank(5 * i, c1 - c0), ["bank%d" % (5 * i)], ["tb%d" % i], F.Sign, bias=2.0 ** -100)
         if r == 0: act(T.tb[:, OWN:OWN + C], bank(0), ["bank0"], ["tb1"], F.Sign, bias=2.0 ** -100)
 
-    def layer(r, i):
+    def layer(r, i, n=4):
         (q, qs), (c0, c1) = codes(r), runs(r)[i]
-        for b, k in enumerate(LAYER[i]):
+        for b, k in enumerate(four(r, i)):
             mm(k, T.wq[:, 128 * b:128 * b + 128], T.wqs[:, 128 * b:128 * b + 128], q[:, c0:c1], qs[:, c0:c1], [qtags(r)[i], "wq", "wqs"], c1 - c0)
-        for b, k in enumerate(LAYER[i]):
-            act(T.hb[:, 4 * c0 + b:4 * c1:4], bank(k, c1 - c0), ["bank%d" % k], ["hb%d.%d" % (i, b)], scale=0.03125)
+        for b in range(n): scaled("S", r, i, b)
+
+    def scaled(e, r, i, b):
+        (c0, c1), k = runs(r)[i], four(r, i)[b]
+        out, tags = T.hb[:, 4 * c0 + b:4 * c1:4], (["bank%d" % k], ["hb%d.%d" % (i, b)])
+        if e == "S": act(out, bank(k, c1 - c0), *tags, scale=0.03125)
+        else: vts(out, bank(k, c1 - c0), 0.03125, None, A.mult, None, *tags)
 
     def pack(r, i):
         (c0, c1), hq, hs, t = runs(r)[i], T["hq%d" % r], T["hs%d" % r], "hq%d.%d" % (r, i)
         quant(hq[:, c0:c1], hs[:, c0:c1], T.hb[:, 4 * c0:4 * c1], ["hb%d.%d" % (i, b) for b in range(4)], [t])
-        sem, k = "h%d_%d" % (r, i), len(topo.engines(core, partner[r]))
-        if i == 0 and relay[r] is not None:
-            send(hq[:, c0:c1].bitcast(dt.uint8), hq[:, c0:c1].bitcast(dt.uint8), "hand", relay[r], [t])
-            lastw["lq%d.%d" % (r, i)] = (sem, k + len(topo.engines(theirs[r], core)))
-        else:
-            send(T["lq%d" % r][:, c0:c1].bitcast(dt.uint8), hq[:, c0:c1].bitcast(dt.uint8), sem, partner[r], [t])
-            lastw["lq%d.%d" % (r, i)] = (sem, 2 * k)
-        send(T["lqs%d" % r][:, c0:c1], hs[:, c0:c1], sem, partner[r], [t])
+        for j, (kind, a, b) in enumerate(ways(topo, core, relay[r])[0] if relay[r] is not None else []):
+            if c0 <= a < c1: send(piece(T, "h", kind, r, a, b), piece(T, "h", kind, r, a, b), "hand%d" % j, relay[r], [t], aside(topo, core, relay[r], partner[r]))
+        if i == 0: post(r, i)
+
+    def post(r, i):
+        c0, c1 = runs(r)[i]
+        mine = come = [], [("q", c0, c1), ("s", c0, c1)]
+        if relay[r] is not None: mine, come = ways(topo, core, relay[r]), ways(topo, partner[r], theirs[r])
+        for kind, a, b in mine[1]:
+            if c0 <= a < c1: send(piece(T, "l", kind, r, a, b), piece(T, "h", kind, r, a, b), "h%d_%d" % (r, i), partner[r], ["hq%d.%d" % (r, i)])
+        lastw["lq%d.%d" % (r, i)] = ("h%d_%d" % (r, i), sum(len(topo.engines(src, core)) for src, pieces in zip((theirs[r], partner[r]), come) for kind, a, b in pieces if c0 <= a < c1))
 
     def unpack(banks, q, qs, r, n):
         for b, k in enumerate(banks):
@@ -205,11 +238,25 @@ def rank_program(g, core, T, topo):
     def fw(e, b, k): copy(e, T.fw[:, C * b:C * b + C], bank(k), ["bank%d" % k], ["fw%d" % b])
     def fg(e, b): copy(e, T.fg[:, C * b:C * b + C], T.fw[:, C * b:C * b + C].indirect(T.parl[:, 0:20]), ["fw%d" % b, "parl"], ["fg%d" % b])
 
-    def arrived(r, i, banks):
+    def pick(e, r, j):
+        (q, qs), at = codes(r), T.pair[:, 8 * j:8 * j + 8]
+        if e == "V": vcp(T["pq%d" % r][:, 128 * j:128 * j + 128].bitcast(dt.uint32), q[:, 0:C].bitcast(dt.uint32).indirect(at), qtags(r) + ["pair"], ["pq%d" % j])
+        else: act(T["pqs%d" % r][:, 128 * j:128 * j + 128], qs[:, 0:C].indirect(at), qtags(r) + ["pair"], ["pqs%d" % j])
+
+    def above(r, h):
+        for b, k in enumerate(four(r, 0)):
+            j = 4 + 4 * h + b
+            mm(k, T.eq[:, 128 * j:128 * j + 128], T.es[:, 128 * j:128 * j + 128], T["pq%d" % r][:, C * h:C * h + C], T["pqs%d" % r][:, C * h:C * h + C],
+               [t % n for t in ("pq%d", "pqs%d") for n in range(2 * h, 2 * h + 3)] + ["eq%d" % j], C, h == 0, h == 1)
+
+    def kept(r, b): act(T.fg[:, C * b:C * b + C], bank(four(r, 0)[b]), ["bank%d" % four(r, 0)[b]], ["fg%d" % b])
+
+    def arrived(r, i, banks, turns=((0, "S"), (1, "S"), (2, "S"), (3, "S"))):
         c0, c1 = runs(r)[i]
-        unpack(banks, T["lq%d" % r][:, c0:c1], T["lqs%d" % r][:, c0:c1], ["lq%d.%d" % (r, i)], c1 - c0)
-        for b, k in enumerate(banks):
-            act(T.aw[:, C * b + c0:C * b + c1], bank(k, c1 - c0), ["bank%d" % k], ["aw%d.%d" % (i, b)])
+        for b, e in turns:
+            mm(banks[b], T.eq[:, 128 * b:128 * b + 128], T.es[:, 128 * b:128 * b + 128], T["lq%d" % r][:, c0:c1], T["ls%d" % r][:, c0:c1], ["lq%d.%d" % (r, i), "eq%d" % b], c1 - c0)
+        for b, e in turns:
+            copy(e, T.aw[:, C * b + c0:C * b + c1], bank(banks[b], c1 - c0), ["bank%d" % banks[b]], ["aw%d.%d" % (i, b)])
 
     E0 = ["e0.%d" % j for j in range(10)]
 
@@ -233,12 +280,18 @@ def rank_program(g, core, T, topo):
     def spread(k):
         act(T.lr[:, 512 * k:512 * k + 512], T.it[:, :].indirect(T.ll[:, 32 * k:32 * k + 32]), ["it0", "it1", "it2", "ll%d" % k], ["lr%d" % k])
 
-    def prep(r): act(T.prep[:, :], T.it[:, 0:520].indirect(T.pl[:, 32 * r:32 * r + 32]), ["it0", "it1", "it2", "pl%d" % r], ["prep"])
-    def brep(): act(T.brep[:, :], T.prep[:, :].indirect(T.al[:, 0:20]), ["prep", "al"], ["brep"])
-    def zt(r): vcp(T.zt[:, :].indirect(T.pa[:, 32 * r:32 * r + 32]), T.lr[:, 512 * r:512 * r + 512], ["pa%d" % r, "lr%d" % r], ["zt", "zt1"])
+    def prep(r, ee="SV"):
+        for h, e in enumerate(ee):
+            copy(e, T.prep[:, 256 * h:256 * h + 256], T.it[:, 0:520].indirect(T.pl[:, 32 * r + 16 * h:32 * r + 16 * h + 16]), ["it0", "it1", "it2", "pl%d" % r], ["prep%d" % h])
+
+    def brep(ee="SV"):
+        for h, e in enumerate(ee):
+            copy(e, T.brep[:, 160 * h:160 * h + 160], T.prep[:, :].indirect(T.al[:, 10 * h:10 * h + 10]), ["prep0", "prep1", "al"], ["brep%d" % h])
+
+    def zt(r): vcp(T.zt[:, :].indirect(T.pa[:, 32 * r:32 * r + 32]), T.lr[:, 512 * r:512 * r + 512], ["pa%d" % r, "lr%d" % r], ["zt"])
 
     def placed():
-        latch(T.bsc[:, :], T.brep[:, :], C, ["brep"], ["bsc"])
+        latch(T.bsc[:, :], T.brep[:, :], C, ["brep0", "brep1"], ["bsc"])
         fill()
         listed(T.bl[:, :], T.bsc[:, 15:C:16], ["bsc"], ["bl"])
 
@@ -251,21 +304,36 @@ def rank_program(g, core, T, topo):
             listed(T.ml[:, c0 // 16:c1 // 16], T.msc[:, c0 + 15:c1:16], ["msc%d" % i], ["ml%d" % i])
 
     def state(r, i):
+        def mapped_h(j, b): return T.aw[:, C * b:C * b + C].indirect(T.ml[:, PARTS[j][0] // 16:PARTS[j][1] // 16]), ["aw0.%d" % b, "aw1.%d" % b, "ml%d" % j]
+
+        if r and i == 0:
+            for j, (c0, c1) in enumerate(PARTS):
+                for b in (2, 3): act(T.ag[:, C * (b - 2) + c0:C * (b - 2) + c1], *mapped_h(j, b), ["ag%d.%d" % (j, b)])
         for j, b in ([(0, 0), (0, 1), (0, 2), (0, 3), (1, 0)], [(1, 1), (1, 2), (1, 3)])[i]:
-            c0, c1 = PARTS[j]
-            vtt(T.xr[:, 4 * c0 + b:4 * c1:4], T.aw[:, C * b:C * b + C].indirect(T.ml[:, c0 // 16:c1 // 16]), T.fg[:, C * b + c0:C * b + c1], A.add,
-                ["aw0.%d" % b, "aw1.%d" % b, "ml%d" % j, "fg%d" % b], ["xr%d.%d" % (j, b)])
+            (c0, c1), (a, tags) = PARTS[j], mapped_h(j, b)
+            out = T.xr[:, 4 * c0 + b:4 * c1:4]
+            if r and b >= 2:
+                k = held(r)[b - 2]
+                vtt(out, T.ag[:, C * (b - 2) + c0:C * (b - 2) + c1], T.ps[:, 512 * k + c0:512 * k + c1], A.add, ["ag%d.%d" % (j, b), "bank%d" % k], ["xr%d.%d" % (j, b)])
+            else:
+                vtt(out, a, T.fg[:, C * b + c0:C * b + c1], A.add, tags + ["fg%d" % b], ["xr%d.%d" % (j, b)])
         (q, qs), (c0, c1) = codes(r + 1), PARTS[i]
         quant(q[:, c0:c1], qs[:, c0:c1], T.xr[:, 4 * c0:4 * c1], ["xr%d.%d" % (i, b) for b in range(4)], [qtags(r + 1)[i]])
 
     load("Y", T.sei[:, :], T.se[:, :], "sei", "lse")
-    load("S", T.ub[:, :], T.u[:, :], "ub", "lu")
-    load("Y", T.x0[:, :], T.x[:, :], "x0", "lx")
-    load("S", T.wq[:, :].bitcast(dt.uint8), T.wc[:, :], "wq", "lwc")
-    load("Y", T.wqs[:, :], T.ws[:, :], "wqs", "lws")
-    load("Y", T.vb[:, :], T.v[:, :], "vb", "lv")
-
     op("G", lambda e: e.iota(T.pi[:, :], [[0, 1]], 0, 1), [], ["pi"])
+    order("S", ["pi"], [])
+    load("S", T.x0[:, :], T.x[:, :], "x0", "lx")
+    load("Y", T.wq[:, :].bitcast(dt.uint8), T.wc[:, :], "wq", "lwc")
+    load("S", T.wqs[:, :], T.ws[:, :], "wqs", "lws")
+    load("Y", T.ub[:, :], T.u[:, :], "ub", "lu")
+    order("Y", ["ub"], [])
+    load("Y", T.vb[:, :], T.v[:, :], "vb", "lv")
+    for k in range(0, 128, 16):
+        for h in range(2):
+            g.sync.dma_start(T.sp[k:k + 16, 20 * h:20 * h + 20], T.se[k - k % 32 + 16 * h:k - k % 32 + 16 * h + 16, :]).then_inc(T.sem.lsp, 16)
+    mark([], ["sp"], ("lsp", 256))
+
     iota(T.it[:, 0:C], [[1, C]], 0, 0, ["it0"])
     iota(T.i16[:, :], [[0, 20], [1, 16]], 0, 0, ["i16"])
     iota(T.p4[:, :], [[0, 1]], -3, -4, ["p4"])
@@ -286,85 +354,90 @@ def rank_program(g, core, T, topo):
         iota(ap, pat, base, 0, [E0[j]])
     iota(T.ji[:, :], [[16, 32]], 4 * C, 1, ["ji"])
 
-    bits = {m: T.xi[:, j:j + 1] for j, m in enumerate((15, 8, 4, 2, 1, 3, 7))}
-    ln = {n: T.ln[:, j:j + 1] for j, n in enumerate(("trash", "right", "left", "b1", "b2", "b3", "lane", "at1", "at2", "root", "top", "mid", "none"))}
+    bits = {m: T.xi[:, j:j + 1] for j, m in enumerate((15, 8, 4, 2, 1, 3, 7, 16))}
+    ln = {n: T.ln[:, j:j + 1] for j, n in enumerate(("trash", "right", "left", "b1", "b2", "b3", "lane", "at1", "at2", "root", "top", "mid", "none", "even", "odd"))}
     for m in bits:
         vts(bits[m], T.pi[:, :], m, None, A.bitwise_and, None, ["pi"], ["x%d" % m])
-    vset(T.mk[:, 0:16], 1.0, ["mk1"])
-    vset(T.d0t[:, :], 1.0, ["d0t", "d0t1"])
-    for n, m, s1, s2, o0, o1 in (
-            ("trash", 15, 0.0, 2.0 * C, A.is_equal, A.mult), ("lane", 15, 1.0, None, A.mult, None), ("mid", 15, 16.0, 8.0, A.mult, A.add),
-            ("right", 8, 0.25, None, A.mult, None), ("left", 8, -0.25, 2.0, A.mult, A.add),
-            ("b1", 4, 0.25, None, A.mult, None), ("b2", 2, 0.5, None, A.mult, None), ("b3", 1, 1.0, None, A.mult, None),
-            ("at1", 7, 4.0, 0.5, A.is_equal, A.mult), ("at2", 3, 2.0, None, A.is_equal, None),
-            ("root", 15, 8.0, float(OWN), A.is_equal, A.mult), ("none", 15, 0.0, 256.0, A.is_equal, A.mult)):
-        vts(ln[n], bits[m], s1, s2, o0, o1, ["x%d" % m], [n])
+    made = {
+        "trash": (15, 0.0, 2.0 * C, A.is_equal, A.mult), "lane": (15, 1.0, None, A.mult, None), "mid": (15, 16.0, 8.0, A.mult, A.add),
+        "right": (8, 0.25, None, A.mult, None), "left": (8, -0.25, 2.0, A.mult, A.add),
+        "b1": (4, 0.25, None, A.mult, None), "b2": (2, 0.5, None, A.mult, None), "b3": (1, 1.0, None, A.mult, None),
+        "at1": (7, 4.0, 0.5, A.is_equal, A.mult), "at2": (3, 2.0, None, A.is_equal, None),
+        "root": (15, 8.0, float(OWN), A.is_equal, A.mult), "none": (15, 0.0, 256.0, A.is_equal, A.mult),
+        "even": (16, 0.0, 0.5, A.is_equal, A.mult), "odd": (16, 16.0, 0.5, A.is_equal, A.mult)}
+
+    def lanes(names):
+        for n in names.split():
+            m, s1, s2, o0, o1 = made[n]
+            vts(ln[n], bits[m], s1, s2, o0, o1, ["x%d" % m], [n])
+
+    lanes("trash lane mid right left")
     vcp(T.kid[:, 2 * OWN:2 * OWN + 2 * C:2], T.it[:, 0:C], ["it0"], ["kid0"])
     vcp(T.kid[:, 2 * OWN + 1:2 * OWN + 2 * C:2], T.it[:, 0:C], ["it0"], ["kid1"])
-    vset(T.d0t[:, 32:77:5], 0.0, ["d0t"])
-    vset(T.zt[:, 0:1], 0.0, ["zt"])
-    vset(T.zt[:, 512:520], 0.0, ["zt1"])
-    vset(T.d0t[:, 0:32:16], 0.0, ["d0t1"])
-    vts(T.mk[:, 16:336], T.i16[:, :], ln["lane"], None, A.is_equal, None, ["i16", "lane"], ["mk"])
+    lanes("b1 b2 b3 at1 root")
     act(T.sv[:, :], T.it[:, 0:C], ["it0"], ["sv"], F.Identity, bias=float(OWN))
     act(T.it[:, OWN:OWN + C], T.it[:, 0:C], ["it0"], ["it2"])
-    act(ln["top"], ln["at1"], ["at1", "root"], ["top"], F.Identity, bias=ln["root"], scale=-1.0)
     act(T.subl[:, :], ln["lane"], ["lane"], ["subl"], F.Identity, bias=15360.0, scale=-1024.0)
     act(T.d0r[:, :], T.i16[:, 0:256], ["i16"], ["d0r"], F.Sign)
     act(T.sg[:, :], T.i16[:, 0:16], ["i16", "mid"], ["sg"], F.Sign, bias=ln["mid"], scale=-16.0)
     act(T.ad[:, :], T.i16[:, 0:16], ["i16", "mid"], ["ad"], F.Abs, bias=ln["mid"], scale=-16.0)
-    act(T.d0l[:, :], T.mk[:, 16:336], ["mk"], ["d0l"], F.Identity, bias=1024.0, scale=-66560.0)
+    act(ln["top"], ln["at1"], ["at1", "root"], ["top"], F.Identity, bias=ln["root"], scale=-1.0)
     act(T.ea[:, :], T.it[:, 0:520], ["it0", "it1", "it2", "p4"], ["ea"], F.Abs, bias=T.p4[:, 0:1])
-    for b in range(4):
-        act(T.eb[:, 512 * b:512 * b + 512], T.ea[:, 3 - b:515 - b], ["ea"], ["eb%d" % b], F.Relu, bias=0.5, scale=-1.0)
-    act(T.j4[:, :], T.ji[:, :], ["ji"], ["j4"], scale=0.25)
 
     vts(T.ofl[:, 0:1], T.sei[:, 0:1], ln["trash"], None, A.add, None, ["sei", "trash"], ["ofl0"])
     vcp(T.ofl[:, 1:20], T.sei[:, 1:20], ["sei"], ["ofl"])
+    vts(T.mk[:, 16:336], T.i16[:, :], ln["lane"], None, A.is_equal, None, ["i16", "lane"], ["mk"])
     vcp(T.kid[:, 2 * OWN:2 * OWN + 2 * C + 16].indirect(T.ofl[:, 0:20]), T.sv[:, :], ["ofl", "ofl0", "sv"], ["kid0", "kid1"])
+    lanes("at2 none")
+    vset(T.mk[:, 0:16], 1.0, ["mk1"])
+    vset(T.d0t[:, :], 1.0, ["d0t", "d0t1"])
+    act(T.d0l[:, :], T.mk[:, 16:336], ["mk"], ["d0l"], F.Identity, bias=1024.0, scale=-66560.0)
+    act(T.eb[:, 0:520], T.ea[:, :], ["ea"], ["eb0"], F.Relu, bias=0.5, scale=-1.0)
     KID, kid = ["kid0", "kid1", "kid2"], T.kid[:, 0:2 * OWN + 2 * C]
 
     def pick_u():
         vcp(T.ur[:, 0:128].bitcast(dt.uint32), T.uq[:, 0:128].bitcast(dt.uint32).indirect(T.ull[:, 0:8]), ["uq", "ull"], ["ur"])
         act(T.urs[:, 0:128], T.us[:, 0:128].indirect(T.ull[:, 0:8]), ["uq", "ull"], ["urs"])
-        scores(0, 0)
 
     def first():
         quant(T.q0[:, 0:C], T.qs0[:, 0:C], T.x0[:, 0:1280], ["x0"], ["q0.0"])
         layer(0, 0)
+        scores(0, 0)
 
-    def tiles(b):
-        quant(T.eq[:, 128 * b:128 * b + 128], T.es[:, 128 * b:128 * b + 128], T.eb[:, 512 * b:512 * b + 512], ["eb%d" % b], ["eq%d" % b])
-        if b < 3: return
-        own(0, LAYER[1])
-        for j in range(4): fw("S", j, LAYER[1][j])
-        for j in range(4): fg("S", j)
+    def tiles(j):
+        at = 520 * (j // 4) + 3 - j % 4
+        quant(T.eq[:, 128 * j:128 * j + 128], T.es[:, 128 * j:128 * j + 128], T.eb[:, at:at + 512], ["eb%d" % (j // 4)], ["eq%d" % j])
+        if j != 3: return
+        own(0, four(0, 1))
+        for b in range(4): fw("S", b, four(0, 1)[b])
+        for b in range(4): fg("S", b)
 
-    later(vcp, T.ull[:, :], T.it[:, 0:128:16], ["it0"], ["ull"])
-    later(quant, T.uq[:, :], T.us[:, :], T.ub[:, :], ["ub"], ["uq"])
-    later(vtt, T.an[:, :], T.ad[:, :], T.zz[:, :], A.is_lt, ["ad"] + ZZ, ["an"])
-    later(first)
-    later(vtt, T.w1[:, :], T.sg[:, :], T.zz[:, :], A.mult, ["sg"] + ZZ, ["w1"])
-    later(vts, T.tp[:, 1:2], T.wo[:, 2:3], ln["at1"], ln["top"], A.mult, A.add, ["wo1", "at1", "top"], ["tp1"])
-    later(pick_u)
-    later(vts, T.tp[:, 2:3], T.yt[:, 2:3], ln["at2"], T.tp[:, 1:2], A.mult, A.add, ["yt2", "at2", "tp1"], ["tp2"])
-    later(vtt, T.zl[:, :], T.zz[:, :], T.mk[:, 16:32], A.mult, ZZ + ["mk"], ["zl"])
-    later(vts, T.cl[:, 0:1], T.yt[:, 3:4], ln["b3"], T.tp[:, 2:3], A.mult, A.add, ["yt3", "b3", "tp2"], ["cl0"])
-    later(tiles, 0)
-    later(vtt, T.e0[:, 0:16], T.w1[:, :], T.an[:, :], A.mult, ["w1", "an"], [E0[6]])
-    later(vred, T.zr[:, :], T.zl[:, :], ["zl"], ["zr"])
-    later(vts, T.ai[:, :], T.sei[:, :], 1, None, A.arith_shift_right, None, ["sei"], ["ai"])
-    later(pack, 0, 0)
-    later(vcp, T.parl[:, :], T.ai[:, :], ["ai"], ["parl"])
-    later(tiles, 1)
-    later(vts, T.tm[:, :], T.zz[:, :], T.zr[:, 0:1], -1.0, A.is_le, A.mult, ZZ + ["zr"], ["tm"])
-    later(latch, T.fs[:, :], T.fc[:, :], 128, FC, ["fs"])
-    later(tiles, 2)
-    later(vtt, T.e0[:, 16:32], T.e0[:, 0:16], T.tm[:, :], A.mult, [E0[6], "tm"], [E0[7]])
-    later(listed, T.tl[:, :], T.fs[:, 15:128:16], ["fs"], ["tl"])
-    later(tiles, 3)
-    later(vset, T.e0[:, 0:1], 0.0, [E0[6]])
-    later(vcp, T.e0[:, 16:17], ln["none"], ["none"], [E0[7]])
+    def halves():
+        lanes("even odd")
+        for h, n in ((1, "even"), (2, "odd")):
+            act(T.eb[:, 520 * h:520 * h + 520], T.ea[:, :], ["ea", n], ["eb%d" % h], F.Relu, bias=ln[n], scale=-1.0)
+
+    side = {
+        "ull": (vcp, T.ull[:, :], T.it[:, 0:128:16], ["it0"], ["ull"]), "qu": (quant, T.uq[:, :], T.us[:, :], T.ub[:, :], ["ub"], ["uq"]),
+        "pu": (pick_u,), "first": (first,), "pack": (pack, 0, 0), "halves": (halves,),
+        "sq": (vts, T.sq[:, :], T.sp[:, :], 1, None, A.arith_shift_right, None, ["sp"], ["sq"]), "pair": (vcp, T.pair[:, :], T.sq[:, :], ["sq"], ["pair"]),
+        "ai": (vts, T.ai[:, :], T.sei[:, :], 1, None, A.arith_shift_right, None, ["sei"], ["ai"]), "parl": (vcp, T.parl[:, :], T.ai[:, :], ["ai"], ["parl"]),
+        "tp1": (vts, T.tp[:, 1:2], T.wo[:, 2:3], ln["at1"], ln["top"], A.mult, A.add, ["wo1", "at1", "top"], ["tp1"]),
+        "tp2": (vts, T.tp[:, 2:3], T.yt[:, 2:3], ln["at2"], T.tp[:, 1:2], A.mult, A.add, ["yt2", "at2", "tp1"], ["tp2"]),
+        "cl0": (vts, T.cl[:, 0:1], T.yt[:, 3:4], ln["b3"], T.tp[:, 2:3], A.mult, A.add, ["yt3", "b3", "tp2"], ["cl0"]),
+        "cl1": (vts, T.cl[:, 1:8], T.wv[:, 2:16:2], 0.5, None, A.mult, None, ["wv1a", "wv2a", "wv4a"], ["cl1"]),
+        "an": (vtt, T.an[:, :], T.ad[:, :], T.zz[:, :], A.is_lt, ["ad"] + ZZ, ["an"]), "w1": (vtt, T.w1[:, :], T.sg[:, :], T.zz[:, :], A.mult, ["sg"] + ZZ, ["w1"]),
+        "zl": (vtt, T.zl[:, :], T.zz[:, :], T.mk[:, 16:32], A.mult, ZZ + ["mk"], ["zl"]), "zr": (vred, T.zr[:, :], T.zl[:, :], ["zl"], ["zr"]),
+        "tm": (vts, T.tm[:, :], T.zz[:, :], T.zr[:, 0:1], -1.0, A.is_le, A.mult, ZZ + ["zr"], ["tm"]),
+        "down": (vtt, T.e0[:, 0:16], T.w1[:, :], T.an[:, :], A.mult, ["w1", "an"], [E0[6]]),
+        "back": (vtt, T.e0[:, 16:32], T.e0[:, 0:16], T.tm[:, :], A.mult, [E0[6], "tm"], [E0[7]]),
+        "z0": (vset, T.e0[:, 0:1], 0.0, [E0[6]]), "z16": (vcp, T.e0[:, 16:17], ln["none"], ["none"], [E0[7]]),
+        "j4": (vts, T.j4[:, :], T.ji[:, :], 0.25, None, A.mult, None, ["ji"], ["j4"]),
+        "d0": (vset, T.d0t[:, 32:77:5], 0.0, ["d0t"]), "d1": (vset, T.d0t[:, 0:32:16], 0.0, ["d0t1"]),
+        "fs": (latch, T.fs[:, :], T.fc[:, :], 128, FC, ["fs"]), "tl": (listed, T.tl[:, :], T.fs[:, 15:128:16], ["fs"], ["tl"])}
+    side.update({"t%d" % j: (tiles, j) for j in range(12)})
+    for names in BESIDE.split("|"):
+        later(lambda names=names: [side[n][0](*side[n][1:]) for n in names.split()])
 
     vts(T.tp[:, 0:1], T.kid[:, 2 * OWN + 1:2 * OWN + 2], ln["right"], ln["b1"], A.mult, A.add, ["kid1", "right", "b1"], ["tp0"])
     vts(T.kid[:, 0:2 * C], T.kid[:, 2 * OWN:2 * OWN + 2 * C], OWN - 1, None, A.bitwise_and, None, ["kid0", "kid1"], ["kid2"])
@@ -395,9 +468,7 @@ def rank_program(g, core, T, topo):
         yield
 
     for n in (1, 2, 4):
-        if n == 4: spare.insert(0, lambda: vts(T.cl[:, 1:8], T.wv[:, 2:16:2], 0.5, None, A.mult, None, ["wv1a", "wv2a", "wv4a"], ["cl1"]))
-        for _c in below(n): fill(2)
-    fill(len(spare))
+        for _c in below(n): fill()
 
     chain, leaves = positions(0), below(8)
     next(chain)
@@ -414,46 +485,55 @@ def rank_program(g, core, T, topo):
     next(chain)
     labels(1)
     labels(2)
-    prep(0)
+    prep(0, "SS")
     vts(T.ol[:, :], T.o32[:, :], 4.0, None, A.mult, None, ["o32a", "o32b"], ["ol"])
     vcp(T.ci[:, :], T.cl[:, 0:16], ["cl0", "cl1", "cl8"], ["ci"])
     vcp(T.at[:, :].indirect(T.ol[:, 0:32]), T.it[:, 0:512], ["ol", "it0", "it1"], ["at"])
     vts(T.cj[:, :], T.ci[:, :], OWN - 1, None, A.bitwise_and, None, ["ci"], ["cj"])
+    fill()
     latch(T.als[:, :], T.at[:, 4 * OWN:4 * (OWN + C):4], C, ["at"], ["als"])
     vcp(T.ls[:, :], T.cj[:, :], ["cj"], ["ls"])
+    fill()
     listed(T.al[:, :], T.als[:, 15:C:16], ["als"], ["al"])
+    fill()
     spread(0)
-    brep()
-    arrived(0, 0, LAYER[0])
+    brep("SS")
+    arrived(0, 0, four(0, 0))
     zt(0)
     placed()
     mapped(0)
 
     for r in (1, 2):
-        spread(r)
+        far = relay[r] is not None
+        if r == 1: spread(r)
         state(r - 1, 0)
-        layer(r, 0)
+        if r == 2: spread(r)
+        layer(r, 0, 3)
         scores(r, 0)
         state(r - 1, 1)
         scores(r, 1)
+        scaled("V", r, 0, 3)
         layer(r, 1)
-        pack(r, 0)
-        own(r, LAYER[0])
-        for _c in positions(r): pass
-        pack(r, 1)
-        fw("S", 0, LAYER[0][0])
-        prep(r)
-        for b in (1, 2, 3): fw("V", b, LAYER[0][b])
-        brep()
         if r == 1: quant(T.vq[:, :], T.vs[:, :], T.vb[:, :], ["vb"], ["vq"])
-        fg("V", 0)
+        pack(r, 0)
+        for j in range(5): pick("S", r, j)
+        gaps = [(pick, "V", r, 0), (pack, r, 1), (pick, "V", r, 1), (pick, "V", r, 2), (pick, "V", r, 3)]
+        for _c, gap in zip(positions(r), gaps): gap[0](*gap[1:])
+        above(r, 0)
+        post(r, 1)
+        prep(r)
+        pick("V", r, 4)
+        brep()
         placed()
-        for b in (1, 2, 3): fg("S", b)
-        if relay[r] is None: arrived(r, 0, LAYER[1])
+        if not far: arrived(r, 0, four(r, 1))
+        above(r, 1)
+        for b in range(2): kept(r, b)
         zt(r)
         mapped(r)
-        arrived(r, 1, LAYER[0])
-        if relay[r] is not None: arrived(r, 0, LAYER[1])
+        if far:
+            arrived(r, 0, four(r, 1))
+            arrived(r, 1, four(r, 2), ((2, "S"), (0, "V"), (3, "S"), (1, "V")))
+        else: arrived(r, 1, four(r, 2))
     store("Y", T.im[:, :], T.mr[0:128:16, :], ["mr0", "mr1"])
 
     for i, (c0, c1) in enumerate(PARTS):

@@ -2,13 +2,18 @@ from concourse.mybir import dt, AluOpType, AxisListType, ActivationFunctionType
 
 C = 320
 MACHINE = 64
-MATE = False
 STEP = [1, 2, 4]
 PARTS = [(0, 192), (192, 320)]
-WAYS = {True: ([("q", 0, 144), ("s", 192, 320)], [("q", 144, 192), ("s", 0, 192), ("q", 192, 320)]), False: ([("q", 0, 192), ("s", 192, 320)], [("s", 0, 192), ("q", 192, 320)])}
-ASIDE = False
+HANDED, DIRECT = [("q", 0, 144), ("s", 192, 320)], [("q", 144, 192), ("s", 0, 192), ("q", 192, 320)]
 OWN = 512
-BESIDE = "ull an w1|zl tp1 down|zr qu|pu|tp2 tm ai halves|first|t0 cl0|t1 parl|back d0 d1|fs z0|t2 z16|tl t3|t4|pack|t5|j4 t6|cl1 t7|t8||t9|t10|t11 sq|pair"
+ROUNDS = [
+    'sublS sv way1S way2S midS it2 trash some kid0 kid1 wayS subl1S mk1S sg d0tS ofl ofl0 ull kid w1 m4 mk * ad up0S d0r an q0 * * qu layer0 * ai down * up1 up3 * d0l ea h00S h01S z0S pu zt0S h03S h02S sc0 d1S sg0 * fs * zl * par zr * one own tm * tl upm back * top pack0 wu cl0 xp01S eb xp11S sg1 d0S * t0 * t1 cl1 * s1 * clab t2 st pos yf * pos * lab0 ci pos o16 t3 xp20S xp00S xp10S xp30S xp31S xp21S pos ol st0 pos lab1 lab2 at pq lr1S lr0S ar1V cj un0 above zt ar0S aw00S aw02S als af aw01S aw03S met0S k0S met1V al ls mr0V mr1S k1S msc0 msc1 ml0 ml1',
+    'ag02S x00 x10 x01 ag03S ag13S ag12S lr0S lr1S x03 x02 x11 x13 x12 q0 q1 sc0 sc1 xp20S sg0 layer0 xp10V xp01V xp00V sg1 layer1 h00S pos h11V h01S h03S h02S h13S h10S h12S pos pack0 pos xp11V xp30S xp21S xp31S pos pos pack1 post1 prep0S prep1V pq brep0S brep1V un0 above bsc aw02S aw01S aw03S aw00S k0S zt bl un1 aw12S aw10S aw11S vq mr0V mr1S k1S aw13V msc0 msc1 ml0 ml1',
+    'x00 x01 lr1S ag02S ag03S x02 ag12S ag13S lr0S x03 x11 q0 layer0 sc0 x10 x12 x13 h01S h00S sg0 q1 sc1 sg1 h02V layer1 h03V xp00S xp01S xp11S h13S h12S h11S pack0 h10S pos pos xp21V xp31S xp20S pos xp30V pos pack1 pos post1 prep0S xp10S prep1V brep1V pq brep0S above un0 bsc zt k0S k1S bl mr0V aw02S aw00S aw03S aw01S un1 mr1V msc0 msc1 aw10S aw12S ml0 aw13S ml1 aw11V',
+    'x00 ag02S x01 ag03S x02 x03 x11 ag12S ag13S q0 x13 x10 x12 im out0S q1 out1V']
+LEAVES = "S"
+CUT = [160, 192, 192]
+HELD = [(0, 2), (0, 3), (1, 2), (1, 3)]
 A = AluOpType
 F = ActivationFunctionType
 
@@ -17,23 +22,22 @@ for _n, _w, _d in (
         ("x0", 1280, "bfloat16"), ("ub", 512, "bfloat16"), ("vb", 512, "bfloat16"), ("sei", 20, "int32"),
         ("uq", 128, "float8_e4m3fn_x4"), ("us", 128, "uint8"), ("ur", 128, "float8_e4m3fn_x4"), ("urs", 128, "uint8"),
         ("vq", 128, "float8_e4m3fn_x4"), ("vs", 128, "uint8"), ("wq", 512, "float8_e4m3fn_x4"), ("wqs", 512, "uint8"),
-        ("ea", 520, "bfloat16"), ("eb", 1560, "bfloat16"), ("eq", 1536, "float8_e4m3fn_x4"), ("es", 1536, "uint8"),
-        ("sp", 40, "int32"), ("sq", 40, "int32"), ("pair", 40, "uint16"), ("ag", 640, "bfloat16"),
-        ("pq1", 640, "float8_e4m3fn_x4"), ("pqs1", 640, "uint8"), ("pq2", 640, "float8_e4m3fn_x4"), ("pqs2", 640, "uint8"),
-        ("pi", 1, "int32"), ("p4", 1, "float32"), ("xi", 8, "int32"), ("ln", 16, "float32"),
-        ("i16", 320, "float32"), ("it", OWN + C, "float32"), ("sv", 320, "float32"),
-        ("mk", 336, "bfloat16"), ("d0r", 256, "bfloat16"), ("d0l", 320, "float32"), ("d0t", 80, "float32"), ("subl", 1, "float32"),
+        ("ea", 520, "bfloat16"), ("eb", 520, "bfloat16"), ("eq", 512, "float8_e4m3fn_x4"), ("es", 512, "uint8"),
+        ("xp", 1280, "bfloat16"), ("pq", 320, "float8_e4m3fn_x4"), ("pqs", 320, "uint8"),
+        ("pi", 1, "int32"), ("p4", 1, "float32"), ("xi", 8, "int32"), ("ln", 24, "float32"),
+        ("i16", 320, "bfloat16"), ("it", OWN + C, "float32"), ("sv", 320, "float32"), ("kr", 256, "float32"),
+        ("mk", 336, "bfloat16"), ("d0r", 256, "bfloat16"), ("d0l", 320, "float32"), ("d0t", 96, "float32"),
         ("zz", 16, "float32"), ("ad", 16, "float32"), ("sg", 16, "float32"), ("an", 16, "float32"),
         ("w1", 16, "float32"), ("zl", 16, "float32"), ("zr", 1, "float32"), ("tm", 16, "float32"),
-        ("ji", 32, "float32"), ("j4", 32, "float32"), ("fc", 128, "float32"), ("fs", 128, "float32"), ("tl", 8, "uint16"), ("ull", 8, "uint16"),
-        ("ai", 20, "int32"), ("ofl", 20, "uint16"), ("parl", 20, "uint16"), ("kid", 2 * OWN + 2 * C + 16, "int32"), ("wo", 8, "uint16"), ("wv", 32, "uint16"),
-        ("g16", 48, "float32"), ("yt", 8, "float32"), ("tp", 4, "float32"), ("gg", 512, "float32"), ("gs", 512, "float32"),
-        ("cl", 32, "uint16"), ("ci", 16, "int32"), ("cj", 16, "int32"), ("ls", 16, "uint16"), ("yf", 16, "float32"), ("o32", 32, "float32"), ("ol", 32, "uint16"),
-        ("at", 4 * (OWN + C), "float32"), ("als", 320, "float32"), ("al", 20, "uint16"),
-        ("tb", OWN + C, "bfloat16"), ("sm", 496, "bfloat16"), ("e0", 80, "float32"), ("e1", 80, "float32"),
-        ("pp", 80, "float32"), ("prep", 512, "float32"), ("brep", 320, "float32"), ("bsc", 320, "float32"), ("bl", 20, "uint16"),
+        ("ji", 16, "float32"), ("fc", 144, "float32"), ("fs", 144, "float32"), ("tl", 8, "uint16"), ("ull", 8, "uint16"), ("m4", 128, "bfloat16"), ("one", 15, "float32"),
+        ("ai", 20, "int32"), ("ofl", 20, "uint16"), ("parl", 80, "uint16"), ("kid", 2 * OWN + 2 * C + 16, "int32"), ("wo", 132, "uint16"), ("wv", 34, "uint16"),
+        ("g4", 128, "float32"), ("yt", 2, "float32"), ("up", 15, "float32"), ("upm", 15, "float32"), ("gg", 512, "float32"), ("gs", 512, "float32"),
+        ("cl", 34, "uint16"), ("ci", 16, "int32"), ("cj", 16, "int32"), ("ls", 16, "uint16"), ("yf", 16, "float32"), ("o16", 16, "float32"), ("ol", 16, "uint16"),
+        ("at", 4 * (OWN + C), "float32"), ("ar", 320, "float32"), ("als", 320, "float32"), ("s1", 20, "int32"), ("st", 20, "float32"), ("af", 20, "float32"), ("al", 20, "uint16"),
+        ("tb", OWN + C, "bfloat16"), ("sm", 496, "bfloat16"), ("e0", 96, "float32"), ("e1", 96, "float32"),
+        ("pp", 96, "float32"), ("prep", 512, "float32"), ("brep", 320, "float32"), ("bsc", 320, "float32"), ("bl", 20, "uint16"),
         ("zt", 520, "float32"), ("msc", 320, "float32"), ("ml", 20, "uint16"), ("mr", 320, "float32"), ("ysb", 320, "float32"),
-        ("fw", 1280, "bfloat16"), ("fg", 1280, "bfloat16"), ("aw", 1280, "bfloat16"),
+        ("fg", 640, "bfloat16"), ("aw", 1280, "bfloat16"), ("ag", 1280, "bfloat16"),
         ("pl", 96, "uint16"), ("pa", 96, "uint16"), ("ll", 96, "uint16"), ("lr", 1536, "float32")):
     SCRATCH[_n] = ("sbuf", [128, _w], _d)
 for _r in range(2):
@@ -46,7 +50,7 @@ for _r in range(3):
     SCRATCH["lq%d" % _r] = ("sbuf", [128, 320], "float8_e4m3fn_x4")
     SCRATCH["ls%d" % _r] = ("sbuf", [128, 320], "uint8")
 
-SEMAPHORES = ["cV", "cS", "cT", "cG", "sent", "stored", "lse", "lsp", "lx", "lu", "lv", "lwc", "lws"] + ["hand%d" % _j for _j in range(4)]
+SEMAPHORES = ["cV", "cS", "cT", "cG", "sent", "stored", "lse", "lx", "lu", "lv", "lwc", "lws"] + ["hand%d" % _j for _j in range(len(HANDED))]
 for _r in range(3):
     SEMAPHORES += ["pr%d" % _r, "lb%d" % _r, "h%d_0" % _r, "h%d_1" % _r]
 
@@ -55,19 +59,8 @@ def relay_of(T, topo, rank, s):
     core, dst = T.cores[rank], T.cores[rank ^ s]
     if topo.chip(core) == topo.chip(dst): return None
     mine = [c for c in topo.cores_of(core) if T.rank_of(c) is not None]
-    beside = [c for c in range(MACHINE) if topo.mates(topo.chip(c), topo.chip(dst)) and topo.die(c) == topo.die(core) and topo.may_write(c, dst)]
-    able = [c for c in mine if all(topo.may_write(c, b) for b in beside)]
-    if MATE and core in able: return beside[able.index(core) % len(beside)]
     free = [c for c in topo.cores_of(core) if T.rank_of(c) is None and topo.die(c) != topo.die(core) and topo.may_write(c, dst)]
     return free[mine.index(core) % len(free)]
-
-
-def ways(topo, core, relay):
-    return WAYS[topo.chip(core) == topo.chip(relay)]
-
-
-def aside(topo, core, relay, dst):
-    return [e for e in topo.engines(core, relay) if e not in topo.engines(core, dst) or not ASIDE] or topo.engines(core, relay)
 
 
 def piece(T, side, kind, r, a, b):
@@ -81,14 +74,14 @@ def hand_on(g, core, T, topo):
             if relay_of(T, topo, rank, s) != core: continue
             src, dst = T.cores[rank], T.cores[rank ^ s]
             rid, pid, _s = topo.addr(dst)
-            m, n, handed = topo.mask(core, dst), len(topo.engines(core, dst)), ways(topo, src, core)[0]
+            m, n, come = topo.mask(core, dst), len(topo.engines(core, dst)), len(topo.engines(src, core))
             ll = T.ll[:, 32 * k:32 * k + 32]
-            g.wait_ge(T.sem["lb%d" % k], len(topo.engines(src, core)))
+            g.wait_ge(T.sem["lb%d" % k], come)
             g.remote_dma(ll, ll, T.sem["lb%d" % k], T.sem.sent, pid, rid, m)
-            for j, (kind, a, b) in enumerate(handed):
-                g.wait_ge(T.sem["hand%d" % j], len(aside(topo, src, core, dst)))
+            for j, (kind, a, b) in enumerate(HANDED):
+                g.wait_ge(T.sem["hand%d" % j], come)
                 g.remote_dma(piece(T, "l", kind, k, a, b), piece(T, "h", kind, k, a, b), T.sem["h%d_%d" % (k, a >= PARTS[1][0])], T.sem.sent, pid, rid, m)
-            g.wait_ge(T.sem.sent, (1 + len(handed)) * n)
+            g.wait_ge(T.sem.sent, (1 + len(HANDED)) * n)
 
 
 def rank_program(g, core, T, topo):
@@ -151,13 +144,16 @@ def rank_program(g, core, T, topo):
     def vred(out, in_, r, w): op("V", lambda e: e.tensor_reduce(out, in_, AxisListType.X, A.add), r, w)
     def vscan(out, d0, d1, ini, o0, o1, r, w): op("V", lambda e: e.tensor_tensor_scan(out, d0, d1, ini, o0, o1), r, w)
     def iota(ap, pat, base, cm, w): op("G", lambda e: e.iota(ap, pat, base, cm, allow_small_or_imprecise_dtypes=True), [], w)
-    def act(out, in_, r, w, f=F.Copy, **k): op("S", lambda e: e.activation(out, in_, f, **k), r, w)
+    def act(out, in_, r, w, f=F.Copy, bias=None, scale=None):
+        k = {n: v for n, v in (("bias", bias), ("scale", scale)) if v is not None}
+        op("S", lambda e: e.activation(out, in_, f, **k), r, w)
+
     def quant(c, s, t, r, w): op("V", lambda e: e.quantize_mx(c, s, t), r, w)
     def copy(q, *a): (vcp if q == "V" else act)(*a)
 
-    def mm(bank, lc, lsc, rc, rsc, r, n=C, start=True, stop=True):
+    def mm(bank, lc, lsc, rc, rsc, r, n=C):
         out = T.ps[:, 512 * bank:512 * bank + n]
-        op("T", lambda e: e.matmul_mx(out, lc, lsc, rc, rsc, start, stop), r, ["bank%d" % bank])
+        op("T", lambda e: e.matmul_mx(out, lc, lsc, rc, rsc, True, True), r, ["bank%d" % bank])
 
     def bank(b, n=C): return T.ps[:, 512 * b:512 * b + n]
 
@@ -165,49 +161,40 @@ def rank_program(g, core, T, topo):
         vscan(out, T.d0l[:, 0:n], row, 0.0, A.add, A.max, r + ["d0l"], w)
 
     def listed(out, latched, r, w):
-        vts(out, latched, T.subl[:, 0:1], None, A.subtract, None, r + ["subl"], w)
+        vts(out, latched, ln["subl"], None, A.subtract, None, r + ["subl"], w)
 
     sent = [0]
 
-    def send(out, in_, rsem, dst, r, engines=None):
+    def send(out, in_, rsem, dst, r):
         order("G", r, [])
         rid, pid, _s = topo.addr(dst)
-        engines = engines or topo.engines(core, dst)
-        g.remote_dma(out, in_, T.sem[rsem], T.sem.sent, pid, rid, sum(1 << e for e in engines))
-        sent[0] += len(engines)
-
-    spare = []
-
-    def later(f, *a, **k): spare.append(lambda: f(*a, **k))
-
-    def fill(n=1):
-        for _i in range(n):
-            if spare: spare.pop(0)()
+        g.remote_dma(out, in_, T.sem[rsem], T.sem.sent, pid, rid, topo.mask(core, dst))
+        sent[0] += len(topo.engines(core, dst))
 
     partner = [T.cores[rank ^ s] for s in STEP]
     relay = [relay_of(T, topo, rank, s) for s in STEP]
     theirs = [relay_of(T, topo, rank ^ s, s) for s in STEP]
 
     def codes(r): return T["q%d" % (r % 2)], T["qs%d" % (r % 2)]
-    def runs(r): return PARTS if r else [(0, C)]
+    def runs(r): return [(0, CUT[r - 1]), (CUT[r - 1], C)] if r else [(0, C)]
     def qtags(r): return ["q%d.%d" % (r % 2, i) for i in range(len(runs(r)))]
-    def held(r): return [[3, 4], [6, 7]][r % 2]
-    def four(r, i): return [[1, 2] + held(r), held(r + 1) + [0, 5], [1, 2] + held(r + 1)][i]
+    LAYER = [[4, 5, 6, 7], [2, 3, 0, 1]]
 
     def scores(r, i):
         (q, qs), (c0, c1) = codes(r), runs(r)[i]
-        mm(5 * i, T.ur[:, 0:128], T.urs[:, 0:128], q[:, c0:c1], qs[:, c0:c1], [qtags(r)[i], "ur", "urs"], c1 - c0)
-        act(T.tb[:, c0:c1], bank(5 * i, c1 - c0), ["bank%d" % (5 * i)], ["tb%d" % i], F.Sign, bias=2.0 ** -100)
-        if r == 0: act(T.tb[:, OWN:OWN + C], bank(0), ["bank0"], ["tb1"], F.Sign, bias=2.0 ** -100)
+        mm(i, T.ur[:, 0:128], T.urs[:, 0:128], q[:, c0:c1], qs[:, c0:c1], [qtags(r)[i], "ur", "urs"], c1 - c0)
 
-    def layer(r, i, n=4):
+    def signs(r, i):
+        (c0, c1), k = (runs(r)[i], i) if r else ((OWN * i, OWN * i + C), 0)
+        act(T.tb[:, c0:c1], bank(k, c1 - c0), ["bank%d" % k], ["tb%d" % i], F.Sign, bias=2.0 ** -100)
+
+    def layer(r, i):
         (q, qs), (c0, c1) = codes(r), runs(r)[i]
-        for b, k in enumerate(four(r, i)):
+        for b, k in enumerate(LAYER[i]):
             mm(k, T.wq[:, 128 * b:128 * b + 128], T.wqs[:, 128 * b:128 * b + 128], q[:, c0:c1], qs[:, c0:c1], [qtags(r)[i], "wq", "wqs"], c1 - c0)
-        for b in range(n): scaled("S", r, i, b)
 
     def scaled(e, r, i, b):
-        (c0, c1), k = runs(r)[i], four(r, i)[b]
+        (c0, c1), k = runs(r)[i], LAYER[i][b]
         out, tags = T.hb[:, 4 * c0 + b:4 * c1:4], (["bank%d" % k], ["hb%d.%d" % (i, b)])
         if e == "S": act(out, bank(k, c1 - c0), *tags, scale=0.03125)
         else: vts(out, bank(k, c1 - c0), 0.03125, None, A.mult, None, *tags)
@@ -215,110 +202,104 @@ def rank_program(g, core, T, topo):
     def pack(r, i):
         (c0, c1), hq, hs, t = runs(r)[i], T["hq%d" % r], T["hs%d" % r], "hq%d.%d" % (r, i)
         quant(hq[:, c0:c1], hs[:, c0:c1], T.hb[:, 4 * c0:4 * c1], ["hb%d.%d" % (i, b) for b in range(4)], [t])
-        for j, (kind, a, b) in enumerate(ways(topo, core, relay[r])[0] if relay[r] is not None else []):
-            if c0 <= a < c1: send(piece(T, "h", kind, r, a, b), piece(T, "h", kind, r, a, b), "hand%d" % j, relay[r], [t], aside(topo, core, relay[r], partner[r]))
+        for j, (kind, a, b) in enumerate(HANDED if relay[r] is not None else []):
+            if c0 <= a < c1: send(piece(T, "h", kind, r, a, b), piece(T, "h", kind, r, a, b), "hand%d" % j, relay[r], [t])
         if i == 0: post(r, i)
 
     def post(r, i):
         c0, c1 = runs(r)[i]
-        mine = come = [], [("q", c0, c1), ("s", c0, c1)]
-        if relay[r] is not None: mine, come = ways(topo, core, relay[r]), ways(topo, partner[r], theirs[r])
-        for kind, a, b in mine[1]:
+        come = (HANDED, DIRECT) if relay[r] is not None else ([], [("q", c0, c1), ("s", c0, c1)])
+        for kind, a, b in come[1]:
             if c0 <= a < c1: send(piece(T, "l", kind, r, a, b), piece(T, "h", kind, r, a, b), "h%d_%d" % (r, i), partner[r], ["hq%d.%d" % (r, i)])
-        lastw["lq%d.%d" % (r, i)] = ("h%d_%d" % (r, i), sum(len(topo.engines(src, core)) for src, pieces in zip((theirs[r], partner[r]), come) for kind, a, b in pieces if c0 <= a < c1))
+        mark([], ["lq%d.%d" % (r, i)], ("h%d_%d" % (r, i), sum(len(topo.engines(src, core)) for src, pieces in zip((theirs[r], partner[r]), come) for kind, a, b in pieces if c0 <= a < c1)))
 
-    def unpack(banks, q, qs, r, n):
-        for b, k in enumerate(banks):
-            mm(k, T.eq[:, 128 * b:128 * b + 128], T.es[:, 128 * b:128 * b + 128], q, qs, r + ["eq%d" % b], n)
+    XR = ["xr%d.%d" % (i, b) for i in range(2) for b in range(4)]
 
-    def own(r, banks):
-        q, qs = codes(r)
-        unpack(banks, q[:, 0:C], qs[:, 0:C], qtags(r), C)
+    def laid(e, r, b, h):
+        x, tags = (T.xr, XR) if r else (T.x0, ["x0"])
+        copy(e, T.xp[:, 640 * h + b:640 * h + 640:4], x[:, 0:4 * C].indirect(T.parl[:, 20 * b + 10 * h:20 * b + 10 * h + 10]), tags + ["par%d" % b], ["xp%d.%d" % (b, h)])
 
-    def fw(e, b, k): copy(e, T.fw[:, C * b:C * b + C], bank(k), ["bank%d" % k], ["fw%d" % b])
-    def fg(e, b): copy(e, T.fg[:, C * b:C * b + C], T.fw[:, C * b:C * b + C].indirect(T.parl[:, 0:20]), ["fw%d" % b, "parl"], ["fg%d" % b])
+    def requant(): quant(T.pq[:, :], T.pqs[:, :], T.xp[:, :], ["xp%d.%d" % (b, h) for b in range(4) for h in range(2)], ["pq"])
 
-    def pick(e, r, j):
-        (q, qs), at = codes(r), T.pair[:, 8 * j:8 * j + 8]
-        if e == "V": vcp(T["pq%d" % r][:, 128 * j:128 * j + 128].bitcast(dt.uint32), q[:, 0:C].bitcast(dt.uint32).indirect(at), qtags(r) + ["pair"], ["pq%d" % j])
-        else: act(T["pqs%d" % r][:, 128 * j:128 * j + 128], qs[:, 0:C].indirect(at), qtags(r) + ["pair"], ["pqs%d" % j])
+    def above(r):
+        for b in range(4):
+            mm(b, T.eq[:, 128 * b:128 * b + 128], T.es[:, 128 * b:128 * b + 128], T.pq[:, :], T.pqs[:, :], ["pq", "eq%d" % b])
 
-    def above(r, h):
-        for b, k in enumerate(four(r, 0)):
-            j = 4 + 4 * h + b
-            mm(k, T.eq[:, 128 * j:128 * j + 128], T.es[:, 128 * j:128 * j + 128], T["pq%d" % r][:, C * h:C * h + C], T["pqs%d" % r][:, C * h:C * h + C],
-               [t % n for t in ("pq%d", "pqs%d") for n in range(2 * h, 2 * h + 3)] + ["eq%d" % j], C, h == 0, h == 1)
+    def kept(e, r, b):
+        c0, c1 = 0, max(cut(r, j)[1] for j in range(2) if (j, b) not in HELD)
+        copy(e, T.fg[:, C * b + c0:C * b + c1], bank(b, c1), ["bank%d" % b], ["fg%d" % b])
 
-    def kept(r, b): act(T.fg[:, C * b:C * b + C], bank(four(r, 0)[b]), ["bank%d" % four(r, 0)[b]], ["fg%d" % b])
-
-    def arrived(r, i, banks, turns=((0, "S"), (1, "S"), (2, "S"), (3, "S"))):
+    def arrived(r, i):
         c0, c1 = runs(r)[i]
-        for b, e in turns:
-            mm(banks[b], T.eq[:, 128 * b:128 * b + 128], T.es[:, 128 * b:128 * b + 128], T["lq%d" % r][:, c0:c1], T["ls%d" % r][:, c0:c1], ["lq%d.%d" % (r, i), "eq%d" % b], c1 - c0)
-        for b, e in turns:
-            copy(e, T.aw[:, C * b + c0:C * b + c1], bank(banks[b], c1 - c0), ["bank%d" % banks[b]], ["aw%d.%d" % (i, b)])
+        for b in (2, 0, 3, 1):
+            mm(4 + b, T.eq[:, 128 * b:128 * b + 128], T.es[:, 128 * b:128 * b + 128], T["lq%d" % r][:, c0:c1], T["ls%d" % r][:, c0:c1], ["lq%d.%d" % (r, i), "eq%d" % b], c1 - c0)
+
+    def taken(e, r, i, b):
+        (c0, c1), k = runs(r)[i], 4 + b
+        copy(e, T.aw[:, C * b + c0:C * b + c1], bank(k, c1 - c0), ["bank%d" % k], ["aw%d.%d" % (i, b)])
 
     E0 = ["e0.%d" % j for j in range(10)]
 
     def positions(r):
         eo, en, te, tn = (T.e0, T.e1, E0, ["e1"]) if r % 2 == 0 else (T.e1, T.e0, ["e1"], E0)
-        signs = T.tb[:, 0:C].indirect(T.ls[:, 0:16]) if r else T.tb[:, 0:OWN + C].indirect(T.cl[:, 0:16])
+        turns = T.tb[:, 0:C].indirect(T.ls[:, 0:16]) if r else T.tb[:, 0:OWN + C].indirect(T.cl[:, 0:16])
         pl = T.pl[:, 32 * r:32 * r + 32]
-        yield vtt(T.sm[:, 240:496], signs, T.mk[:, 0:256], A.mult, ["tb0", "tb1", "mk", "mk1", "ls" if r else "cl0", "cl1", "cl8"], ["mg"])
+        yield vtt(T.sm[:, 240:496], turns, T.mk[:, 0:256], A.mult, ["tb0", "tb1", "mk", "mk1", "ls" if r else "cl0", "cl1", "cl8"], ["mg"])
         yield vscan(T.sm[:, 0:240], T.d0r[:, 0:240], T.sm[:, 256:496], 0.0, A.mult, A.add, ["mg", "d0r"], ["sc"])
-        yield vtt(en[:, :], T.sm[:, 0:256].indirect(T.tl[:, 0:5]), eo[:, :], A.mult, ["sc", "mg", "tl"] + te, tn)
+        yield vtt(en[:, :], T.sm[:, 0:256].indirect(T.tl[:, 0:6]), eo[:, :], A.mult, ["sc", "mg", "tl"] + te, tn)
         yield vscan(T.pp[:, :], T.d0t[:, :], en[:, :], 0.0, A.mult, A.add, tn + ["d0t", "d0t1"], ["pp"])
-        vts(pl, T.pp[:, 16:80].indirect(T.tl[:, 6:8]), T.pp[:, 15:16], 256.0, A.add, A.add, ["pp", "tl"], ["pl%d" % r])
+        vts(pl, T.pp[:, 16:96].indirect(T.tl[:, 6:8]), T.pp[:, 15:16], 256.0, A.add, A.add, ["pp", "tl"], ["pl%d" % r])
         send(T.pa[:, 32 * r:32 * r + 32], pl, "pr%d" % r, partner[r], ["pl%d" % r])
-        lastw["pa%d" % r] = ("pr%d" % r, len(topo.engines(core, partner[r])))
+        mark([], ["pa%d" % r], ("pr%d" % r, len(topo.engines(core, partner[r]))))
         yield
 
     def labels(k):
-        send(T.ll[:, 32 * k:32 * k + 32], T.cl[:, 0:32], "lb%d" % k, relay[k] or partner[k], ["cl0", "cl1", "cl8", "cl16"])
-        lastw["ll%d" % k] = ("lb%d" % k, len(topo.engines(theirs[k] or partner[k], core)))
+        send(T.ll[:, 32 * k:32 * k + 32], T.cl[:, 2:34], "lb%d" % k, relay[k] or partner[k], ["cl1", "cl8", "cl16", "clab"])
+        mark([], ["ll%d" % k], ("lb%d" % k, len(topo.engines(theirs[k] or partner[k], core))))
 
-    def spread(k):
-        act(T.lr[:, 512 * k:512 * k + 512], T.it[:, :].indirect(T.ll[:, 32 * k:32 * k + 32]), ["it0", "it1", "it2", "ll%d" % k], ["lr%d" % k])
+    def spread(e, k, h):
+        j = 2 * k + h
+        copy(e, T.lr[:, 256 * j:256 * j + 256], T.it[:, :].indirect(T.ll[:, 16 * j:16 * j + 16]), ["it0", "it1", "it2", "ll%d" % k], ["lr%d" % j])
 
-    def prep(r, ee="SV"):
-        for h, e in enumerate(ee):
-            copy(e, T.prep[:, 256 * h:256 * h + 256], T.it[:, 0:520].indirect(T.pl[:, 32 * r + 16 * h:32 * r + 16 * h + 16]), ["it0", "it1", "it2", "pl%d" % r], ["prep%d" % h])
+    def prep(e, r, h):
+        copy(e, T.prep[:, 256 * h:256 * h + 256], T.it[:, 0:520].indirect(T.pl[:, 32 * r + 16 * h:32 * r + 16 * h + 16]), ["it0", "it1", "it2", "pl%d" % r], ["prep%d" % h])
 
-    def brep(ee="SV"):
-        for h, e in enumerate(ee):
-            copy(e, T.brep[:, 160 * h:160 * h + 160], T.prep[:, :].indirect(T.al[:, 10 * h:10 * h + 10]), ["prep0", "prep1", "al"], ["brep%d" % h])
+    def brep(e, h):
+        copy(e, T.brep[:, 160 * h:160 * h + 160], T.prep[:, :].indirect(T.al[:, 10 * h:10 * h + 10]), ["prep0", "prep1", "al"], ["brep%d" % h])
 
-    def zt(r): vcp(T.zt[:, :].indirect(T.pa[:, 32 * r:32 * r + 32]), T.lr[:, 512 * r:512 * r + 512], ["pa%d" % r, "lr%d" % r], ["zt"])
+    def zt(r): vcp(T.zt[:, :].indirect(T.pa[:, 32 * r:32 * r + 32]), T.lr[:, 512 * r:512 * r + 512], ["pa%d" % r, "lr%d" % (2 * r), "lr%d" % (2 * r + 1)], ["zt"])
 
-    def placed():
-        latch(T.bsc[:, :], T.brep[:, :], C, ["brep0", "brep1"], ["bsc"])
-        fill()
-        listed(T.bl[:, :], T.bsc[:, 15:C:16], ["bsc"], ["bl"])
+    def placed(): latch(T.bsc[:, :], T.brep[:, :], C, ["brep0", "brep1"], ["bsc"])
 
-    def mapped(r):
-        for e, (i, (c0, c1)) in zip("VS", enumerate(PARTS)):
-            copy(e, T.mr[:, c0:c1], T.zt[:, :].indirect(T.bl[:, c0 // 16:c1 // 16]), ["zt", "bl"], ["mr%d" % i])
-        for i, (c0, c1) in enumerate(PARTS):
-            latch(T.msc[:, c0:c1], T.mr[:, c0:c1], c1 - c0, ["mr%d" % i], ["msc%d" % i])
-        for i, (c0, c1) in enumerate(PARTS):
-            listed(T.ml[:, c0 // 16:c1 // 16], T.msc[:, c0 + 15:c1:16], ["msc%d" % i], ["ml%d" % i])
+    def met(e, h):
+        copy(e, T.prep[:, 256 * h:256 * h + 256], T.zt[:, :].indirect(T.pl[:, 16 * h:16 * h + 16]), ["zt", "pl0"], ["prep%d" % h])
 
-    def state(r, i):
-        def mapped_h(j, b): return T.aw[:, C * b:C * b + C].indirect(T.ml[:, PARTS[j][0] // 16:PARTS[j][1] // 16]), ["aw0.%d" % b, "aw1.%d" % b, "ml%d" % j]
+    def cut(r, j): return [(0, CUT[r]), (CUT[r], C)][j]
 
-        if r and i == 0:
-            for j, (c0, c1) in enumerate(PARTS):
-                for b in (2, 3): act(T.ag[:, C * (b - 2) + c0:C * (b - 2) + c1], *mapped_h(j, b), ["ag%d.%d" % (j, b)])
-        for j, b in ([(0, 0), (0, 1), (0, 2), (0, 3), (1, 0)], [(1, 1), (1, 2), (1, 3)])[i]:
-            (c0, c1), (a, tags) = PARTS[j], mapped_h(j, b)
-            out = T.xr[:, 4 * c0 + b:4 * c1:4]
-            if r and b >= 2:
-                k = held(r)[b - 2]
-                vtt(out, T.ag[:, C * (b - 2) + c0:C * (b - 2) + c1], T.ps[:, 512 * k + c0:512 * k + c1], A.add, ["ag%d.%d" % (j, b), "bank%d" % k], ["xr%d.%d" % (j, b)])
-            else:
-                vtt(out, a, T.fg[:, C * b + c0:C * b + c1], A.add, tags + ["fg%d" % b], ["xr%d.%d" % (j, b)])
-        (q, qs), (c0, c1) = codes(r + 1), PARTS[i]
-        quant(q[:, c0:c1], qs[:, c0:c1], T.xr[:, 4 * c0:4 * c1], ["xr%d.%d" % (i, b) for b in range(4)], [qtags(r + 1)[i]])
+    def mapped(r, i, stage, e="V"):
+        c0, c1 = cut(r, i)
+        if stage == 0 and r == 0: copy(e, T.mr[:, c0:c1], T.prep[:, :].indirect(T.al[:, c0 // 16:c1 // 16]), ["prep0", "prep1", "al"], ["mr%d" % i])
+        if stage == 0 and r > 0: copy(e, T.mr[:, c0:c1], T.zt[:, :].indirect(T.bl[:, c0 // 16:c1 // 16]), ["zt", "bl"], ["mr%d" % i])
+        if stage == 1: latch(T.msc[:, c0:c1], T.mr[:, c0:c1], c1 - c0, ["mr%d" % i], ["msc%d" % i])
+        if stage == 2: listed(T.ml[:, c0 // 16:c1 // 16], T.msc[:, c0 + 15:c1:16], ["msc%d" % i], ["ml%d" % i])
+
+    def mapped_h(r, j, b): return T.aw[:, C * b:C * b + C].indirect(T.ml[:, cut(r, j)[0] // 16:cut(r, j)[1] // 16]), ["aw0.%d" % b, "aw1.%d" % b, "ml%d" % j]
+
+    def picked(e, r, j, b):
+        c0, c1 = cut(r, j)
+        copy(e, T.ag[:, C * b + c0:C * b + c1], *mapped_h(r, j, b), ["ag%d.%d" % (j, b)])
+
+    def summed(r, j, b):
+        (c0, c1), (a, tags) = cut(r, j), mapped_h(r, j, b)
+        out = T.xr[:, 4 * c0 + b:4 * c1:4]
+        if (j, b) in HELD:
+            vtt(out, T.ag[:, C * b + c0:C * b + c1], T.ps[:, 512 * b + c0:512 * b + c1], A.add, ["ag%d.%d" % (j, b), "bank%d" % b], ["xr%d.%d" % (j, b)])
+        else:
+            vtt(out, a, T.fg[:, C * b + c0:C * b + c1], A.add, tags + ["fg%d" % b], ["xr%d.%d" % (j, b)])
+
+    def made_q(r, i):
+        (q, qs), (c0, c1), x = codes(r), runs(r)[i], T.xr if r else T.x0
+        quant(q[:, c0:c1], qs[:, c0:c1], x[:, 4 * c0:4 * c1], ["xr%d.%d" % (j, b) for b in range(4) for j in range(2) if cut(r - 1, j)[0] < c1 and c0 < cut(r - 1, j)[1]] if r else ["x0"], [qtags(r)[i]])
 
     load("Y", T.sei[:, :], T.se[:, :], "sei", "lse")
     op("G", lambda e: e.iota(T.pi[:, :], [[0, 1]], 0, 1), [], ["pi"])
@@ -329,222 +310,167 @@ def rank_program(g, core, T, topo):
     load("Y", T.ub[:, :], T.u[:, :], "ub", "lu")
     order("Y", ["ub"], [])
     load("Y", T.vb[:, :], T.v[:, :], "vb", "lv")
-    for k in range(0, 128, 16):
-        for h in range(2):
-            g.sync.dma_start(T.sp[k:k + 16, 20 * h:20 * h + 20], T.se[k - k % 32 + 16 * h:k - k % 32 + 16 * h + 16, :]).then_inc(T.sem.lsp, 16)
-    mark([], ["sp"], ("lsp", 256))
 
     iota(T.it[:, 0:C], [[1, C]], 0, 0, ["it0"])
+    ZZ = ["zz%d" % j for j in range(4)]
+    for j in range(3):
+        iota(T.zz[:, 1 << j:16:2 << j], [[0, 8 >> j]], 16 << j, 0, [ZZ[j]])
+    iota(T.zz[:, 0:16:8], [[-1, 2]], 129, 0, [ZZ[3]])
     iota(T.i16[:, :], [[0, 20], [1, 16]], 0, 0, ["i16"])
     iota(T.p4[:, :], [[0, 1]], -3, -4, ["p4"])
     iota(T.it[:, C:512], [[1, 512 - C]], C, 0, ["it1"])
-    ZZ = ["zz%d" % j for j in range(4)]
-    for j in range(4):
-        iota(T.zz[:, (1 << j) % 8:16:min(2 << j, 8)], [[0, max(8 >> j, 2)]], 16 << j, 0, [ZZ[j]])
-    FC = ["fc%d" % j for j in range(12)]
+    FC = ["fc%d" % j for j in range(16)]
     for j, (ap, pat, base) in enumerate((
-            (T.fc[:, 32:72:5], [[0, 8]], 15), (T.fc[:, 33:72:5], [[16, 2], [0, 4]], 31), (T.fc[:, 34:72:5], [[16, 4], [0, 2]], 63),
-            (T.fc[:, 35:72:5], [[16, 8]], 127), (T.fc[:, 36:72:5], [[16, 8]], 127), (T.fc[:, 0:32], [[0, 2], [1, 16]], 240), (T.fc[:, 72:96], [[0, 24]], 0),
-            (T.fc[:, 96:98], [[41, 2]], 15), (T.fc[:, 98:100], [[20, 2]], 16), (T.fc[:, 100:104], [[10, 4]], 17), (T.fc[:, 104:112], [[5, 8]], 18),
-            (T.fc[:, 112:128], [[5, 8], [1, 2]], 19))):
+            (T.fc[:, 132:144:8], [[1, 2]], 0), (T.fc[:, 130:144:4], [[1, 2], [2, 2]], 2), (T.fc[:, 129:144:2], [[1, 2], [2, 2], [4, 2]], 6), (T.fc[:, 128:144:8], [[-1, 2]], 15),
+            (T.fc[:, 48:88:5], [[0, 8]], 15), (T.fc[:, 49:88:5], [[16, 2], [0, 4]], 31), (T.fc[:, 50:88:5], [[16, 4], [0, 2]], 63),
+            (T.fc[:, 51:88:5], [[16, 8]], 127), (T.fc[:, 52:88:5], [[16, 8]], 127), (T.fc[:, 0:48], [[0, 3], [1, 16]], 240), (T.fc[:, 88:96], [[0, 8]], 0),
+            (T.fc[:, 96:98], [[20, 2]], 32), (T.fc[:, 98:102], [[10, 4]], 33), (T.fc[:, 102:110], [[5, 8]], 34),
+            (T.fc[:, 110:126], [[5, 8], [1, 2]], 35), (T.fc[:, 126:128], [[-16, 2]], 31))):
         iota(ap, pat, base, 0, [FC[j]])
     for j, (ap, pat, base) in enumerate((
-            (T.e0[:, 32:72:5], [[16, 2], [0, 4]], -8), (T.e0[:, 33:72:5], [[0, 2], [8, 2], [0, 2]], -4), (T.e0[:, 34:72:5], [[0, 4], [4, 2]], -2),
-            (T.e0[:, 35:72:5], [[0, 8]], -1), (T.e0[:, 36:72:5], [[0, 8]], 2), (T.e0[:, 72:80], [[0, 8]], 0))):
+            (T.e0[:, 48:88:5], [[16, 2], [0, 4]], -8), (T.e0[:, 49:88:5], [[0, 2], [8, 2], [0, 2]], -4), (T.e0[:, 50:88:5], [[0, 4], [4, 2]], -2),
+            (T.e0[:, 51:88:5], [[0, 8]], -1), (T.e0[:, 52:88:5], [[0, 8]], 2), (T.e0[:, 88:96], [[0, 8]], 0))):
         iota(ap, pat, base, 0, [E0[j]])
-    iota(T.ji[:, :], [[16, 32]], 4 * C, 1, ["ji"])
+    iota(T.ji[:, :], [[16, 16]], 4 * C, 1, ["ji"])
+    iota(T.kr[:, 0:16], [[1, 16]], 480, 0, ["kr0"])
+    iota(T.kr[:, 16:256], [[32, 15], [1, 16]], 0, 0, ["kr1"])
 
-    bits = {m: T.xi[:, j:j + 1] for j, m in enumerate((15, 8, 4, 2, 1, 3, 7, 16))}
-    ln = {n: T.ln[:, j:j + 1] for j, n in enumerate(("trash", "right", "left", "b1", "b2", "b3", "lane", "at1", "at2", "root", "top", "mid", "none", "even", "odd"))}
-    for m in bits:
-        vts(bits[m], T.pi[:, :], m, None, A.bitwise_and, None, ["pi"], ["x%d" % m])
-    made = {
-        "trash": (15, 0.0, 2.0 * C, A.is_equal, A.mult), "lane": (15, 1.0, None, A.mult, None), "mid": (15, 16.0, 8.0, A.mult, A.add),
-        "right": (8, 0.25, None, A.mult, None), "left": (8, -0.25, 2.0, A.mult, A.add),
-        "b1": (4, 0.25, None, A.mult, None), "b2": (2, 0.5, None, A.mult, None), "b3": (1, 1.0, None, A.mult, None),
-        "at1": (7, 4.0, 0.5, A.is_equal, A.mult), "at2": (3, 2.0, None, A.is_equal, None),
-        "root": (15, 8.0, float(OWN), A.is_equal, A.mult), "none": (15, 0.0, 256.0, A.is_equal, A.mult),
-        "even": (16, 0.0, 0.5, A.is_equal, A.mult), "odd": (16, 16.0, 0.5, A.is_equal, A.mult)}
+    BITS = (15, 8, 4, 2, 1)
+    for j, m in enumerate(BITS):
+        vts(T.xi[:, j:j + 1], T.pi[:, :], m, None, A.bitwise_and, None, ["pi"], ["xi%d" % m])
+    vcp(T.ln[:, 0:5], T.xi[:, 0:5], ["xi%d" % m for m in BITS], ["x%d" % m for m in BITS])
+    made = (
+        ("mid", "x15", 16.0, 8.0), ("subl", "x15", -1024.0, 15360.0), ("way1", "x8", 2.0, "x1"), ("subl1", "trash", -8.0 / (2 * C), "subl"), ("way2", "x4", 8.0, "way1"), ("way", "x2", 32.0, "way2"))
+    ln = {n: T.ln[:, j:j + 1] for j, n in enumerate(["x%d" % m for m in BITS] + ["trash", "some"] + [m[0] for m in made])}
+    side = {}
 
-    def lanes(names):
-        for n in names.split():
-            m, s1, s2, o0, o1 = made[n]
-            vts(ln[n], bits[m], s1, s2, o0, o1, ["x%d" % m], [n])
+    def lane(e, n, x, scale, bias):
+        if e == "V": vts(ln[n], ln[x], scale, ln.get(bias, bias), A.mult, A.add, [x, str(bias)], [n])
+        else: act(ln[n], ln[x], [x, str(bias)], [n], F.Identity, ln.get(bias, bias), scale)
 
-    lanes("trash lane mid right left")
-    vcp(T.kid[:, 2 * OWN:2 * OWN + 2 * C:2], T.it[:, 0:C], ["it0"], ["kid0"])
-    vcp(T.kid[:, 2 * OWN + 1:2 * OWN + 2 * C:2], T.it[:, 0:C], ["it0"], ["kid1"])
-    lanes("b1 b2 b3 at1 root")
-    act(T.sv[:, :], T.it[:, 0:C], ["it0"], ["sv"], F.Identity, bias=float(OWN))
-    act(T.it[:, OWN:OWN + C], T.it[:, 0:C], ["it0"], ["it2"])
-    act(T.subl[:, :], ln["lane"], ["lane"], ["subl"], F.Identity, bias=15360.0, scale=-1024.0)
-    act(T.d0r[:, :], T.i16[:, 0:256], ["i16"], ["d0r"], F.Sign)
-    act(T.sg[:, :], T.i16[:, 0:16], ["i16", "mid"], ["sg"], F.Sign, bias=ln["mid"], scale=-16.0)
-    act(T.ad[:, :], T.i16[:, 0:16], ["i16", "mid"], ["ad"], F.Abs, bias=ln["mid"], scale=-16.0)
-    act(ln["top"], ln["at1"], ["at1", "root"], ["top"], F.Identity, bias=ln["root"], scale=-1.0)
-    act(T.ea[:, :], T.it[:, 0:520], ["it0", "it1", "it2", "p4"], ["ea"], F.Abs, bias=T.p4[:, 0:1])
+    def const(e, ap, n, c, w):
+        if e == "V": vset(ap, c, w)
+        else: act(ap, T.it[:, 0:n], ["it0"], w, F.Identity, c, 0.0)
 
-    vts(T.ofl[:, 0:1], T.sei[:, 0:1], ln["trash"], None, A.add, None, ["sei", "trash"], ["ofl0"])
-    vcp(T.ofl[:, 1:20], T.sei[:, 1:20], ["sei"], ["ofl"])
-    vts(T.mk[:, 16:336], T.i16[:, :], ln["lane"], None, A.is_equal, None, ["i16", "lane"], ["mk"])
-    vcp(T.kid[:, 2 * OWN:2 * OWN + 2 * C + 16].indirect(T.ofl[:, 0:20]), T.sv[:, :], ["ofl", "ofl0", "sv"], ["kid0", "kid1"])
-    lanes("at2 none")
-    vset(T.mk[:, 0:16], 1.0, ["mk1"])
-    vset(T.d0t[:, :], 1.0, ["d0t", "d0t1"])
-    act(T.d0l[:, :], T.mk[:, 16:336], ["mk"], ["d0l"], F.Identity, bias=1024.0, scale=-66560.0)
-    act(T.eb[:, 0:520], T.ea[:, :], ["ea"], ["eb0"], F.Relu, bias=0.5, scale=-1.0)
-    KID, kid = ["kid0", "kid1", "kid2"], T.kid[:, 0:2 * OWN + 2 * C]
+    for e in "SV":
+        side.update({m[0] + e: (lane, e) + m for m in made})
+        for n, ap, k, c, w in (("mk1", T.mk[:, 0:16], 16, 1.0, ["mk1"]), ("up0", T.up[:, 14:15], 1, float(OWN), ["up0"]), ("d0t", T.d0t[:, :], 96, 1.0, ["d0t", "d0t1"]),
+                               ("d0", T.d0t[:, 48:88:5], 8, 0.0, ["d0t"]), ("d1", T.d0t[:, 0:32:16], 2, 0.0, ["d0t1"]), ("zt0", T.zt[:, 0:513:512], 2, 0.0, ["zt"]), ("z0", T.e0[:, 0:1], 1, 0.0, [E0[6]])):
+            side[n + e] = (const, e, ap, k, c, w)
+    side.update({
+        "trash": (vts, ln["trash"], T.xi[:, 0:1], 0.0, 2.0 * C, A.is_equal, A.mult, ["xi15"], ["trash"]), "some": (vts, ln["some"], T.xi[:, 0:1], 1.0, None, A.min, None, ["xi15"], ["some"]),
+        "sv": (act, T.sv[:, :], T.it[:, 0:C], ["it0"], ["sv"], F.Identity, float(OWN)), "it2": (act, T.it[:, OWN:OWN + C], T.it[:, 0:C], ["it0"], ["it2"]),
+        "sg": (act, T.sg[:, :], T.it[:, 0:16], ["it0", "mid"], ["sg"], F.Sign, ln["mid"], -16.0), "ad": (act, T.ad[:, :], T.it[:, 0:16], ["it0", "mid"], ["ad"], F.Abs, ln["mid"], -16.0),
+        "ull": (vcp, T.ull[:, :], T.it[:, 0:128:16], ["it0"], ["ull"]), "d0r": (act, T.d0r[:, :], T.i16[:, 0:256], ["i16"], ["d0r"], F.Sign),
+        "ea": (act, T.ea[:, :], T.it[:, 0:520], ["it0", "it1", "it2", "p4"], ["ea"], F.Abs, T.p4[:, 0:1]), "eb": (act, T.eb[:, :], T.ea[:, :], ["ea"], ["eb"], F.Relu, 0.5, -1.0),
+        "kid0": (vcp, T.kid[:, 2 * OWN:2 * OWN + 2 * C:2], T.it[:, 0:C], ["it0"], ["kid0"]), "kid1": (vcp, T.kid[:, 2 * OWN + 1:2 * OWN + 2 * C:2], T.it[:, 0:C], ["it0"], ["kid1"]),
+        "ofl0": (vts, T.ofl[:, 0:1], T.sei[:, 0:1], ln["trash"], None, A.add, None, ["sei", "trash"], ["ofl0"]), "ofl": (vcp, T.ofl[:, 1:20], T.sei[:, 1:20], ["sei"], ["ofl"]),
+        "kid": (vcp, T.kid[:, 2 * OWN:2 * OWN + 2 * C + 16].indirect(T.ofl[:, 0:20]), T.sv[:, :], ["ofl", "ofl0", "sv"], ["kid0", "kid1"])})
+    KID, kid, WO3 = ["kid0", "kid1", "kid2"], T.kid[:, 0:2 * OWN + 2 * C], ["wo3.%d" % c for c in range(4)]
 
     def pick_u():
         vcp(T.ur[:, 0:128].bitcast(dt.uint32), T.uq[:, 0:128].bitcast(dt.uint32).indirect(T.ull[:, 0:8]), ["uq", "ull"], ["ur"])
         act(T.urs[:, 0:128], T.us[:, 0:128].indirect(T.ull[:, 0:8]), ["uq", "ull"], ["urs"])
 
-    def first():
-        quant(T.q0[:, 0:C], T.qs0[:, 0:C], T.x0[:, 0:1280], ["x0"], ["q0.0"])
-        layer(0, 0)
-        scores(0, 0)
+    def tiles(b): quant(T.eq[:, 128 * b:128 * b + 128], T.es[:, 128 * b:128 * b + 128], T.eb[:, 3 - b:515 - b], ["eb"], ["eq%d" % b])
 
-    def tiles(j):
-        at = 520 * (j // 4) + 3 - j % 4
-        quant(T.eq[:, 128 * j:128 * j + 128], T.es[:, 128 * j:128 * j + 128], T.eb[:, at:at + 512], ["eb%d" % (j // 4)], ["eq%d" % j])
-        if j != 3: return
-        own(0, four(0, 1))
-        for b in range(4): fw("S", b, four(0, 1)[b])
-        for b in range(4): fg("S", b)
+    def parents():
+        for b in range(4): vts(T.parl[:, 20 * b:20 * b + 20], T.ai[:, :], 4.0, float(b), A.mult, A.add, ["ai"], ["par%d" % b])
 
-    def halves():
-        lanes("even odd")
-        for h, n in ((1, "even"), (2, "odd")):
-            act(T.eb[:, 520 * h:520 * h + 520], T.ea[:, :], ["ea", n], ["eb%d" % h], F.Relu, bias=ln[n], scale=-1.0)
+    def pair(at, y, r, n):
+        vts(T.wv[:, at:at + 2 * n:2], y, 2.0, None, A.mult, None, r, ["wv%da" % at])
+        vts(T.wv[:, at + 1:at + 2 * n:2], y, 2.0, 1.0, A.mult, A.add, r, ["wv%db" % at])
 
-    side = {
-        "ull": (vcp, T.ull[:, :], T.it[:, 0:128:16], ["it0"], ["ull"]), "qu": (quant, T.uq[:, :], T.us[:, :], T.ub[:, :], ["ub"], ["uq"]),
-        "pu": (pick_u,), "first": (first,), "pack": (pack, 0, 0), "halves": (halves,),
-        "sq": (vts, T.sq[:, :], T.sp[:, :], 1, None, A.arith_shift_right, None, ["sp"], ["sq"]), "pair": (vcp, T.pair[:, :], T.sq[:, :], ["sq"], ["pair"]),
-        "ai": (vts, T.ai[:, :], T.sei[:, :], 1, None, A.arith_shift_right, None, ["sei"], ["ai"]), "parl": (vcp, T.parl[:, :], T.ai[:, :], ["ai"], ["parl"]),
-        "tp1": (vts, T.tp[:, 1:2], T.wo[:, 2:3], ln["at1"], ln["top"], A.mult, A.add, ["wo1", "at1", "top"], ["tp1"]),
-        "tp2": (vts, T.tp[:, 2:3], T.yt[:, 2:3], ln["at2"], T.tp[:, 1:2], A.mult, A.add, ["yt2", "at2", "tp1"], ["tp2"]),
-        "cl0": (vts, T.cl[:, 0:1], T.yt[:, 3:4], ln["b3"], T.tp[:, 2:3], A.mult, A.add, ["yt3", "b3", "tp2"], ["cl0"]),
-        "cl1": (vts, T.cl[:, 1:8], T.wv[:, 2:16:2], 0.5, None, A.mult, None, ["wv1a", "wv2a", "wv4a"], ["cl1"]),
+    side.update({
+        "qu": (quant, T.uq[:, :], T.us[:, :], T.ub[:, :], ["ub"], ["uq"]),
+        "pu": (pick_u,),
+        "ai": (vts, T.ai[:, :], T.sei[:, :], 1, None, A.arith_shift_right, None, ["sei"], ["ai"]), "par": (parents,),
+        "up1": (vts, T.up[:, 0:6], T.wo[:, 0:12:2], ln["x1"], 0.5, A.subtract, A.mult, ["wo1", "wo2.0", "wo2.1", "x1"], ["up1"]),
+        "up3": (vts, T.up[:, 6:14], T.wo[:, 68:76], ln["x1"], 0.5, A.subtract, A.mult, WO3 + ["x1"], ["up3"]),
+        "one": (vts, T.one[:, :], T.it[:, 0:15], ln["subl"], T.fs[:, 143:144], A.add, A.is_equal, ["it0", "subl", "fs"], ["one"]),
+        "upm": (vtt, T.upm[:, :], T.up[:, :], T.one[:, :], A.mult, ["up0", "up1", "up3", "one"], ["upm"]), "top": (vred, T.yt[:, 1:2], T.upm[:, :], ["upm"], ["top"]),
+        "cl0": (vcp, T.cl[:, 0:1], T.yt[:, 1:2], ["top"], ["cl0"]), "wu": (pair, 16, T.yt[:, 1:2], ["top"], 1),
+        "clab": (vts, T.cl[:, 32:34], T.gs[:, 239:256:16], ln["some"], None, A.mult, None, ["gs4", "some"], ["clab"]),
+        "m4": (vts, T.m4[:, :], T.it[:, 0:128], ln["way"], None, A.is_equal, None, ["it0", "way"], ["m4"]),
+        "mk": (vts, T.mk[:, 16:336], T.i16[:, :], ln["x15"], None, A.is_equal, None, ["i16", "x15"], ["mk"]),
+        "d0l": (act, T.d0l[:, :], T.mk[:, 16:336], ["mk"], ["d0l"], F.Identity, 1024.0, -66560.0),
         "an": (vtt, T.an[:, :], T.ad[:, :], T.zz[:, :], A.is_lt, ["ad"] + ZZ, ["an"]), "w1": (vtt, T.w1[:, :], T.sg[:, :], T.zz[:, :], A.mult, ["sg"] + ZZ, ["w1"]),
-        "zl": (vtt, T.zl[:, :], T.zz[:, :], T.mk[:, 16:32], A.mult, ZZ + ["mk"], ["zl"]), "zr": (vred, T.zr[:, :], T.zl[:, :], ["zl"], ["zr"]),
-        "tm": (vts, T.tm[:, :], T.zz[:, :], T.zr[:, 0:1], -1.0, A.is_le, A.mult, ZZ + ["zr"], ["tm"]),
         "down": (vtt, T.e0[:, 0:16], T.w1[:, :], T.an[:, :], A.mult, ["w1", "an"], [E0[6]]),
+        "cl1": (vts, T.cl[:, 1:8], T.wv[:, 2:16:2], 0.5, None, A.mult, None, ["wv2a", "wv4a", "wv8a"], ["cl1"]),
+        "zl": (vtt, T.zl[:, :], T.zz[:, :], T.mk[:, 16:32], A.mult, ZZ + ["mk"], ["zl"]), "zr": (vred, T.zr[:, :], T.zl[:, :], ["zl"], ["zr"]),
+        "tm": (vts, T.tm[:, :], T.zz[:, :], T.zr[:, 0:1], -1.0, A.is_lt, A.mult, ZZ + ["zr"], ["tm"]),
         "back": (vtt, T.e0[:, 16:32], T.e0[:, 0:16], T.tm[:, :], A.mult, [E0[6], "tm"], [E0[7]]),
-        "z0": (vset, T.e0[:, 0:1], 0.0, [E0[6]]), "z16": (vcp, T.e0[:, 16:17], ln["none"], ["none"], [E0[7]]),
-        "j4": (vts, T.j4[:, :], T.ji[:, :], 0.25, None, A.mult, None, ["ji"], ["j4"]),
-        "d0": (vset, T.d0t[:, 32:77:5], 0.0, ["d0t"]), "d1": (vset, T.d0t[:, 0:32:16], 0.0, ["d0t1"]),
-        "fs": (latch, T.fs[:, :], T.fc[:, :], 128, FC, ["fs"]), "tl": (listed, T.tl[:, :], T.fs[:, 15:128:16], ["fs"], ["tl"])}
-    side.update({"t%d" % j: (tiles, j) for j in range(12)})
-    for names in BESIDE.split("|"):
-        later(lambda names=names: [side[n][0](*side[n][1:]) for n in names.split()])
+        "own": (vts, T.e0[:, 32:48], T.zl[:, :], -2.0, -256.0, A.mult, A.max, ["zl"], [E0[8]]),
+        "s1": (vts, T.s1[:, :], T.sei[:, :], 1, None, A.bitwise_and, None, ["sei"], ["s1"]),
+        "st": (vts, T.st[:, 1:20], T.s1[:, 1:20], 16.0, ln["subl"], A.mult, A.subtract, ["s1", "subl"], ["st"]),
+        "st0": (vts, T.st[:, 0:1], T.s1[:, 0:1], 16.0, ln["subl1"], A.mult, A.subtract, ["s1", "subl1"], ["st0"]),
+        "ci": (vcp, T.ci[:, :], T.cl[:, 0:16], ["cl0", "cl1", "cl8"], ["ci"]), "cj": (vts, T.cj[:, :], T.ci[:, :], OWN - 1, None, A.bitwise_and, None, ["ci"], ["cj"]),
+        "ls": (vcp, T.ls[:, :], T.cj[:, :], ["cj"], ["ls"]),
+        "fs": (latch, T.fs[:, :], T.fc[:, :], 144, FC, ["fs"]), "tl": (listed, T.tl[:, :], T.fs[:, 15:128:16], ["fs"], ["tl"])})
+    side.update({"t%d" % b: (tiles, b) for b in range(4)})
 
-    vts(T.tp[:, 0:1], T.kid[:, 2 * OWN + 1:2 * OWN + 2], ln["right"], ln["b1"], A.mult, A.add, ["kid1", "right", "b1"], ["tp0"])
-    vts(T.kid[:, 0:2 * C], T.kid[:, 2 * OWN:2 * OWN + 2 * C], OWN - 1, None, A.bitwise_and, None, ["kid0", "kid1"], ["kid2"])
-    vts(T.wo[:, 2:3], T.kid[:, 2 * OWN:2 * OWN + 1], ln["left"], T.tp[:, 0:1], A.mult, A.add, ["kid0", "left", "tp0"], ["wo1"])
-    fill()
-    for j in range(1, 4):
-        vtt(T.g16[:, 16 * j - 16:16 * j], kid.indirect(T.wo[:, 2 * j:2 * j + 1]), T.mk[:, 16:32], A.mult, KID + ["wo%d" % j, "mk"], ["g16%d" % j])
-        fill()
-        vred(T.yt[:, j + 1:j + 2], T.g16[:, 16 * j - 16:16 * j], ["g16%d" % j], ["yt%d" % (j + 1)])
-        fill()
-        y = T.yt[:, j + 1:j + 2]
-        if j < 3:
-            vts(T.wo[:, 2 * j + 2:2 * j + 3], y, 2.0, ln["b%d" % (j + 1)], A.mult, A.add, ["yt%d" % (j + 1), "b%d" % (j + 1)], ["wo%d" % (j + 1)])
-        else:
-            vts(T.wv[:, 2:3], y, 2.0, None, A.mult, None, ["yt4"], ["wv1a"])
-            vts(T.wv[:, 3:4], y, 2.0, 1.0, A.mult, A.add, ["yt4"], ["wv1b"])
-        fill()
+    def tree():
+        vts(T.wo[:, 0:4:2], T.kid[:, 2 * OWN:2 * OWN + 2], 2.0, ln["x1"], A.mult, A.add, ["kid0", "kid1", "x1"], ["wo1"])
+        yield vts(T.kid[:, 0:2 * C], T.kid[:, 2 * OWN:2 * OWN + 2 * C], OWN - 1, None, A.bitwise_and, None, ["kid0", "kid1"], ["kid2"])
+        for c in range(2): vts(T.wo[:, 4 + 2 * c:68:4], kid.indirect(T.wo[:, 2 * c:2 * c + 1]), 2.0, ln["x1"], A.mult, A.add, KID + ["wo1", "x1"], ["wo2.%d" % c])
+        yield
+        for c in range(4): vts(T.wo[:, 68 + c:132:4], kid.indirect(T.wo[:, 4 + 2 * c:5 + 2 * c]), 2.0, ln["x1"], A.mult, A.add, KID + ["wo2.%d" % (c % 2), "x1"], ["wo3.%d" % c])
+        yield
+        yield vtt(T.g4[:, :], kid.indirect(T.wo[:, 68:76]), T.m4[:, :], A.mult, KID + WO3 + ["m4"], ["g4"])
+        yield vred(T.yt[:, 0:1], T.g4[:, :], ["g4"], ["yt"])
+        yield pair(2, T.yt[:, 0:1], ["yt"], 1)
+        for n in (1, 2, 4, 8): yield from below(n)
 
     def below(n):
-        k, h = 32 * n, 32 * (n - 1)
-        yield vtt(T.gg[:, h:h + k], kid.indirect(T.wv[:, 2 * n:4 * n]), T.mk[:, 16:16 + k], A.mult, KID + ["wv%da" % n, "wv%db" % n, "mk"], ["gg%d" % n])
+        a, b = {1: (2, 4), 2: (4, 8), 4: (8, 18), 8: (18, 34)}[n]
+        h, k = 16 * a - 32, 16 * (b - a)
+        if n == 8 and LEAVES == "S":
+            yield act(T.gg[:, h:h + k], kid.indirect(T.wv[:, a:b]), KID + ["wv18a", "wv18b"], ["gg8"])
+            yield latch(T.gs[:, h:h + k], T.gg[:, h:h + k], k, ["gg8"], ["gs8"])
+            yield listed(T.cl[:, 16:32], T.gs[:, h + 15:h + k:16], ["gs8"], ["cl16"])
+        yield vtt(T.gg[:, h:h + k], kid.indirect(T.wv[:, a:b]), T.mk[:, 16:16 + k], A.mult, KID + ["wv%d%s" % (j, c) for j in (a, b - 2 * (n == 4)) for c in "ab"] + ["mk"], ["gg%d" % n])
         yield vscan(T.gs[:, h:h + k], T.d0r[:, 0:k], T.gg[:, h:h + k], 0.0, A.mult, A.add, ["gg%d" % n, "d0r"], ["gs%d" % n])
-        y = T.gs[:, h + 15:h + k:16]
+        y = T.gs[:, h + 15:h + 32 * n:16]
+        if n < 8: pair(b, y, ["gs%d" % n], 2 * n)
         if n >= 4: vcp(T.cl[:, 2 * n:4 * n], y, ["gs%d" % n], ["cl%d" % (2 * n)])
-        if n < 8:
-            vts(T.wv[:, 4 * n:8 * n:2], y, 2.0, None, A.mult, None, ["gs%d" % n], ["wv%da" % (2 * n)])
-            vts(T.wv[:, 4 * n + 1:8 * n:2], y, 2.0, 1.0, A.mult, A.add, ["gs%d" % n], ["wv%db" % (2 * n)])
         yield
 
-    for n in (1, 2, 4):
-        for _c in below(n): fill()
+    side.update({
+        "*": (next, tree()), "lab0": (labels, 0), "lab1": (labels, 1), "lab2": (labels, 2),
+        "yf": (vts, T.yf[:, :], T.cl[:, 0:16], 4.0, None, A.mult, None, ["cl0", "cl1", "cl8"], ["yf"]),
+        "o16": (vtt, T.o16[:, :], T.yf[:, :], T.ji[:, :], A.max, ["yf", "ji"], ["o16"]), "ol": (vcp, T.ol[:, :], T.o16[:, :], ["o16"], ["ol"]),
+        "at": (vcp, T.at[:, :].indirect(T.ol[:, 0:16]), T.kr[:, :], ["ol", "kr0", "kr1"], ["at"]),
+        "als": (latch, T.als[:, :], T.ar[:, :], C, ["ar0", "ar1"], ["als"]),
+        "af": (vtt, T.af[:, :], T.als[:, 15:C:16], T.st[:, :], A.add, ["als", "st", "st0"], ["af"]), "al": (vcp, T.al[:, :], T.af[:, :], ["af"], ["al"]),
+        "vq": (quant, T.vq[:, :], T.vs[:, :], T.vb[:, :], ["vb"], ["vq"])})
 
-    chain, leaves = positions(0), below(8)
-    next(chain)
-    next(leaves)
-    next(chain)
-    vcp(T.yf[:, :], T.cl[:, 0:16], ["cl0", "cl1", "cl8"], ["yf"])
-    next(leaves)
-    next(chain)
-    next(leaves)
-    labels(0)
-    vtt(T.o32[:, 16:32], T.gs[:, 224 + 15:480:16], T.j4[:, 16:32], A.max, ["gs8", "j4"], ["o32b"])
-    next(chain)
-    vtt(T.o32[:, 0:16], T.yf[:, :], T.j4[:, 0:16], A.max, ["yf", "j4"], ["o32a"])
-    next(chain)
-    labels(1)
-    labels(2)
-    prep(0, "SS")
-    vts(T.ol[:, :], T.o32[:, :], 4.0, None, A.mult, None, ["o32a", "o32b"], ["ol"])
-    vcp(T.ci[:, :], T.cl[:, 0:16], ["cl0", "cl1", "cl8"], ["ci"])
-    vcp(T.at[:, :].indirect(T.ol[:, 0:32]), T.it[:, 0:512], ["ol", "it0", "it1"], ["at"])
-    vts(T.cj[:, :], T.ci[:, :], OWN - 1, None, A.bitwise_and, None, ["ci"], ["cj"])
-    fill()
-    latch(T.als[:, :], T.at[:, 4 * OWN:4 * (OWN + C):4], C, ["at"], ["als"])
-    vcp(T.ls[:, :], T.cj[:, :], ["cj"], ["ls"])
-    fill()
-    listed(T.al[:, :], T.als[:, 15:C:16], ["als"], ["al"])
-    fill()
-    spread(0)
-    brep("SS")
-    arrived(0, 0, four(0, 0))
-    zt(0)
-    placed()
-    mapped(0)
+    def beside(e, h): copy(e, T.ar[:, 160 * h:160 * h + 160], T.at[:, 4 * OWN:4 * (OWN + C)].indirect(T.parl[:, 10 * h:10 * h + 10]), ["at", "par0"], ["ar%d" % h])
 
-    for r in (1, 2):
-        far = relay[r] is not None
-        if r == 1: spread(r)
-        state(r - 1, 0)
-        if r == 2: spread(r)
-        layer(r, 0, 3)
-        scores(r, 0)
-        state(r - 1, 1)
-        scores(r, 1)
-        scaled("V", r, 0, 3)
-        layer(r, 1)
-        if r == 1: quant(T.vq[:, :], T.vs[:, :], T.vb[:, :], ["vb"], ["vq"])
-        pack(r, 0)
-        for j in range(5): pick("S", r, j)
-        gaps = [(pick, "V", r, 0), (pack, r, 1), (pick, "V", r, 1), (pick, "V", r, 2), (pick, "V", r, 3)]
-        for _c, gap in zip(positions(r), gaps): gap[0](*gap[1:])
-        above(r, 0)
-        post(r, 1)
-        prep(r)
-        pick("V", r, 4)
-        brep()
-        placed()
-        if not far: arrived(r, 0, four(r, 1))
-        above(r, 1)
-        for b in range(2): kept(r, b)
-        zt(r)
-        mapped(r)
-        if far:
-            arrived(r, 0, four(r, 1))
-            arrived(r, 1, four(r, 2), ((2, "S"), (0, "V"), (3, "S"), (1, "V")))
-        else: arrived(r, 1, four(r, 2))
-    store("Y", T.im[:, :], T.mr[0:128:16, :], ["mr0", "mr1"])
-
-    for i, (c0, c1) in enumerate(PARTS):
-        state(2, i)
-        t = "q1.%d" % i
-        mm(5 * i, T.vq[:, 0:128], T.vs[:, 0:128], T.q1[:, c0:c1], T.qs1[:, c0:c1], [t, "vq"], c1 - c0)
-        act(T.ysb[:, c0:c1], bank(5 * i, c1 - c0), ["bank%d" % (5 * i)], ["ysb%d" % i])
+    def out(i, e):
+        (c0, c1), t = runs(3)[i], "q1.%d" % i
+        mm(4 + i, T.vq[:, 0:128], T.vs[:, 0:128], T.q1[:, c0:c1], T.qs1[:, c0:c1], [t, "vq"], c1 - c0)
+        copy(e, T.ysb[:, c0:c1], bank(4 + i, c1 - c0), ["bank%d" % (4 + i)], ["ysb%d" % i])
         store("Y", T.oc[:, 4 * c0:4 * c1], T.q1[:, c0:c1].bitcast(dt.uint8), [t])
         store("S", T.y[:, c0:c1], T.ysb[:, c0:c1], ["ysb%d" % i])
         for k in range(4):
             store("Y", T.osc[4 * k:4 * k + 4, c0:c1], T.qs1[32 * k:32 * k + 4, c0:c1], [t])
+
+    for r in range(4):
+        step = {"pos": (next, positions(r)), "pq": (requant,), "above": (above, r), "zt": (zt, r), "bsc": (placed,), "bl": (listed, T.bl[:, :], T.bsc[:, 15:C:16], ["bsc"], ["bl"]),
+                "im": (store, "Y", T.im[:, :], T.mr[0:128:16, :], ["mr0", "mr1"])}
+        for i in range(2):
+            step.update({"q%d" % i: (made_q, r, i), "layer%d" % i: (layer, r, i), "sc%d" % i: (scores, r, i), "sg%d" % i: (signs, r, i), "pack%d" % i: (pack, r, i), "post%d" % i: (post, r, i),
+                         "un%d" % i: (arrived, r, i), "msc%d" % i: (mapped, r, i, 1), "ml%d" % i: (mapped, r, i, 2)})
+            step.update({"x%d%d" % (i, b): (summed, r - 1, i, b) for b in range(4)})
+            for e in "SV":
+                step.update({"lr%d%s" % (i, e): (spread, e, r, i), "next%d%s" % (i, e): (spread, e, r + 1, i), "prep%d%s" % (i, e): (prep, e, r, i), "brep%d%s" % (i, e): (brep, e, i),
+                             "ar%d%s" % (i, e): (beside, e, i), "mr%d%s" % (i, e): (mapped, r, i, 0, e), "met%d%s" % (i, e): (met, e, i), "k%d%s" % (i, e): (kept, e, r, i),
+                             "out%d%s" % (i, e): (out, i, e)})
+                for b in range(4):
+                    step.update({"h%d%d%s" % (i, b, e): (scaled, e, r, i, b), "xp%d%d%s" % (b, i, e): (laid, e, r, b, i), "aw%d%d%s" % (i, b, e): (taken, e, r, i, b), "ag%d%d%s" % (i, b, e): (picked, e, r - 1, i, b)})
+        for n in ROUNDS[r if r in (0, 3) else 1 if relay[r] is None else 2].split():
+            f = step.get(n) or side[n]
+            f[0](*f[1:])
     for k in ("V", "S", "T", "G"):
         wait("G", ("c" + k, cnt[k]))
     g.wait_ge(T.sem.stored, stores[0])

@@ -7,10 +7,17 @@ PARTS = [(0, 192), (192, 320)]
 HANDED, DIRECT = [("q", 0, 144), ("s", 192, 320)], [("q", 144, 192), ("s", 0, 192), ("q", 192, 320)]
 OWN = 512
 ROUNDS = [
-    'sublS sv way1S way2S midS it2 trash some kid0 kid1 wayS subl1S mk1S sg d0tS ofl ofl0 ull kid w1 m4 mk * ad up0S d0r an q0 * * qu layer0 * ai down * up1 up3 * d0l ea h00S h01S z0S pu zt0S h03S h02S sc0 d1S sg0 * fs * zl * par zr * one own tm * tl upm back * top pack0 wu cl0 xp01S eb xp11S sg1 d0S * t0 * t1 cl1 * s1 * clab t2 st pos yf * pos * lab0 ci pos o16 t3 xp20S xp00S xp10S xp30S xp31S xp21S pos ol st0 pos lab1 lab2 at pq lr1S lr0S ar1V cj un0 above zt ar0S aw00S aw02S als af aw01S aw03S met0S k0S met1V al ls mr0V mr1S k1S msc0 msc1 ml0 ml1',
-    'ag02S x00 x10 x01 ag03S ag13S ag12S lr0S lr1S x03 x02 x11 x13 x12 q0 q1 sc0 sc1 xp20S sg0 layer0 xp10V xp01V xp00V sg1 layer1 h00S pos h11V h01S h03S h02S h13S h10S h12S pos pack0 pos xp11V xp30S xp21S xp31S pos pos pack1 post1 prep0S prep1V pq brep0S brep1V un0 above bsc aw02S aw01S aw03S aw00S k0S zt bl un1 aw12S aw10S aw11S vq mr0V mr1S k1S aw13V msc0 msc1 ml0 ml1',
-    'x00 x01 lr1S ag02S ag03S x02 ag12S ag13S lr0S x03 x11 q0 layer0 sc0 x10 x12 x13 h01S h00S sg0 q1 sc1 sg1 h02V layer1 h03V xp00S xp01S xp11S h13S h12S h11S pack0 h10S pos pos xp21V xp31S xp20S pos xp30V pos pack1 pos post1 prep0S xp10S prep1V brep1V pq brep0S above un0 bsc zt k0S k1S bl mr0V aw02S aw00S aw03S aw01S un1 mr1V msc0 msc1 aw10S aw12S ml0 aw13S ml1 aw11V',
-    'x00 ag02S x01 ag03S x02 x03 x11 ag12S ag13S q0 x13 x10 x12 im out0S q1 out1V']
+    'kr trash last subl0S zt0S sv d0tV nextS up0V subl1S it2 sublS midS d1S way1S d0S way2S kid1 kid0 ofl0 ofl ull d0a wayS d0b kid d0l m4 * mk d16S mk1S d32S ea * q0 * q1 d64S eb d128S ad sg d0r * layer0 qu s1 up1 * some w1 zl up3 * fs * pu h00S h01S h02S h03S sc0 one * zr ai upm * an st tl own top * down par * wu pack0 * pack1 post0 * tm t3 * cl1 t0 cl0 * xp00S sg0 z0S xp10S sg1 * xp20S xp30S xp21S xp11S xp31S back clab small pos yf t1 pos * pos * o16 st0 t2 pos ol lab0 pq0 pos lab1 at lr1V un0 step0S xp01S d256S pq1 above lr0S ar0S ar1S aw01S k0S aw02S zt met0S als af met1V al s0b ci s0a step1V mr0V cj aw00S mr1S k1S aw03S msc0 msc1 d0s ml0 ls ml1',
+    'lc s16V ag02S ag03S x01 x00 x10 x03 x02 ag12S s32S ag13S lr1S lr0S x11 x12 x13 q0 sc0 s64V q1 sc1 layer0 xp10V lt xp30V xp20V xp00S sg0 sg1 s128S tnS rows pos xp01V pos pq0 pos g03V pos g13V h00S h02S h01S xp11S xp21S pos prep0S pack0 pack1 prep1V xp31S post0 lab2 brep0S brep1V pq1 above bsc un0 k0S step0S step1S k1S aw02S aw00S aw03S aw01S zt out2 bl mr0V mr1V msc0 msc1 ml0 vq ml1',
+    'x00 x01 ag02S ag03S x02 ag12S ag13S x03 x11 q0 layer0 sc0 x12 x10 x13 h01S h02S sg0 h00V q1 sc1 h03V sg1 layer1 xp20S tnS xp30V pack0 post0 pos xp10V pos h10V pos h13V h11S h12S xp00S xp11S xp01S pos pq0 pos pack1 post1 prep0S prep1V xp21S xp31V brep0S brep1V pq1 above bsc un0 zt k0S k1S bl mr0V aw00V mr1S aw02S un1 msc0 msc1 aw10V ml0 aw03S aw12S aw01S ml1 aw13V aw11S',
+    'ag02S x00 x10 x01 x02 ag03S ag12S ag13S mfS x03 x11 x12 x13 q0 im oc0 q1 oc1 osc out0S out1V']
+BIG = 2.0 ** 26
+UN1 = [1, 4, 0, 6]
+LEARN = True
+SPLIT = False
+ROWS = [2]
+MASKED = [True, False, False, True]
+WHOLE = True
 LEAVES = "S"
 CUT = [160, 192, 192]
 HELD = [(0, 2), (0, 3), (1, 2), (1, 3)]
@@ -26,20 +33,22 @@ for _n, _w, _d in (
         ("xp", 1280, "bfloat16"), ("pq", 320, "float8_e4m3fn_x4"), ("pqs", 320, "uint8"),
         ("pi", 1, "int32"), ("p4", 1, "float32"), ("xi", 8, "int32"), ("ln", 24, "float32"),
         ("i16", 320, "bfloat16"), ("it", OWN + C, "float32"), ("sv", 320, "float32"), ("kr", 256, "float32"),
-        ("mk", 336, "bfloat16"), ("d0r", 256, "bfloat16"), ("d0l", 320, "float32"), ("d0t", 96, "float32"),
+        ("mk", 336, "bfloat16"), ("d0r", 256, "bfloat16"), ("d0l", 320, "bfloat16"), ("d0t", 96, "bfloat16"), ("d0a", 64, "bfloat16"), ("d0s", 256, "bfloat16"),
         ("zz", 16, "float32"), ("ad", 16, "float32"), ("sg", 16, "float32"), ("an", 16, "float32"),
         ("w1", 16, "float32"), ("zl", 16, "float32"), ("zr", 1, "float32"), ("tm", 16, "float32"),
         ("ji", 16, "float32"), ("fc", 144, "float32"), ("fs", 144, "float32"), ("tl", 8, "uint16"), ("ull", 8, "uint16"), ("m4", 128, "bfloat16"), ("one", 15, "float32"),
         ("ai", 20, "int32"), ("ofl", 20, "uint16"), ("parl", 80, "uint16"), ("kid", 2 * OWN + 2 * C + 16, "int32"), ("wo", 132, "uint16"), ("wv", 34, "uint16"),
-        ("g4", 128, "float32"), ("yt", 2, "float32"), ("up", 15, "float32"), ("upm", 15, "float32"), ("gg", 512, "float32"), ("gs", 512, "float32"),
-        ("cl", 34, "uint16"), ("ci", 16, "int32"), ("cj", 16, "int32"), ("ls", 16, "uint16"), ("yf", 16, "float32"), ("o16", 16, "float32"), ("ol", 16, "uint16"),
-        ("at", 4 * (OWN + C), "float32"), ("ar", 320, "float32"), ("als", 320, "float32"), ("s1", 20, "int32"), ("st", 20, "float32"), ("af", 20, "float32"), ("al", 20, "uint16"),
-        ("tb", OWN + C, "bfloat16"), ("sm", 496, "bfloat16"), ("e0", 96, "float32"), ("e1", 96, "float32"),
-        ("pp", 96, "float32"), ("prep", 512, "float32"), ("brep", 320, "float32"), ("bsc", 320, "float32"), ("bl", 20, "uint16"),
-        ("zt", 520, "float32"), ("msc", 320, "float32"), ("ml", 20, "uint16"), ("mr", 320, "float32"), ("ysb", 320, "float32"),
+        ("g4", 128, "float16"), ("g5", 128, "float16"), ("yt", 2, "float32"), ("up", 15, "float32"), ("upm", 15, "float32"), ("gg", 256, "float16"), ("gs", 256, "float16"), ("lg", 256, "float32"), ("lf", 256, "float32"),
+        ("cl", 34, "uint16"), ("ci", 34, "int32"), ("cj", 34, "int32"), ("lc", 32, "bfloat16"), ("lt", 32, "bfloat16"), ("ls", 16, "uint16"), ("yf", 16, "float32"), ("o16", 16, "float32"), ("ol", 16, "uint16"),
+        ("at", 4 * (OWN + C), "float32"), ("ar", 320, "bfloat16"), ("als", 320, "float16"), ("s1", 20, "int32"), ("st", 20, "float32"), ("af", 20, "float32"), ("al", 20, "uint16"),
+        ("tb", OWN + C, "bfloat16"), ("sm", 496, "bfloat16"), ("e0", 96, "bfloat16"), ("e1", 96, "bfloat16"),
+        ("pp", 96, "bfloat16"), ("prep", 512, "float32"), ("brep", 320, "bfloat16"), ("bsc", 320, "float16"), ("bl", 20, "uint16"),
+        ("zt", 520, "float32"), ("msc", 320, "float16"), ("ml", 20, "uint16"), ("mr", 320, "bfloat16"), ("mf", 320, "float32"), ("ysb", 320, "float32"),
         ("fg", 640, "bfloat16"), ("aw", 1280, "bfloat16"), ("ag", 1280, "bfloat16"),
-        ("pl", 96, "uint16"), ("pa", 96, "uint16"), ("ll", 96, "uint16"), ("lr", 1536, "float32")):
+        ("pl", 96, "uint16"), ("pa", 96, "uint16"), ("ll", 96, "uint16"), ("lr", 1536, "bfloat16")):
     SCRATCH[_n] = ("sbuf", [128, _w], _d)
+for _n in ("dl", "dr1", "dr2"):
+    SCRATCH[_n] = ("dram", [128, 32], "bfloat16")
 for _r in range(2):
     SCRATCH["q%d" % _r] = ("sbuf", [128, 320], "float8_e4m3fn_x4")
     SCRATCH["qs%d" % _r] = ("sbuf", [128, 320], "uint8")
@@ -50,7 +59,7 @@ for _r in range(3):
     SCRATCH["lq%d" % _r] = ("sbuf", [128, 320], "float8_e4m3fn_x4")
     SCRATCH["ls%d" % _r] = ("sbuf", [128, 320], "uint8")
 
-SEMAPHORES = ["cV", "cS", "cT", "cG", "sent", "stored", "lse", "lx", "lu", "lv", "lwc", "lws"] + ["hand%d" % _j for _j in range(len(HANDED))]
+SEMAPHORES = ["cV", "cS", "cT", "cG", "sent", "stored", "lse", "lx", "lu", "lv", "lwc", "lws", "dl", "lr1", "lr2"] + ["hand%d" % _j for _j in range(len(HANDED))]
 for _r in range(3):
     SEMAPHORES += ["pr%d" % _r, "lb%d" % _r, "h%d_0" % _r, "h%d_1" % _r]
 
@@ -75,7 +84,7 @@ def hand_on(g, core, T, topo):
             src, dst = T.cores[rank], T.cores[rank ^ s]
             rid, pid, _s = topo.addr(dst)
             m, n, come = topo.mask(core, dst), len(topo.engines(core, dst)), len(topo.engines(src, core))
-            ll = T.ll[:, 32 * k:32 * k + 32]
+            ll = T["dr%d" % k][:, :] if k in ROWS else T.ll[:, 32 * k:32 * k + 32]
             g.wait_ge(T.sem["lb%d" % k], come)
             g.remote_dma(ll, ll, T.sem["lb%d" % k], T.sem.sent, pid, rid, m)
             for j, (kind, a, b) in enumerate(HANDED):
@@ -92,13 +101,14 @@ def rank_program(g, core, T, topo):
     eng = {"V": g.vector, "S": g.scalar, "T": g.tensor, "G": g, "Y": g.sync}
     cnt = {"V": 0, "S": 0, "T": 0, "G": 0}
     known = {q: {} for q in eng}
-    lastw, readers = {}, {}
+    lastw, readers, behind = {}, {}, {}
 
     def wait(q, stamp):
         sem, val = stamp
         if known[q].get(sem, 0) < val:
             eng[q].wait_ge(T.sem[sem], val)
             known[q][sem] = val
+            for s, v in behind.get(stamp, {}).items(): known[q][s] = max(known[q].get(s, 0), v)
 
     def order(q, r, w):
         need = {}
@@ -107,7 +117,7 @@ def rank_program(g, core, T, topo):
         for t in w:
             if t in lastw: need[lastw[t][0]] = max(need.get(lastw[t][0], 0), lastw[t][1])
             for s, v in readers.get(t, []): need[s] = max(need.get(s, 0), v)
-        for s in sorted(need): wait(q, (s, need[s]))
+        for s in sorted(need, key=lambda s: -sum(behind.get((s, need[s]), {}).get(x, 0) >= need[x] for x in need)): wait(q, (s, need[s]))
 
     def mark(r, w, stamp):
         for t in r: readers.setdefault(t, []).append(stamp)
@@ -121,11 +131,18 @@ def rank_program(g, core, T, topo):
         order(q, r, w)
         cnt[q] += 1
         call(eng[q]).then_inc(T.sem["c" + q], 1)
+        if LEARN: behind["c" + q, cnt[q]] = dict(known[q])
         mark(r, w, ("c" + q, cnt[q]))
 
     def load(q, out, in_, w, sem):
         eng[q].dma_start(out, in_).then_inc(T.sem[sem], 16)
         mark([], [w], (sem, 16))
+
+    def moves(pairs, r, w, sem):
+        order("Y", r, w)
+        for out, in_ in pairs:
+            g.sync.dma_start(out, in_).then_inc(T.sem[sem], 16)
+        mark(r, w, (sem, 16 * len(pairs)))
 
     stores = [0]
 
@@ -158,10 +175,14 @@ def rank_program(g, core, T, topo):
     def bank(b, n=C): return T.ps[:, 512 * b:512 * b + n]
 
     def latch(out, row, n, r, w):
-        vscan(out, T.d0l[:, 0:n], row, 0.0, A.add, A.max, r + ["d0l"], w)
+        vscan(out, T.d0l[:, 0:n], row, 0.0, A.add, A.max, r + ["d0l%d" % j for j in range(6) if 8 << j < n], w)
 
-    def listed(out, latched, r, w):
-        vts(out, latched, ln["subl"], None, A.subtract, None, r + ["subl"], w)
+    def listed(out, latched, r, w, mid=0.0):
+        vts(out, latched, ln["subl"], mid, A.subtract, A.add, r + ["subl"], w)
+
+    def shifted(e, out, in_, by, r, w):
+        if e == "V": vts(out, in_, by, None, A.add, None, r, w)
+        else: act(out, in_, r, w, F.Identity, by)
 
     sent = [0]
 
@@ -177,40 +198,45 @@ def rank_program(g, core, T, topo):
 
     def codes(r): return T["q%d" % (r % 2)], T["qs%d" % (r % 2)]
     def runs(r): return [(0, CUT[r - 1]), (CUT[r - 1], C)] if r else [(0, C)]
-    def qtags(r): return ["q%d.%d" % (r % 2, i) for i in range(len(runs(r)))]
-    LAYER = [[4, 5, 6, 7], [2, 3, 0, 1]]
+    def qtags(r): return ["q%d.%d" % (r % 2, i) for i in range(2)]
+    LAYER, UNPACK = [[4, 5, 6, 7], [2, 3, 0, 1]], [[4, 5, 6, 7], UN1]
+    def sends(r): return runs(r) if relay[r] is not None or not WHOLE else [(0, C)]
 
     def scores(r, i):
         (q, qs), (c0, c1) = codes(r), runs(r)[i]
-        mm(i, T.ur[:, 0:128], T.urs[:, 0:128], q[:, c0:c1], qs[:, c0:c1], [qtags(r)[i], "ur", "urs"], c1 - c0)
+        mm(i, T.ur[:, 0:128], T.urs[:, 0:128], q[:, c0:c1], qs[:, c0:c1], (qtags(r)[i:i + 1] if r else qtags(r)) + ["ur", "urs"], c1 - c0)
 
     def signs(r, i):
         (c0, c1), k = (runs(r)[i], i) if r else ((OWN * i, OWN * i + C), 0)
         act(T.tb[:, c0:c1], bank(k, c1 - c0), ["bank%d" % k], ["tb%d" % i], F.Sign, bias=2.0 ** -100)
 
     def layer(r, i):
-        (q, qs), (c0, c1) = codes(r), runs(r)[i]
+        (q, qs), (c0, c1) = codes(r), sends(r)[i]
         for b, k in enumerate(LAYER[i]):
-            mm(k, T.wq[:, 128 * b:128 * b + 128], T.wqs[:, 128 * b:128 * b + 128], q[:, c0:c1], qs[:, c0:c1], [qtags(r)[i], "wq", "wqs"], c1 - c0)
+            mm(k, T.wq[:, 128 * b:128 * b + 128], T.wqs[:, 128 * b:128 * b + 128], q[:, c0:c1], qs[:, c0:c1], (qtags(r) if c1 - c0 == C else [qtags(r)[i]]) + ["wq", "wqs"], c1 - c0)
 
     def scaled(e, r, i, b):
-        (c0, c1), k = runs(r)[i], LAYER[i][b]
-        out, tags = T.hb[:, 4 * c0 + b:4 * c1:4], (["bank%d" % k], ["hb%d.%d" % (i, b)])
+        (c0, c1), k = sends(r)[i], LAYER[i][b]
+        out, tags = T.hb[:, 4 * c0 + b:4 * c1:4], (["bank%d" % k], ["hb%d.%d" % (j, b) for j in range(2) if j == i or c1 - c0 == C])
         if e == "S": act(out, bank(k, c1 - c0), *tags, scale=0.03125)
         else: vts(out, bank(k, c1 - c0), 0.03125, None, A.mult, None, *tags)
 
+    def halved(e, h, b):
+        out, in_, tags = T.hb[:, 640 * h + b:640 * h + 640:4], T.ps[:, 512 * (4 + b) + 160 * h:512 * (4 + b) + 160 * h + 160], (["bank%d" % (4 + b)], ["hb%d.%d" % (h, b)])
+        if e == "S": act(out, in_, *tags, scale=0.03125)
+        else: vts(out, in_, 0.03125, None, A.mult, None, *tags)
+
     def pack(r, i):
-        (c0, c1), hq, hs, t = runs(r)[i], T["hq%d" % r], T["hs%d" % r], "hq%d.%d" % (r, i)
+        (c0, c1), hq, hs, t = sends(r)[i] if relay[r] is not None else (160 * i, 160 * i + 160), T["hq%d" % r], T["hs%d" % r], "hq%d.%d" % (r, i)
         quant(hq[:, c0:c1], hs[:, c0:c1], T.hb[:, 4 * c0:4 * c1], ["hb%d.%d" % (i, b) for b in range(4)], [t])
         for j, (kind, a, b) in enumerate(HANDED if relay[r] is not None else []):
             if c0 <= a < c1: send(piece(T, "h", kind, r, a, b), piece(T, "h", kind, r, a, b), "hand%d" % j, relay[r], [t])
-        if i == 0: post(r, i)
 
     def post(r, i):
-        c0, c1 = runs(r)[i]
+        c0, c1 = sends(r)[i]
         come = (HANDED, DIRECT) if relay[r] is not None else ([], [("q", c0, c1), ("s", c0, c1)])
         for kind, a, b in come[1]:
-            if c0 <= a < c1: send(piece(T, "l", kind, r, a, b), piece(T, "h", kind, r, a, b), "h%d_%d" % (r, i), partner[r], ["hq%d.%d" % (r, i)])
+            if c0 <= a < c1: send(piece(T, "l", kind, r, a, b), piece(T, "h", kind, r, a, b), "h%d_%d" % (r, i), partner[r], ["hq%d.%d" % (r, j) for j in range(2) if j == i or c1 - c0 == C])
         mark([], ["lq%d.%d" % (r, i)], ("h%d_%d" % (r, i), sum(len(topo.engines(src, core)) for src, pieces in zip((theirs[r], partner[r]), come) for kind, a, b in pieces if c0 <= a < c1)))
 
     XR = ["xr%d.%d" % (i, b) for i in range(2) for b in range(4)]
@@ -219,55 +245,88 @@ def rank_program(g, core, T, topo):
         x, tags = (T.xr, XR) if r else (T.x0, ["x0"])
         copy(e, T.xp[:, 640 * h + b:640 * h + 640:4], x[:, 0:4 * C].indirect(T.parl[:, 20 * b + 10 * h:20 * b + 10 * h + 10]), tags + ["par%d" % b], ["xp%d.%d" % (b, h)])
 
-    def requant(): quant(T.pq[:, :], T.pqs[:, :], T.xp[:, :], ["xp%d.%d" % (b, h) for b in range(4) for h in range(2)], ["pq"])
+    def requant(h): quant(T.pq[:, 160 * h:160 * h + 160], T.pqs[:, 160 * h:160 * h + 160], T.xp[:, 640 * h:640 * h + 640], ["xp%d.%d" % (b, h) for b in range(4)], ["pq%d" % h])
 
     def above(r):
         for b in range(4):
-            mm(b, T.eq[:, 128 * b:128 * b + 128], T.es[:, 128 * b:128 * b + 128], T.pq[:, :], T.pqs[:, :], ["pq", "eq%d" % b])
+            mm(b, T.eq[:, 128 * b:128 * b + 128], T.es[:, 128 * b:128 * b + 128], T.pq[:, :], T.pqs[:, :], ["pq0", "pq1", "eq%d" % b])
 
     def kept(e, r, b):
         c0, c1 = 0, max(cut(r, j)[1] for j in range(2) if (j, b) not in HELD)
         copy(e, T.fg[:, C * b + c0:C * b + c1], bank(b, c1), ["bank%d" % b], ["fg%d" % b])
 
     def arrived(r, i):
-        c0, c1 = runs(r)[i]
+        c0, c1 = sends(r)[i]
         for b in (2, 0, 3, 1):
-            mm(4 + b, T.eq[:, 128 * b:128 * b + 128], T.es[:, 128 * b:128 * b + 128], T["lq%d" % r][:, c0:c1], T["ls%d" % r][:, c0:c1], ["lq%d.%d" % (r, i), "eq%d" % b], c1 - c0)
+            mm(UNPACK[i][b], T.eq[:, 128 * b:128 * b + 128], T.es[:, 128 * b:128 * b + 128], T["lq%d" % r][:, c0:c1], T["ls%d" % r][:, c0:c1], ["lq%d.%d" % (r, i), "eq%d" % b], c1 - c0)
 
     def taken(e, r, i, b):
-        (c0, c1), k = runs(r)[i], 4 + b
+        (c0, c1), k = sends(r)[i], UNPACK[i][b]
         copy(e, T.aw[:, C * b + c0:C * b + c1], bank(k, c1 - c0), ["bank%d" % k], ["aw%d.%d" % (i, b)])
 
     E0 = ["e0.%d" % j for j in range(10)]
 
+    def turned(e, r, h):
+        win, at, tags = (T.tb[:, 0:C], T.ls, ["ls"]) if r else (T.tb[:, 0:OWN + C], T.cl, ["cl0", "cl1", "cl8"])
+        copy(e, T.sm[:, 240 + 128 * h:368 + 128 * h], win.indirect(at[:, 8 * h:8 * h + 8]), ["tb0", "tb1"] + tags, ["mg%d" % h])
+
+    def stepped(e, h):
+        src, tags = (T.e1, ["e1"]) if h < 2 else (T.e0, E0[:6])
+        if h == 0: copy(e, T.e0[:, 0:48], T.e1[:, 0:48], ["e1"], E0[6:])
+        elif e == "V": vts(T.e0[:, 48:96], src[:, 48:96], ln["small"], None, A.mult, None, tags + ["small"], E0[:6])
+        else: act(T.e0[:, 48:96], src[:, 48:96], tags + ["small"], E0[:6], F.Identity, None, ln["small"])
+
     def positions(r):
-        eo, en, te, tn = (T.e0, T.e1, E0, ["e1"]) if r % 2 == 0 else (T.e1, T.e0, ["e1"], E0)
-        turns = T.tb[:, 0:C].indirect(T.ls[:, 0:16]) if r else T.tb[:, 0:OWN + C].indirect(T.cl[:, 0:16])
         pl = T.pl[:, 32 * r:32 * r + 32]
-        yield vtt(T.sm[:, 240:496], turns, T.mk[:, 0:256], A.mult, ["tb0", "tb1", "mk", "mk1", "ls" if r else "cl0", "cl1", "cl8"], ["mg"])
-        yield vscan(T.sm[:, 0:240], T.d0r[:, 0:240], T.sm[:, 256:496], 0.0, A.mult, A.add, ["mg", "d0r"], ["sc"])
-        yield vtt(en[:, :], T.sm[:, 0:256].indirect(T.tl[:, 0:6]), eo[:, :], A.mult, ["sc", "mg", "tl"] + te, tn)
-        yield vscan(T.pp[:, :], T.d0t[:, :], en[:, :], 0.0, A.mult, A.add, tn + ["d0t", "d0t1"], ["pp"])
+        if MASKED[r]:
+            eo, en, te, tn = (T.e0, T.e1, E0, ["e1"]) if r % 2 == 0 else (T.e1, T.e0, ["e1"], E0)
+            turns = T.tb[:, 0:C].indirect(T.ls[:, 0:16]) if r else T.tb[:, 0:OWN + C].indirect(T.cl[:, 0:16])
+            yield vtt(T.sm[:, 240:496], turns, T.mk[:, 0:256], A.mult, ["tb0", "tb1", "mk", "mk1", "ls" if r else "cl0", "cl1", "cl8"], ["mg"])
+            yield vscan(T.sm[:, 0:240], T.d0r[:, 0:240], T.sm[:, 256:496], 0.0, A.mult, A.add, ["mg", "d0r"], ["sc"])
+            yield vtt(en[:, :], T.sm[:, 0:256].indirect(T.tl[:, 0:6]), eo[:, :], A.mult, ["sc", "mg", "tl"] + te, tn)
+            yield vscan(T.pp[:, :], T.d0t[:, :], en[:, :], 0.0, A.mult, A.add, tn + ["d0t", "d0t1"], ["pp"])
+            vts(pl, T.pp[:, 16:96].indirect(T.tl[:, 6:8]), T.pp[:, 15:16], 256.0, A.add, A.add, ["pp", "tl"], ["pl%d" % r])
+            send(T.pa[:, 32 * r:32 * r + 32], pl, "pr%d" % r, partner[r], ["pl%d" % r])
+            mark([], ["pa%d" % r], ("pr%d" % r, len(topo.engines(core, partner[r]))))
+            yield
+        yield turned("V", r, 0)
+        yield vscan(T.sm[:, 0:240], T.d0s[:, 0:240], T.sm[:, 256:496], 0.0, A.mult, A.add, ["mg0", "mg1"] + ["d0s%d" % j for j in range(5)], ["sc"])
+        yield vtt(T.e1[:, :], T.sm[:, 0:256].indirect(T.tl[:, 0:6]), T.e0[:, :], A.mult, ["sc", "mg0", "tl"] + E0, ["e1"])
+        yield vscan(T.pp[:, :], T.d0t[:, :], T.e1[:, :], 0.0, A.mult, A.add, ["e1", "d0t", "d0t1"], ["pp"])
         vts(pl, T.pp[:, 16:96].indirect(T.tl[:, 6:8]), T.pp[:, 15:16], 256.0, A.add, A.add, ["pp", "tl"], ["pl%d" % r])
         send(T.pa[:, 32 * r:32 * r + 32], pl, "pr%d" % r, partner[r], ["pl%d" % r])
         mark([], ["pa%d" % r], ("pr%d" % r, len(topo.engines(core, partner[r]))))
         yield
 
     def labels(k):
-        send(T.ll[:, 32 * k:32 * k + 32], T.cl[:, 2:34], "lb%d" % k, relay[k] or partner[k], ["cl1", "cl8", "cl16", "clab"])
+        if k in ROWS: send(T["dr%d" % k][:, :], T.dl[:, :], "lb%d" % k, relay[k] or partner[k], ["dl"])
+        elif not SPLIT: send(T.ll[:, 32 * k:32 * k + 32], T.cl[:, 2:34], "lb%d" % k, relay[k] or partner[k], ["cl1", "cl8", "clab", "cl16"])
+        else: send(T.ll[:, 0:16], T.cl[:, 2:18], "lb0", partner[0], ["cl1", "cl8", "clab"])
         mark([], ["ll%d" % k], ("lb%d" % k, len(topo.engines(theirs[k] or partner[k], core))))
+
+    def leaves():
+        send(T.ll[:, 16:32], T.cl[:, 18:34], "lb3", partner[0], ["cl16"])
+        mark([], ["ll3"], ("lb3", len(topo.engines(partner[0], core))))
+
+    def rows():
+        moves([(T.dl[16 * h:16 * h + 16, :], T.lt[32 * (h // 2):32 * (h // 2) + 32, 16 * (h % 2):16 * (h % 2) + 16]) for h in range(8)], ["lt"], ["dl"], "dl")
+
+    def laid_out(k):
+        moves([(T.lr[j:128:16, 512:1024], T["dr%d" % k][:, :]) for j in range(16)], ["ll%d" % k], ["lr2", "lr3"], "lr%d" % k)
 
     def spread(e, k, h):
         j = 2 * k + h
-        copy(e, T.lr[:, 256 * j:256 * j + 256], T.it[:, :].indirect(T.ll[:, 16 * j:16 * j + 16]), ["it0", "it1", "it2", "ll%d" % k], ["lr%d" % j])
+        shifted(e, T.lr[:, 256 * j:256 * j + 256], T.it[:, :].indirect(T.ll[:, 16 * j:16 * j + 16]), -C / 2, ["it0", "it1", "it2", "ll%d" % k], ["lr%d" % j])
 
     def prep(e, r, h):
-        copy(e, T.prep[:, 256 * h:256 * h + 256], T.it[:, 0:520].indirect(T.pl[:, 32 * r + 16 * h:32 * r + 16 * h + 16]), ["it0", "it1", "it2", "pl%d" % r], ["prep%d" % h])
+        shifted(e, T.prep[:, 256 * h:256 * h + 256], T.it[:, 0:520].indirect(T.pl[:, 32 * r + 16 * h:32 * r + 16 * h + 16]), -256.0, ["it0", "it1", "it2", "pl%d" % r], ["prep%d" % h])
 
     def brep(e, h):
         copy(e, T.brep[:, 160 * h:160 * h + 160], T.prep[:, :].indirect(T.al[:, 10 * h:10 * h + 10]), ["prep0", "prep1", "al"], ["brep%d" % h])
 
-    def zt(r): vcp(T.zt[:, :].indirect(T.pa[:, 32 * r:32 * r + 32]), T.lr[:, 512 * r:512 * r + 512], ["pa%d" % r, "lr%d" % (2 * r), "lr%d" % (2 * r + 1)], ["zt"])
+    def zt(r):
+        k = 1 if r in ROWS else r
+        vcp(T.zt[:, :].indirect(T.pa[:, 32 * r:32 * r + 32]), T.lr[:, 512 * k:512 * k + 512], ["pa%d" % r, "lr%d" % (2 * k), "lr%d" % (2 * k + 1)], ["zt"])
 
     def placed(): latch(T.bsc[:, :], T.brep[:, :], C, ["brep0", "brep1"], ["bsc"])
 
@@ -281,7 +340,7 @@ def rank_program(g, core, T, topo):
         if stage == 0 and r == 0: copy(e, T.mr[:, c0:c1], T.prep[:, :].indirect(T.al[:, c0 // 16:c1 // 16]), ["prep0", "prep1", "al"], ["mr%d" % i])
         if stage == 0 and r > 0: copy(e, T.mr[:, c0:c1], T.zt[:, :].indirect(T.bl[:, c0 // 16:c1 // 16]), ["zt", "bl"], ["mr%d" % i])
         if stage == 1: latch(T.msc[:, c0:c1], T.mr[:, c0:c1], c1 - c0, ["mr%d" % i], ["msc%d" % i])
-        if stage == 2: listed(T.ml[:, c0 // 16:c1 // 16], T.msc[:, c0 + 15:c1:16], ["msc%d" % i], ["ml%d" % i])
+        if stage == 2: listed(T.ml[:, c0 // 16:c1 // 16], T.msc[:, c0 + 15:c1:16], ["msc%d" % i], ["ml%d" % i], C / 2)
 
     def mapped_h(r, j, b): return T.aw[:, C * b:C * b + C].indirect(T.ml[:, cut(r, j)[0] // 16:cut(r, j)[1] // 16]), ["aw0.%d" % b, "aw1.%d" % b, "ml%d" % j]
 
@@ -298,7 +357,7 @@ def rank_program(g, core, T, topo):
             vtt(out, a, T.fg[:, C * b + c0:C * b + c1], A.add, tags + ["fg%d" % b], ["xr%d.%d" % (j, b)])
 
     def made_q(r, i):
-        (q, qs), (c0, c1), x = codes(r), runs(r)[i], T.xr if r else T.x0
+        (q, qs), (c0, c1), x = codes(r), runs(r)[i] if r else (160 * i, 160 * i + 160), T.xr if r else T.x0
         quant(q[:, c0:c1], qs[:, c0:c1], x[:, 4 * c0:4 * c1], ["xr%d.%d" % (j, b) for b in range(4) for j in range(2) if cut(r - 1, j)[0] < c1 and c0 < cut(r - 1, j)[1]] if r else ["x0"], [qtags(r)[i]])
 
     load("Y", T.sei[:, :], T.se[:, :], "sei", "lse")
@@ -325,23 +384,25 @@ def rank_program(g, core, T, topo):
             (T.fc[:, 48:88:5], [[0, 8]], 15), (T.fc[:, 49:88:5], [[16, 2], [0, 4]], 31), (T.fc[:, 50:88:5], [[16, 4], [0, 2]], 63),
             (T.fc[:, 51:88:5], [[16, 8]], 127), (T.fc[:, 52:88:5], [[16, 8]], 127), (T.fc[:, 0:48], [[0, 3], [1, 16]], 240), (T.fc[:, 88:96], [[0, 8]], 0),
             (T.fc[:, 96:98], [[20, 2]], 32), (T.fc[:, 98:102], [[10, 4]], 33), (T.fc[:, 102:110], [[5, 8]], 34),
-            (T.fc[:, 110:126], [[5, 8], [1, 2]], 35), (T.fc[:, 126:128], [[-16, 2]], 31))):
+            (T.fc[:, 110:112], [[-16, 2]], 31), (T.fc[:, 112:128], [[5, 8], [1, 2]], 35))):
         iota(ap, pat, base, 0, [FC[j]])
     for j, (ap, pat, base) in enumerate((
             (T.e0[:, 48:88:5], [[16, 2], [0, 4]], -8), (T.e0[:, 49:88:5], [[0, 2], [8, 2], [0, 2]], -4), (T.e0[:, 50:88:5], [[0, 4], [4, 2]], -2),
             (T.e0[:, 51:88:5], [[0, 8]], -1), (T.e0[:, 52:88:5], [[0, 8]], 2), (T.e0[:, 88:96], [[0, 8]], 0))):
         iota(ap, pat, base, 0, [E0[j]])
     iota(T.ji[:, :], [[16, 16]], 4 * C, 1, ["ji"])
-    iota(T.kr[:, 0:16], [[1, 16]], 480, 0, ["kr0"])
-    iota(T.kr[:, 16:256], [[32, 15], [1, 16]], 0, 0, ["kr1"])
+    def firsts():
+        iota(T.kr[:, 0:16], [[1, 16]], 224 - 256, 0, ["kr0"])
+        iota(T.kr[:, 16:128], [[32, 7], [1, 16]], -256, 0, ["kr1"])
+        iota(T.kr[:, 128:256], [[32, 8], [1, 16]], 0, 0, ["kr2"])
 
     BITS = (15, 8, 4, 2, 1)
     for j, m in enumerate(BITS):
         vts(T.xi[:, j:j + 1], T.pi[:, :], m, None, A.bitwise_and, None, ["pi"], ["xi%d" % m])
     vcp(T.ln[:, 0:5], T.xi[:, 0:5], ["xi%d" % m for m in BITS], ["x%d" % m for m in BITS])
     made = (
-        ("mid", "x15", 16.0, 8.0), ("subl", "x15", -1024.0, 15360.0), ("way1", "x8", 2.0, "x1"), ("subl1", "trash", -8.0 / (2 * C), "subl"), ("way2", "x4", 8.0, "way1"), ("way", "x2", 32.0, "way2"))
-    ln = {n: T.ln[:, j:j + 1] for j, n in enumerate(["x%d" % m for m in BITS] + ["trash", "some"] + [m[0] for m in made])}
+        ("mid", "x15", 16.0, 8.0), ("next", "x15", 1.0, 1.0), ("subl", "last", -1024.0, 1024.0), ("way1", "x8", 2.0, "x1"), ("subl0", "last", -1024.0, 768.0), ("subl1", "trash", -8.0 / (2 * C), "subl0"), ("way2", "x4", 8.0, "way1"), ("way", "x2", 32.0, "way2"))
+    ln = {n: T.ln[:, j:j + 1] for j, n in enumerate(["x%d" % m for m in BITS] + ["trash", "some", "last", "small"] + [m[0] for m in made])}
     side = {}
 
     def lane(e, n, x, scale, bias):
@@ -390,10 +451,18 @@ def rank_program(g, core, T, topo):
         "one": (vts, T.one[:, :], T.it[:, 0:15], ln["subl"], T.fs[:, 143:144], A.add, A.is_equal, ["it0", "subl", "fs"], ["one"]),
         "upm": (vtt, T.upm[:, :], T.up[:, :], T.one[:, :], A.mult, ["up0", "up1", "up3", "one"], ["upm"]), "top": (vred, T.yt[:, 1:2], T.upm[:, :], ["upm"], ["top"]),
         "cl0": (vcp, T.cl[:, 0:1], T.yt[:, 1:2], ["top"], ["cl0"]), "wu": (pair, 16, T.yt[:, 1:2], ["top"], 1),
-        "clab": (vts, T.cl[:, 32:34], T.gs[:, 239:256:16], ln["some"], None, A.mult, None, ["gs4", "some"], ["clab"]),
+        "clab": (vts, T.cl[:, 16:18], T.gs[:, 239:256:16], ln["some"], None, A.mult, None, ["gs4", "some"], ["clab"]),
         "m4": (vts, T.m4[:, :], T.it[:, 0:128], ln["way"], None, A.is_equal, None, ["it0", "way"], ["m4"]),
         "mk": (vts, T.mk[:, 16:336], T.i16[:, :], ln["x15"], None, A.is_equal, None, ["i16", "x15"], ["mk"]),
-        "d0l": (act, T.d0l[:, :], T.mk[:, 16:336], ["mk"], ["d0l"], F.Identity, 1024.0, -66560.0),
+        "d0a": (vts, T.d0a[:, 0:16], T.it[:, 0:16], ln["x15"], -4096.0, A.is_equal, A.mult, ["it0", "x15"], ["d0a"]),
+        "d0b": (vts, T.d0a[:, 16:32], T.it[:, 0:16], ln["next"], 1024.0, A.is_equal, A.mult, ["it0", "next"], ["d0b"]),
+        "d0l": (vtt, T.d0l[:, 0:16], T.d0a[:, 0:16], T.d0a[:, 16:32], A.add, ["d0a", "d0b"], ["d0l0"]),
+        **{"d%d%s" % (n, e): (copy, e, T.d0l[:, n:min(2 * n, C)], T.d0l[:, 0:min(n, C - n)], ["d0l%d" % i for i in range(j + 1)], ["d0l%d" % (j + 1)]) for j, n in enumerate((16, 32, 64, 128, 256)) for e in "SV"},
+        "last": (vts, ln["last"], T.xi[:, 0:1], 15.0, None, A.is_equal, None, ["xi15"], ["last"]), "small": (vts, ln["small"], ln["last"], 1.0 / BIG, None, A.max, None, ["last"], ["small"]),
+        "s0a": (vts, T.d0a[:, 32:48], T.it[:, 0:16], ln["next"], BIG, A.is_equal, A.mult, ["it0", "next"], ["s0a"]),
+        "s0b": (vts, T.d0a[:, 48:64], T.it[:, 0:16], ln["x15"], None, A.not_equal, None, ["it0", "x15"], ["s0b"]),
+        "d0s": (vtt, T.d0s[:, 0:16], T.d0a[:, 32:48], T.d0a[:, 48:64], A.max, ["s0a", "s0b"], ["d0s0"]),
+        **{"s%d%s" % (16 << j, e): (copy, e, T.d0s[:, 16 << j:32 << j], T.d0s[:, 0:16 << j], ["d0s%d" % i for i in range(j + 1)], ["d0s%d" % (j + 1)]) for j in range(4) for e in "SV"},
         "an": (vtt, T.an[:, :], T.ad[:, :], T.zz[:, :], A.is_lt, ["ad"] + ZZ, ["an"]), "w1": (vtt, T.w1[:, :], T.sg[:, :], T.zz[:, :], A.mult, ["sg"] + ZZ, ["w1"]),
         "down": (vtt, T.e0[:, 0:16], T.w1[:, :], T.an[:, :], A.mult, ["w1", "an"], [E0[6]]),
         "cl1": (vts, T.cl[:, 1:8], T.wv[:, 2:16:2], 0.5, None, A.mult, None, ["wv2a", "wv4a", "wv8a"], ["cl1"]),
@@ -402,10 +471,12 @@ def rank_program(g, core, T, topo):
         "back": (vtt, T.e0[:, 16:32], T.e0[:, 0:16], T.tm[:, :], A.mult, [E0[6], "tm"], [E0[7]]),
         "own": (vts, T.e0[:, 32:48], T.zl[:, :], -2.0, -256.0, A.mult, A.max, ["zl"], [E0[8]]),
         "s1": (vts, T.s1[:, :], T.sei[:, :], 1, None, A.bitwise_and, None, ["sei"], ["s1"]),
-        "st": (vts, T.st[:, 1:20], T.s1[:, 1:20], 16.0, ln["subl"], A.mult, A.subtract, ["s1", "subl"], ["st"]),
+        "st": (vts, T.st[:, 1:20], T.s1[:, 1:20], 16.0, ln["subl0"], A.mult, A.subtract, ["s1", "subl0"], ["st"]),
         "st0": (vts, T.st[:, 0:1], T.s1[:, 0:1], 16.0, ln["subl1"], A.mult, A.subtract, ["s1", "subl1"], ["st0"]),
-        "ci": (vcp, T.ci[:, :], T.cl[:, 0:16], ["cl0", "cl1", "cl8"], ["ci"]), "cj": (vts, T.cj[:, :], T.ci[:, :], OWN - 1, None, A.bitwise_and, None, ["ci"], ["cj"]),
-        "ls": (vcp, T.ls[:, :], T.cj[:, :], ["cj"], ["ls"]),
+        "lc": (vts, T.lc[:, :], T.cj[:, 2:34], -C / 2, None, A.add, None, ["cj"], ["lc"]), "lt": (op, "V", lambda e: e.transpose(T.lt[:, :], T.lc[:, :]), ["lc"], ["lt"]),
+        "rows": (rows,), "out1": (laid_out, 1), "out2": (laid_out, 2),
+        "ci": (vcp, T.ci[:, :], T.cl[:, :], ["cl0", "cl1", "cl8", "cl16", "clab"], ["ci"]), "cj": (vts, T.cj[:, :], T.ci[:, :], OWN - 1, None, A.bitwise_and, None, ["ci"], ["cj"]),
+        "ls": (vcp, T.ls[:, :], T.cj[:, 0:16], ["cj"], ["ls"]),
         "fs": (latch, T.fs[:, :], T.fc[:, :], 144, FC, ["fs"]), "tl": (listed, T.tl[:, :], T.fs[:, 15:128:16], ["fs"], ["tl"])})
     side.update({"t%d" % b: (tiles, b) for b in range(4)})
 
@@ -417,17 +488,17 @@ def rank_program(g, core, T, topo):
         for c in range(4): vts(T.wo[:, 68 + c:132:4], kid.indirect(T.wo[:, 4 + 2 * c:5 + 2 * c]), 2.0, ln["x1"], A.mult, A.add, KID + ["wo2.%d" % (c % 2), "x1"], ["wo3.%d" % c])
         yield
         yield vtt(T.g4[:, :], kid.indirect(T.wo[:, 68:76]), T.m4[:, :], A.mult, KID + WO3 + ["m4"], ["g4"])
-        yield vred(T.yt[:, 0:1], T.g4[:, :], ["g4"], ["yt"])
-        yield pair(2, T.yt[:, 0:1], ["yt"], 1)
+        yield vscan(T.g5[:, :], T.g4[:, :], T.g4[:, :], 0.0, A.max, A.max, ["g4"], ["yt"])
+        yield pair(2, T.g5[:, 127:128], ["yt"], 1)
         for n in (1, 2, 4, 8): yield from below(n)
 
     def below(n):
         a, b = {1: (2, 4), 2: (4, 8), 4: (8, 18), 8: (18, 34)}[n]
         h, k = 16 * a - 32, 16 * (b - a)
         if n == 8 and LEAVES == "S":
-            yield act(T.gg[:, h:h + k], kid.indirect(T.wv[:, a:b]), KID + ["wv18a", "wv18b"], ["gg8"])
-            yield latch(T.gs[:, h:h + k], T.gg[:, h:h + k], k, ["gg8"], ["gs8"])
-            yield listed(T.cl[:, 16:32], T.gs[:, h + 15:h + k:16], ["gs8"], ["cl16"])
+            yield act(T.lg[:, :], kid.indirect(T.wv[:, a:b]), KID + ["wv18a", "wv18b"], ["gg8"])
+            yield latch(T.lf[:, :], T.lg[:, :], k, ["gg8"], ["gs8"])
+            yield listed(T.cl[:, 18:34], T.lf[:, 15:k:16], ["gs8"], ["cl16"])
         yield vtt(T.gg[:, h:h + k], kid.indirect(T.wv[:, a:b]), T.mk[:, 16:16 + k], A.mult, KID + ["wv%d%s" % (j, c) for j in (a, b - 2 * (n == 4)) for c in "ab"] + ["mk"], ["gg%d" % n])
         yield vscan(T.gs[:, h:h + k], T.d0r[:, 0:k], T.gg[:, h:h + k], 0.0, A.mult, A.add, ["gg%d" % n, "d0r"], ["gs%d" % n])
         y = T.gs[:, h + 15:h + 32 * n:16]
@@ -436,10 +507,10 @@ def rank_program(g, core, T, topo):
         yield
 
     side.update({
-        "*": (next, tree()), "lab0": (labels, 0), "lab1": (labels, 1), "lab2": (labels, 2),
+        "*": (next, tree()), "lab0": (labels, 0), "lab3": (leaves,), "kr": (firsts,), **{"sg2" + e: (copy, e, T.tb[:, OWN:OWN + C], T.tb[:, 0:C], ["tb0"], ["tb1"]) for e in "SV"}, "lab1": (labels, 1), "lab2": (labels, 2),
         "yf": (vts, T.yf[:, :], T.cl[:, 0:16], 4.0, None, A.mult, None, ["cl0", "cl1", "cl8"], ["yf"]),
         "o16": (vtt, T.o16[:, :], T.yf[:, :], T.ji[:, :], A.max, ["yf", "ji"], ["o16"]), "ol": (vcp, T.ol[:, :], T.o16[:, :], ["o16"], ["ol"]),
-        "at": (vcp, T.at[:, :].indirect(T.ol[:, 0:16]), T.kr[:, :], ["ol", "kr0", "kr1"], ["at"]),
+        "at": (vcp, T.at[:, :].indirect(T.ol[:, 0:16]), T.kr[:, :], ["ol", "kr0", "kr1", "kr2"], ["at"]),
         "als": (latch, T.als[:, :], T.ar[:, :], C, ["ar0", "ar1"], ["als"]),
         "af": (vtt, T.af[:, :], T.als[:, 15:C:16], T.st[:, :], A.add, ["als", "st", "st0"], ["af"]), "al": (vcp, T.al[:, :], T.af[:, :], ["af"], ["al"]),
         "vq": (quant, T.vq[:, :], T.vs[:, :], T.vb[:, :], ["vb"], ["vq"])})
@@ -450,14 +521,18 @@ def rank_program(g, core, T, topo):
         (c0, c1), t = runs(3)[i], "q1.%d" % i
         mm(4 + i, T.vq[:, 0:128], T.vs[:, 0:128], T.q1[:, c0:c1], T.qs1[:, c0:c1], [t, "vq"], c1 - c0)
         copy(e, T.ysb[:, c0:c1], bank(4 + i, c1 - c0), ["bank%d" % (4 + i)], ["ysb%d" % i])
-        store("Y", T.oc[:, 4 * c0:4 * c1], T.q1[:, c0:c1].bitcast(dt.uint8), [t])
         store("S", T.y[:, c0:c1], T.ysb[:, c0:c1], ["ysb%d" % i])
-        for k in range(4):
-            store("Y", T.osc[4 * k:4 * k + 4, c0:c1], T.qs1[32 * k:32 * k + 4, c0:c1], [t])
+
+    def out_codes(i):
+        c0, c1 = runs(3)[i]
+        store("Y", T.oc[:, 4 * c0:4 * c1], T.q1[:, c0:c1].bitcast(dt.uint8), ["q1.%d" % i])
+
+    def out_scales():
+        for k in range(4): store("Y", T.osc[4 * k:4 * k + 4, :], T.qs1[32 * k:32 * k + 4, :], ["q1.0", "q1.1"])
 
     for r in range(4):
-        step = {"pos": (next, positions(r)), "pq": (requant,), "above": (above, r), "zt": (zt, r), "bsc": (placed,), "bl": (listed, T.bl[:, :], T.bsc[:, 15:C:16], ["bsc"], ["bl"]),
-                "im": (store, "Y", T.im[:, :], T.mr[0:128:16, :], ["mr0", "mr1"])}
+        step = {"pos": (next, positions(r)), "tnS": (turned, "S", r, 1), "tnV": (turned, "V", r, 1), **{"step%d%s" % (h, e): (stepped, e, h) for h in range(3) for e in "SV"}, "pq0": (requant, 0), "pq1": (requant, 1), "oc0": (out_codes, 0), "oc1": (out_codes, 1), "osc": (out_scales,), "above": (above, r), "zt": (zt, r), "bsc": (placed,), "bl": (listed, T.bl[:, :], T.bsc[:, 15:C:16], ["bsc"], ["bl"], 256.0),
+                "im": (store, "Y", T.im[:, :], T.mf[0:128:16, :], ["mf"]), **{"mf" + e: (shifted, e, T.mf[:, :], T.mr[:, :], C / 2, ["mr0", "mr1"], ["mf"]) for e in "SV"}}
         for i in range(2):
             step.update({"q%d" % i: (made_q, r, i), "layer%d" % i: (layer, r, i), "sc%d" % i: (scores, r, i), "sg%d" % i: (signs, r, i), "pack%d" % i: (pack, r, i), "post%d" % i: (post, r, i),
                          "un%d" % i: (arrived, r, i), "msc%d" % i: (mapped, r, i, 1), "ml%d" % i: (mapped, r, i, 2)})
@@ -467,7 +542,7 @@ def rank_program(g, core, T, topo):
                              "ar%d%s" % (i, e): (beside, e, i), "mr%d%s" % (i, e): (mapped, r, i, 0, e), "met%d%s" % (i, e): (met, e, i), "k%d%s" % (i, e): (kept, e, r, i),
                              "out%d%s" % (i, e): (out, i, e)})
                 for b in range(4):
-                    step.update({"h%d%d%s" % (i, b, e): (scaled, e, r, i, b), "xp%d%d%s" % (b, i, e): (laid, e, r, b, i), "aw%d%d%s" % (i, b, e): (taken, e, r, i, b), "ag%d%d%s" % (i, b, e): (picked, e, r - 1, i, b)})
+                    step.update({"h%d%d%s" % (i, b, e): (scaled, e, r, i, b), "g%d%d%s" % (i, b, e): (halved, e, i, b), "xp%d%d%s" % (b, i, e): (laid, e, r, b, i), "aw%d%d%s" % (i, b, e): (taken, e, r, i, b), "ag%d%d%s" % (i, b, e): (picked, e, r - 1, i, b)})
         for n in ROUNDS[r if r in (0, 3) else 1 if relay[r] is None else 2].split():
             f = step.get(n) or side[n]
             f[0](*f[1:])

from concourse.mybir import dt, AluOpType, AxisListType, ActivationFunctionType

C = 320
MACHINE = 64
STEP = [1, 2, 4]
PARTS = [(0, 192), (192, 320)]
HANDED, DIRECT = [("q", 0, 144), ("s", 192, 320)], [("q", 144, 192), ("s", 0, 192), ("q", 192, 320)]
OWN = 512
ROUNDS = [
    'kr trash last subl0S zt0S sv d0tV nextS up0V subl1S it2 sublS midS d1S way1S d0S way2S kid1 kid0 ofl0 ofl ull d0a wayS d0b kid d0l m4 * mk d16S mk1S d32S ea * q0 * q1 d64S eb d128S ad sg d0r * layer0 qu s1 up1 * some w1 zl up3 * fs * pu h00S h01S h02S h03S sc0 one * zr ai upm * an st tl own top * down par * wu pack0 * pack1 post0 * tm t3 * cl1 t0 cl0 * xp00S sg0 z0S xp10S sg1 * xp20S xp30S xp21S xp11S xp31S back clab small pos yf t1 pos * pos * o16 st0 t2 pos ol lab0 pq0 pos lab1 at lr1V un0 step0S xp01S d256S pq1 above lr0S ar0S ar1S aw01S k0S aw02S zt met0S als af met1V al s0b ci s0a step1V mr0V cj aw00S mr1S k1S aw03S msc0 msc1 d0s ml0 ls ml1',
    'lc s16V ag02S ag03S x01 x00 x10 x03 x02 ag12S s32S ag13S lr1S lr0S x11 x12 x13 q0 sc0 s64V q1 sc1 layer0 xp10V lt xp30V xp20V xp00S sg0 sg1 s128S tnS rows pos xp01V pos pq0 pos g03V pos g13V h00S h02S h01S xp11S xp21S pos prep0S pack0 pack1 prep1V xp31S post0 lab2 brep0S brep1V pq1 above bsc un0 k0S step0S step1S k1S aw02S aw00S aw03S aw01S zt out2 bl mr0V mr1V msc0 msc1 ml0 vq ml1',
    'x00 x01 ag02S ag03S x02 ag12S ag13S x03 x11 q0 layer0 sc0 x12 x10 x13 h01S h02S sg0 h00V q1 sc1 h03V sg1 layer1 xp20S tnS xp30V pack0 post0 pos xp10V pos h10V pos h13V h11S h12S xp00S xp11S xp01S pos pq0 pos pack1 post1 prep0S prep1V xp21S xp31V brep0S brep1V pq1 above bsc un0 zt k0S k1S bl mr0V aw00V mr1S aw02S un1 msc0 msc1 aw10V ml0 aw03S aw12S aw01S ml1 aw13V aw11S',
    'ag02S x00 x10 x01 x02 ag03S ag12S ag13S mfS x03 x11 x12 x13 q0 im oc0 q1 oc1 osc out0S out1V']
BIG = 2.0 ** 26
UN1 = [1, 4, 0, 6]
LEARN = True
SPLIT = False
ROWS = [2]
MASKED = [True, False, False, True]
WHOLE = True
LEAVES = "S"
CUT = [160, 192, 192]
HELD = [(0, 2), (0, 3), (1, 2), (1, 3)]
A = AluOpType
F = ActivationFunctionType

SCRATCH = {"ps": ("psum", [128, 4096], "float32")}
for _n, _w, _d in (
        ("x0", 1280, "bfloat16"), ("ub", 512, "bfloat16"), ("vb", 512, "bfloat16"), ("sei", 20, "int32"),
        ("uq", 128, "float8_e4m3fn_x4"), ("us", 128, "uint8"), ("ur", 128, "float8_e4m3fn_x4"), ("urs", 128, "uint8"),
        ("vq", 128, "float8_e4m3fn_x4"), ("vs", 128, "uint8"), ("wq", 512, "float8_e4m3fn_x4"), ("wqs", 512, "uint8"),
        ("ea", 520, "bfloat16"), ("eb", 520, "bfloat16"), ("eq", 512, "float8_e4m3fn_x4"), ("es", 512, "uint8"),
        ("xp", 1280, "bfloat16"), ("pq", 320, "float8_e4m3fn_x4"), ("pqs", 320, "uint8"),
        ("pi", 1, "int32"), ("p4", 1, "float32"), ("xi", 8, "int32"), ("ln", 24, "float32"),
        ("i16", 320, "bfloat16"), ("it", OWN + C, "float32"), ("sv", 320, "float32"), ("kr", 256, "float32"),
        ("mk", 336, "bfloat16"), ("d0r", 256, "bfloat16"), ("d0l", 320, "bfloat16"), ("d0t", 96, "bfloat16"), ("d0a", 64, "bfloat16"), ("d0s", 256, "bfloat16"),
        ("zz", 16, "float32"), ("ad", 16, "float32"), ("sg", 16, "float32"), ("an", 16, "float32"),
        ("w1", 16, "float32"), ("zl", 16, "float32"), ("zr", 1, "float32"), ("tm", 16, "float32"),
        ("ji", 16, "float32"), ("fc", 144, "float32"), ("fs", 144, "float32"), ("tl", 8, "uint16"), ("ull", 8, "uint16"), ("m4", 128, "bfloat16"), ("one", 15, "float32"),
        ("ai", 20, "int32"), ("ofl", 20, "uint16"), ("parl", 80, "uint16"), ("kid", 2 * OWN + 2 * C + 16, "int32"), ("wo", 132, "uint16"), ("wv", 34, "uint16"),
        ("g4", 128, "float16"), ("g5", 128, "float16"), ("yt", 2, "float32"), ("up", 15, "float32"), ("upm", 15, "float32"), ("gg", 256, "float16"), ("gs", 256, "float16"), ("lg", 256, "float32"), ("lf", 256, "float32"),
        ("cl", 34, "uint16"), ("ci", 34, "int32"), ("cj", 34, "int32"), ("lc", 32, "bfloat16"), ("lt", 32, "bfloat16"), ("ls", 16, "uint16"), ("yf", 16, "float32"), ("o16", 16, "float32"), ("ol", 16, "uint16"),
        ("at", 4 * (OWN + C), "float32"), ("ar", 320, "bfloat16"), ("als", 320, "float16"), ("s1", 20, "int32"), ("st", 20, "float32"), ("af", 20, "float32"), ("al", 20, "uint16"),
        ("tb", OWN + C, "bfloat16"), ("sm", 496, "bfloat16"), ("e0", 96, "bfloat16"), ("e1", 96, "bfloat16"),
        ("pp", 96, "bfloat16"), ("prep", 512, "float32"), ("brep", 320, "bfloat16"), ("bsc", 320, "float16"), ("bl", 20, "uint16"),
        ("zt", 520, "float32"), ("msc", 320, "float16"), ("ml", 20, "uint16"), ("mr", 320, "bfloat16"), ("mf", 320, "float32"), ("ysb", 320, "float32"),
        ("fg", 640, "bfloat16"), ("aw", 1280, "bfloat16"), ("ag", 1280, "bfloat16"),
        ("pl", 96, "uint16"), ("pa", 96, "uint16"), ("ll", 96, "uint16"), ("lr", 1536, "bfloat16")):
    SCRATCH[_n] = ("sbuf", [128, _w], _d)
for _n in ("dl", "dr1", "dr2"):
    SCRATCH[_n] = ("dram", [128, 32], "bfloat16")
for _r in range(2):
    SCRATCH["q%d" % _r] = ("sbuf", [128, 320], "float8_e4m3fn_x4")
    SCRATCH["qs%d" % _r] = ("sbuf", [128, 320], "uint8")
SCRATCH["xr"] = SCRATCH["hb"] = ("sbuf", [128, 1280], "bfloat16")
for _r in range(3):
    SCRATCH["hq%d" % _r] = ("sbuf", [128, 320], "float8_e4m3fn_x4")
    SCRATCH["hs%d" % _r] = ("sbuf", [128, 320], "uint8")
    SCRATCH["lq%d" % _r] = ("sbuf", [128, 320], "float8_e4m3fn_x4")
    SCRATCH["ls%d" % _r] = ("sbuf", [128, 320], "uint8")

SEMAPHORES = ["cV", "cS", "cT", "cG", "sent", "stored", "lse", "lx", "lu", "lv", "lwc", "lws", "dl", "lr1", "lr2"] + ["hand%d" % _j for _j in range(len(HANDED))]
for _r in range(3):
    SEMAPHORES += ["pr%d" % _r, "lb%d" % _r, "h%d_0" % _r, "h%d_1" % _r]


def relay_of(T, topo, rank, s):
    core, dst = T.cores[rank], T.cores[rank ^ s]
    if topo.chip(core) == topo.chip(dst): return None
    mine = [c for c in topo.cores_of(core) if T.rank_of(c) is not None]
    free = [c for c in topo.cores_of(core) if T.rank_of(c) is None and topo.die(c) != topo.die(core) and topo.may_write(c, dst)]
    return free[mine.index(core) % len(free)]


def piece(T, side, kind, r, a, b):
    if kind == "q": return T["%sq%d" % (side, r)][:, a:b].bitcast(dt.uint8)
    return T["%ss%d" % (side, r)][:, a:b]


def hand_on(g, core, T, topo):
    for rank in range(len(T.cores)):
        for k, s in enumerate(STEP):
            if relay_of(T, topo, rank, s) != core: continue
            src, dst = T.cores[rank], T.cores[rank ^ s]
            rid, pid, _s = topo.addr(dst)
            m, n, come = topo.mask(core, dst), len(topo.engines(core, dst)), len(topo.engines(src, core))
            ll = T["dr%d" % k][:, :] if k in ROWS else T.ll[:, 32 * k:32 * k + 32]
            g.wait_ge(T.sem["lb%d" % k], come)
            g.remote_dma(ll, ll, T.sem["lb%d" % k], T.sem.sent, pid, rid, m)
            for j, (kind, a, b) in enumerate(HANDED):
                g.wait_ge(T.sem["hand%d" % j], come)
                g.remote_dma(piece(T, "l", kind, k, a, b), piece(T, "h", kind, k, a, b), T.sem["h%d_%d" % (k, a >= PARTS[1][0])], T.sem.sent, pid, rid, m)
            g.wait_ge(T.sem.sent, (1 + len(HANDED)) * n)


def rank_program(g, core, T, topo):
    rank = T.rank_of(core)
    if rank is None:
        hand_on(g, core, T, topo)
        return
    eng = {"V": g.vector, "S": g.scalar, "T": g.tensor, "G": g, "Y": g.sync}
    cnt = {"V": 0, "S": 0, "T": 0, "G": 0}
    known = {q: {} for q in eng}
    lastw, readers, behind = {}, {}, {}

    def wait(q, stamp):
        sem, val = stamp
        if known[q].get(sem, 0) < val:
            eng[q].wait_ge(T.sem[sem], val)
            known[q][sem] = val
            for s, v in behind.get(stamp, {}).items(): known[q][s] = max(known[q].get(s, 0), v)

    def order(q, r, w):
        need = {}
        for t in r:
            if t in lastw: need[lastw[t][0]] = max(need.get(lastw[t][0], 0), lastw[t][1])
        for t in w:
            if t in lastw: need[lastw[t][0]] = max(need.get(lastw[t][0], 0), lastw[t][1])
            for s, v in readers.get(t, []): need[s] = max(need.get(s, 0), v)
        for s in sorted(need, key=lambda s: -sum(behind.get((s, need[s]), {}).get(x, 0) >= need[x] for x in need)): wait(q, (s, need[s]))

    def mark(r, w, stamp):
        for t in r: readers.setdefault(t, []).append(stamp)
        for t in w:
            lastw[t] = stamp
            readers[t] = []

    def op(q, call, r, w):
        bank = [t for t in r if t.startswith("bank")]
        r, w = [t for t in r if t not in bank], list(w) + bank
        order(q, r, w)
        cnt[q] += 1
        call(eng[q]).then_inc(T.sem["c" + q], 1)
        if LEARN: behind["c" + q, cnt[q]] = dict(known[q])
        mark(r, w, ("c" + q, cnt[q]))

    def load(q, out, in_, w, sem):
        eng[q].dma_start(out, in_).then_inc(T.sem[sem], 16)
        mark([], [w], (sem, 16))

    def moves(pairs, r, w, sem):
        order("Y", r, w)
        for out, in_ in pairs:
            g.sync.dma_start(out, in_).then_inc(T.sem[sem], 16)
        mark(r, w, (sem, 16 * len(pairs)))

    stores = [0]

    def store(q, out, in_, r):
        order(q, r, [])
        eng[q].dma_start(out, in_).then_inc(T.sem.stored, 16)
        stores[0] += 16

    def vts(out, in0, s1, s2, op0, op1, r, w):
        if op1 is None: op("V", lambda e: e.tensor_scalar(out, in0, s1, s2, op0), r, w)
        else: op("V", lambda e: e.tensor_scalar(out, in0, s1, s2, op0, op1), r, w)

    def vtt(out, a, b, o, r, w): op("V", lambda e: e.tensor_tensor(out, a, b, o), r, w)
    def vcp(out, in_, r, w): op("V", lambda e: e.tensor_copy(out, in_), r, w)
    def vset(ap, c, w): op("V", lambda e: e.memset(ap, c), [], w)
    def vred(out, in_, r, w): op("V", lambda e: e.tensor_reduce(out, in_, AxisListType.X, A.add), r, w)
    def vscan(out, d0, d1, ini, o0, o1, r, w): op("V", lambda e: e.tensor_tensor_scan(out, d0, d1, ini, o0, o1), r, w)
    def iota(ap, pat, base, cm, w): op("G", lambda e: e.iota(ap, pat, base, cm, allow_small_or_imprecise_dtypes=True), [], w)
    def act(out, in_, r, w, f=F.Copy, bias=None, scale=None):
        k = {n: v for n, v in (("bias", bias), ("scale", scale)) if v is not None}
        op("S", lambda e: e.activation(out, in_, f, **k), r, w)

    def quant(c, s, t, r, w): op("V", lambda e: e.quantize_mx(c, s, t), r, w)
    def copy(q, *a): (vcp if q == "V" else act)(*a)

    def mm(bank, lc, lsc, rc, rsc, r, n=C):
        out = T.ps[:, 512 * bank:512 * bank + n]
        op("T", lambda e: e.matmul_mx(out, lc, lsc, rc, rsc, True, True), r, ["bank%d" % bank])

    def bank(b, n=C): return T.ps[:, 512 * b:512 * b + n]

    def latch(out, row, n, r, w):
        vscan(out, T.d0l[:, 0:n], row, 0.0, A.add, A.max, r + ["d0l%d" % j for j in range(6) if 8 << j < n], w)

    def listed(out, latched, r, w, mid=0.0):
        vts(out, latched, ln["subl"], mid, A.subtract, A.add, r + ["subl"], w)

    def shifted(e, out, in_, by, r, w):
        if e == "V": vts(out, in_, by, None, A.add, None, r, w)
        else: act(out, in_, r, w, F.Identity, by)

    sent = [0]

    def send(out, in_, rsem, dst, r):
        order("G", r, [])
        rid, pid, _s = topo.addr(dst)
        g.remote_dma(out, in_, T.sem[rsem], T.sem.sent, pid, rid, topo.mask(core, dst))
        sent[0] += len(topo.engines(core, dst))

    partner = [T.cores[rank ^ s] for s in STEP]
    relay = [relay_of(T, topo, rank, s) for s in STEP]
    theirs = [relay_of(T, topo, rank ^ s, s) for s in STEP]

    def codes(r): return T["q%d" % (r % 2)], T["qs%d" % (r % 2)]
    def runs(r): return [(0, CUT[r - 1]), (CUT[r - 1], C)] if r else [(0, C)]
    def qtags(r): return ["q%d.%d" % (r % 2, i) for i in range(2)]
    LAYER, UNPACK = [[4, 5, 6, 7], [2, 3, 0, 1]], [[4, 5, 6, 7], UN1]
    def sends(r): return runs(r) if relay[r] is not None or not WHOLE else [(0, C)]

    def scores(r, i):
        (q, qs), (c0, c1) = codes(r), runs(r)[i]
        mm(i, T.ur[:, 0:128], T.urs[:, 0:128], q[:, c0:c1], qs[:, c0:c1], (qtags(r)[i:i + 1] if r else qtags(r)) + ["ur", "urs"], c1 - c0)

    def signs(r, i):
        (c0, c1), k = (runs(r)[i], i) if r else ((OWN * i, OWN * i + C), 0)
        act(T.tb[:, c0:c1], bank(k, c1 - c0), ["bank%d" % k], ["tb%d" % i], F.Sign, bias=2.0 ** -100)

    def layer(r, i):
        (q, qs), (c0, c1) = codes(r), sends(r)[i]
        for b, k in enumerate(LAYER[i]):
            mm(k, T.wq[:, 128 * b:128 * b + 128], T.wqs[:, 128 * b:128 * b + 128], q[:, c0:c1], qs[:, c0:c1], (qtags(r) if c1 - c0 == C else [qtags(r)[i]]) + ["wq", "wqs"], c1 - c0)

    def scaled(e, r, i, b):
        (c0, c1), k = sends(r)[i], LAYER[i][b]
        out, tags = T.hb[:, 4 * c0 + b:4 * c1:4], (["bank%d" % k], ["hb%d.%d" % (j, b) for j in range(2) if j == i or c1 - c0 == C])
        if e == "S": act(out, bank(k, c1 - c0), *tags, scale=0.03125)
        else: vts(out, bank(k, c1 - c0), 0.03125, None, A.mult, None, *tags)

    def halved(e, h, b):
        out, in_, tags = T.hb[:, 640 * h + b:640 * h + 640:4], T.ps[:, 512 * (4 + b) + 160 * h:512 * (4 + b) + 160 * h + 160], (["bank%d" % (4 + b)], ["hb%d.%d" % (h, b)])
        if e == "S": act(out, in_, *tags, scale=0.03125)
        else: vts(out, in_, 0.03125, None, A.mult, None, *tags)

    def pack(r, i):
        (c0, c1), hq, hs, t = sends(r)[i] if relay[r] is not None else (160 * i, 160 * i + 160), T["hq%d" % r], T["hs%d" % r], "hq%d.%d" % (r, i)
        quant(hq[:, c0:c1], hs[:, c0:c1], T.hb[:, 4 * c0:4 * c1], ["hb%d.%d" % (i, b) for b in range(4)], [t])
        for j, (kind, a, b) in enumerate(HANDED if relay[r] is not None else []):
            if c0 <= a < c1: send(piece(T, "h", kind, r, a, b), piece(T, "h", kind, r, a, b), "hand%d" % j, relay[r], [t])

    def post(r, i):
        c0, c1 = sends(r)[i]
        come = (HANDED, DIRECT) if relay[r] is not None else ([], [("q", c0, c1), ("s", c0, c1)])
        for kind, a, b in come[1]:
            if c0 <= a < c1: send(piece(T, "l", kind, r, a, b), piece(T, "h", kind, r, a, b), "h%d_%d" % (r, i), partner[r], ["hq%d.%d" % (r, j) for j in range(2) if j == i or c1 - c0 == C])
        mark([], ["lq%d.%d" % (r, i)], ("h%d_%d" % (r, i), sum(len(topo.engines(src, core)) for src, pieces in zip((theirs[r], partner[r]), come) for kind, a, b in pieces if c0 <= a < c1)))

    XR = ["xr%d.%d" % (i, b) for i in range(2) for b in range(4)]

    def laid(e, r, b, h):
        x, tags = (T.xr, XR) if r else (T.x0, ["x0"])
        copy(e, T.xp[:, 640 * h + b:640 * h + 640:4], x[:, 0:4 * C].indirect(T.parl[:, 20 * b + 10 * h:20 * b + 10 * h + 10]), tags + ["par%d" % b], ["xp%d.%d" % (b, h)])

    def requant(h): quant(T.pq[:, 160 * h:160 * h + 160], T.pqs[:, 160 * h:160 * h + 160], T.xp[:, 640 * h:640 * h + 640], ["xp%d.%d" % (b, h) for b in range(4)], ["pq%d" % h])

    def above(r):
        for b in range(4):
            mm(b, T.eq[:, 128 * b:128 * b + 128], T.es[:, 128 * b:128 * b + 128], T.pq[:, :], T.pqs[:, :], ["pq0", "pq1", "eq%d" % b])

    def kept(e, r, b):
        c0, c1 = 0, max(cut(r, j)[1] for j in range(2) if (j, b) not in HELD)
        copy(e, T.fg[:, C * b + c0:C * b + c1], bank(b, c1), ["bank%d" % b], ["fg%d" % b])

    def arrived(r, i):
        c0, c1 = sends(r)[i]
        for b in (2, 0, 3, 1):
            mm(UNPACK[i][b], T.eq[:, 128 * b:128 * b + 128], T.es[:, 128 * b:128 * b + 128], T["lq%d" % r][:, c0:c1], T["ls%d" % r][:, c0:c1], ["lq%d.%d" % (r, i), "eq%d" % b], c1 - c0)

    def taken(e, r, i, b):
        (c0, c1), k = sends(r)[i], UNPACK[i][b]
        copy(e, T.aw[:, C * b + c0:C * b + c1], bank(k, c1 - c0), ["bank%d" % k], ["aw%d.%d" % (i, b)])

    E0 = ["e0.%d" % j for j in range(10)]

    def turned(e, r, h):
        win, at, tags = (T.tb[:, 0:C], T.ls, ["ls"]) if r else (T.tb[:, 0:OWN + C], T.cl, ["cl0", "cl1", "cl8"])
        copy(e, T.sm[:, 240 + 128 * h:368 + 128 * h], win.indirect(at[:, 8 * h:8 * h + 8]), ["tb0", "tb1"] + tags, ["mg%d" % h])

    def stepped(e, h):
        src, tags = (T.e1, ["e1"]) if h < 2 else (T.e0, E0[:6])
        if h == 0: copy(e, T.e0[:, 0:48], T.e1[:, 0:48], ["e1"], E0[6:])
        elif e == "V": vts(T.e0[:, 48:96], src[:, 48:96], ln["small"], None, A.mult, None, tags + ["small"], E0[:6])
        else: act(T.e0[:, 48:96], src[:, 48:96], tags + ["small"], E0[:6], F.Identity, None, ln["small"])

    def positions(r):
        pl = T.pl[:, 32 * r:32 * r + 32]
        if MASKED[r]:
            eo, en, te, tn = (T.e0, T.e1, E0, ["e1"]) if r % 2 == 0 else (T.e1, T.e0, ["e1"], E0)
            turns = T.tb[:, 0:C].indirect(T.ls[:, 0:16]) if r else T.tb[:, 0:OWN + C].indirect(T.cl[:, 0:16])
            yield vtt(T.sm[:, 240:496], turns, T.mk[:, 0:256], A.mult, ["tb0", "tb1", "mk", "mk1", "ls" if r else "cl0", "cl1", "cl8"], ["mg"])
            yield vscan(T.sm[:, 0:240], T.d0r[:, 0:240], T.sm[:, 256:496], 0.0, A.mult, A.add, ["mg", "d0r"], ["sc"])
            yield vtt(en[:, :], T.sm[:, 0:256].indirect(T.tl[:, 0:6]), eo[:, :], A.mult, ["sc", "mg", "tl"] + te, tn)
            yield vscan(T.pp[:, :], T.d0t[:, :], en[:, :], 0.0, A.mult, A.add, tn + ["d0t", "d0t1"], ["pp"])
            vts(pl, T.pp[:, 16:96].indirect(T.tl[:, 6:8]), T.pp[:, 15:16], 256.0, A.add, A.add, ["pp", "tl"], ["pl%d" % r])
            send(T.pa[:, 32 * r:32 * r + 32], pl, "pr%d" % r, partner[r], ["pl%d" % r])
            mark([], ["pa%d" % r], ("pr%d" % r, len(topo.engines(core, partner[r]))))
            yield
        yield turned("V", r, 0)
        yield vscan(T.sm[:, 0:240], T.d0s[:, 0:240], T.sm[:, 256:496], 0.0, A.mult, A.add, ["mg0", "mg1"] + ["d0s%d" % j for j in range(5)], ["sc"])
        yield vtt(T.e1[:, :], T.sm[:, 0:256].indirect(T.tl[:, 0:6]), T.e0[:, :], A.mult, ["sc", "mg0", "tl"] + E0, ["e1"])
        yield vscan(T.pp[:, :], T.d0t[:, :], T.e1[:, :], 0.0, A.mult, A.add, ["e1", "d0t", "d0t1"], ["pp"])
        vts(pl, T.pp[:, 16:96].indirect(T.tl[:, 6:8]), T.pp[:, 15:16], 256.0, A.add, A.add, ["pp", "tl"], ["pl%d" % r])
        send(T.pa[:, 32 * r:32 * r + 32], pl, "pr%d" % r, partner[r], ["pl%d" % r])
        mark([], ["pa%d" % r], ("pr%d" % r, len(topo.engines(core, partner[r]))))
        yield

    def labels(k):
        if k in ROWS: send(T["dr%d" % k][:, :], T.dl[:, :], "lb%d" % k, relay[k] or partner[k], ["dl"])
        elif not SPLIT: send(T.ll[:, 32 * k:32 * k + 32], T.cl[:, 2:34], "lb%d" % k, relay[k] or partner[k], ["cl1", "cl8", "clab", "cl16"])
        else: send(T.ll[:, 0:16], T.cl[:, 2:18], "lb0", partner[0], ["cl1", "cl8", "clab"])
        mark([], ["ll%d" % k], ("lb%d" % k, len(topo.engines(theirs[k] or partner[k], core))))

    def leaves():
        send(T.ll[:, 16:32], T.cl[:, 18:34], "lb3", partner[0], ["cl16"])
        mark([], ["ll3"], ("lb3", len(topo.engines(partner[0], core))))

    def rows():
        moves([(T.dl[16 * h:16 * h + 16, :], T.lt[32 * (h // 2):32 * (h // 2) + 32, 16 * (h % 2):16 * (h % 2) + 16]) for h in range(8)], ["lt"], ["dl"], "dl")

    def laid_out(k):
        moves([(T.lr[j:128:16, 512:1024], T["dr%d" % k][:, :]) for j in range(16)], ["ll%d" % k], ["lr2", "lr3"], "lr%d" % k)

    def spread(e, k, h):
        j = 2 * k + h
        shifted(e, T.lr[:, 256 * j:256 * j + 256], T.it[:, :].indirect(T.ll[:, 16 * j:16 * j + 16]), -C / 2, ["it0", "it1", "it2", "ll%d" % k], ["lr%d" % j])

    def prep(e, r, h):
        shifted(e, T.prep[:, 256 * h:256 * h + 256], T.it[:, 0:520].indirect(T.pl[:, 32 * r + 16 * h:32 * r + 16 * h + 16]), -256.0, ["it0", "it1", "it2", "pl%d" % r], ["prep%d" % h])

    def brep(e, h):
        copy(e, T.brep[:, 160 * h:160 * h + 160], T.prep[:, :].indirect(T.al[:, 10 * h:10 * h + 10]), ["prep0", "prep1", "al"], ["brep%d" % h])

    def zt(r):
        k = 1 if r in ROWS else r
        vcp(T.zt[:, :].indirect(T.pa[:, 32 * r:32 * r + 32]), T.lr[:, 512 * k:512 * k + 512], ["pa%d" % r, "lr%d" % (2 * k), "lr%d" % (2 * k + 1)], ["zt"])

    def placed(): latch(T.bsc[:, :], T.brep[:, :], C, ["brep0", "brep1"], ["bsc"])

    def met(e, h):
        copy(e, T.prep[:, 256 * h:256 * h + 256], T.zt[:, :].indirect(T.pl[:, 16 * h:16 * h + 16]), ["zt", "pl0"], ["prep%d" % h])

    def cut(r, j): return [(0, CUT[r]), (CUT[r], C)][j]

    def mapped(r, i, stage, e="V"):
        c0, c1 = cut(r, i)
        if stage == 0 and r == 0: copy(e, T.mr[:, c0:c1], T.prep[:, :].indirect(T.al[:, c0 // 16:c1 // 16]), ["prep0", "prep1", "al"], ["mr%d" % i])
        if stage == 0 and r > 0: copy(e, T.mr[:, c0:c1], T.zt[:, :].indirect(T.bl[:, c0 // 16:c1 // 16]), ["zt", "bl"], ["mr%d" % i])
        if stage == 1: latch(T.msc[:, c0:c1], T.mr[:, c0:c1], c1 - c0, ["mr%d" % i], ["msc%d" % i])
        if stage == 2: listed(T.ml[:, c0 // 16:c1 // 16], T.msc[:, c0 + 15:c1:16], ["msc%d" % i], ["ml%d" % i], C / 2)

    def mapped_h(r, j, b): return T.aw[:, C * b:C * b + C].indirect(T.ml[:, cut(r, j)[0] // 16:cut(r, j)[1] // 16]), ["aw0.%d" % b, "aw1.%d" % b, "ml%d" % j]

    def picked(e, r, j, b):
        c0, c1 = cut(r, j)
        copy(e, T.ag[:, C * b + c0:C * b + c1], *mapped_h(r, j, b), ["ag%d.%d" % (j, b)])

    def summed(r, j, b):
        (c0, c1), (a, tags) = cut(r, j), mapped_h(r, j, b)
        out = T.xr[:, 4 * c0 + b:4 * c1:4]
        if (j, b) in HELD:
            vtt(out, T.ag[:, C * b + c0:C * b + c1], T.ps[:, 512 * b + c0:512 * b + c1], A.add, ["ag%d.%d" % (j, b), "bank%d" % b], ["xr%d.%d" % (j, b)])
        else:
            vtt(out, a, T.fg[:, C * b + c0:C * b + c1], A.add, tags + ["fg%d" % b], ["xr%d.%d" % (j, b)])

    def made_q(r, i):
        (q, qs), (c0, c1), x = codes(r), runs(r)[i] if r else (160 * i, 160 * i + 160), T.xr if r else T.x0
        quant(q[:, c0:c1], qs[:, c0:c1], x[:, 4 * c0:4 * c1], ["xr%d.%d" % (j, b) for b in range(4) for j in range(2) if cut(r - 1, j)[0] < c1 and c0 < cut(r - 1, j)[1]] if r else ["x0"], [qtags(r)[i]])

    load("Y", T.sei[:, :], T.se[:, :], "sei", "lse")
    op("G", lambda e: e.iota(T.pi[:, :], [[0, 1]], 0, 1), [], ["pi"])
    order("S", ["pi"], [])
    load("S", T.x0[:, :], T.x[:, :], "x0", "lx")
    load("Y", T.wq[:, :].bitcast(dt.uint8), T.wc[:, :], "wq", "lwc")
    load("S", T.wqs[:, :], T.ws[:, :], "wqs", "lws")
    load("Y", T.ub[:, :], T.u[:, :], "ub", "lu")
    order("Y", ["ub"], [])
    load("Y", T.vb[:, :], T.v[:, :], "vb", "lv")

    iota(T.it[:, 0:C], [[1, C]], 0, 0, ["it0"])
    ZZ = ["zz%d" % j for j in range(4)]
    for j in range(3):
        iota(T.zz[:, 1 << j:16:2 << j], [[0, 8 >> j]], 16 << j, 0, [ZZ[j]])
    iota(T.zz[:, 0:16:8], [[-1, 2]], 129, 0, [ZZ[3]])
    iota(T.i16[:, :], [[0, 20], [1, 16]], 0, 0, ["i16"])
    iota(T.p4[:, :], [[0, 1]], -3, -4, ["p4"])
    iota(T.it[:, C:512], [[1, 512 - C]], C, 0, ["it1"])
    FC = ["fc%d" % j for j in range(16)]
    for j, (ap, pat, base) in enumerate((
            (T.fc[:, 132:144:8], [[1, 2]], 0), (T.fc[:, 130:144:4], [[1, 2], [2, 2]], 2), (T.fc[:, 129:144:2], [[1, 2], [2, 2], [4, 2]], 6), (T.fc[:, 128:144:8], [[-1, 2]], 15),
            (T.fc[:, 48:88:5], [[0, 8]], 15), (T.fc[:, 49:88:5], [[16, 2], [0, 4]], 31), (T.fc[:, 50:88:5], [[16, 4], [0, 2]], 63),
            (T.fc[:, 51:88:5], [[16, 8]], 127), (T.fc[:, 52:88:5], [[16, 8]], 127), (T.fc[:, 0:48], [[0, 3], [1, 16]], 240), (T.fc[:, 88:96], [[0, 8]], 0),
            (T.fc[:, 96:98], [[20, 2]], 32), (T.fc[:, 98:102], [[10, 4]], 33), (T.fc[:, 102:110], [[5, 8]], 34),
            (T.fc[:, 110:112], [[-16, 2]], 31), (T.fc[:, 112:128], [[5, 8], [1, 2]], 35))):
        iota(ap, pat, base, 0, [FC[j]])
    for j, (ap, pat, base) in enumerate((
            (T.e0[:, 48:88:5], [[16, 2], [0, 4]], -8), (T.e0[:, 49:88:5], [[0, 2], [8, 2], [0, 2]], -4), (T.e0[:, 50:88:5], [[0, 4], [4, 2]], -2),
            (T.e0[:, 51:88:5], [[0, 8]], -1), (T.e0[:, 52:88:5], [[0, 8]], 2), (T.e0[:, 88:96], [[0, 8]], 0))):
        iota(ap, pat, base, 0, [E0[j]])
    iota(T.ji[:, :], [[16, 16]], 4 * C, 1, ["ji"])
    def firsts():
        iota(T.kr[:, 0:16], [[1, 16]], 224 - 256, 0, ["kr0"])
        iota(T.kr[:, 16:128], [[32, 7], [1, 16]], -256, 0, ["kr1"])
        iota(T.kr[:, 128:256], [[32, 8], [1, 16]], 0, 0, ["kr2"])

    BITS = (15, 8, 4, 2, 1)
    for j, m in enumerate(BITS):
        vts(T.xi[:, j:j + 1], T.pi[:, :], m, None, A.bitwise_and, None, ["pi"], ["xi%d" % m])
    vcp(T.ln[:, 0:5], T.xi[:, 0:5], ["xi%d" % m for m in BITS], ["x%d" % m for m in BITS])
    made = (
        ("mid", "x15", 16.0, 8.0), ("next", "x15", 1.0, 1.0), ("subl", "last", -1024.0, 1024.0), ("way1", "x8", 2.0, "x1"), ("subl0", "last", -1024.0, 768.0), ("subl1", "trash", -8.0 / (2 * C), "subl0"), ("way2", "x4", 8.0, "way1"), ("way", "x2", 32.0, "way2"))
    ln = {n: T.ln[:, j:j + 1] for j, n in enumerate(["x%d" % m for m in BITS] + ["trash", "some", "last", "small"] + [m[0] for m in made])}
    side = {}

    def lane(e, n, x, scale, bias):
        if e == "V": vts(ln[n], ln[x], scale, ln.get(bias, bias), A.mult, A.add, [x, str(bias)], [n])
        else: act(ln[n], ln[x], [x, str(bias)], [n], F.Identity, ln.get(bias, bias), scale)

    def const(e, ap, n, c, w):
        if e == "V": vset(ap, c, w)
        else: act(ap, T.it[:, 0:n], ["it0"], w, F.Identity, c, 0.0)

    for e in "SV":
        side.update({m[0] + e: (lane, e) + m for m in made})
        for n, ap, k, c, w in (("mk1", T.mk[:, 0:16], 16, 1.0, ["mk1"]), ("up0", T.up[:, 14:15], 1, float(OWN), ["up0"]), ("d0t", T.d0t[:, :], 96, 1.0, ["d0t", "d0t1"]),
                               ("d0", T.d0t[:, 48:88:5], 8, 0.0, ["d0t"]), ("d1", T.d0t[:, 0:32:16], 2, 0.0, ["d0t1"]), ("zt0", T.zt[:, 0:513:512], 2, 0.0, ["zt"]), ("z0", T.e0[:, 0:1], 1, 0.0, [E0[6]])):
            side[n + e] = (const, e, ap, k, c, w)
    side.update({
        "trash": (vts, ln["trash"], T.xi[:, 0:1], 0.0, 2.0 * C, A.is_equal, A.mult, ["xi15"], ["trash"]), "some": (vts, ln["some"], T.xi[:, 0:1], 1.0, None, A.min, None, ["xi15"], ["some"]),
        "sv": (act, T.sv[:, :], T.it[:, 0:C], ["it0"], ["sv"], F.Identity, float(OWN)), "it2": (act, T.it[:, OWN:OWN + C], T.it[:, 0:C], ["it0"], ["it2"]),
        "sg": (act, T.sg[:, :], T.it[:, 0:16], ["it0", "mid"], ["sg"], F.Sign, ln["mid"], -16.0), "ad": (act, T.ad[:, :], T.it[:, 0:16], ["it0", "mid"], ["ad"], F.Abs, ln["mid"], -16.0),
        "ull": (vcp, T.ull[:, :], T.it[:, 0:128:16], ["it0"], ["ull"]), "d0r": (act, T.d0r[:, :], T.i16[:, 0:256], ["i16"], ["d0r"], F.Sign),
        "ea": (act, T.ea[:, :], T.it[:, 0:520], ["it0", "it1", "it2", "p4"], ["ea"], F.Abs, T.p4[:, 0:1]), "eb": (act, T.eb[:, :], T.ea[:, :], ["ea"], ["eb"], F.Relu, 0.5, -1.0),
        "kid0": (vcp, T.kid[:, 2 * OWN:2 * OWN + 2 * C:2], T.it[:, 0:C], ["it0"], ["kid0"]), "kid1": (vcp, T.kid[:, 2 * OWN + 1:2 * OWN + 2 * C:2], T.it[:, 0:C], ["it0"], ["kid1"]),
        "ofl0": (vts, T.ofl[:, 0:1], T.sei[:, 0:1], ln["trash"], None, A.add, None, ["sei", "trash"], ["ofl0"]), "ofl": (vcp, T.ofl[:, 1:20], T.sei[:, 1:20], ["sei"], ["ofl"]),
        "kid": (vcp, T.kid[:, 2 * OWN:2 * OWN + 2 * C + 16].indirect(T.ofl[:, 0:20]), T.sv[:, :], ["ofl", "ofl0", "sv"], ["kid0", "kid1"])})
    KID, kid, WO3 = ["kid0", "kid1", "kid2"], T.kid[:, 0:2 * OWN + 2 * C], ["wo3.%d" % c for c in range(4)]

    def pick_u():
        vcp(T.ur[:, 0:128].bitcast(dt.uint32), T.uq[:, 0:128].bitcast(dt.uint32).indirect(T.ull[:, 0:8]), ["uq", "ull"], ["ur"])
        act(T.urs[:, 0:128], T.us[:, 0:128].indirect(T.ull[:, 0:8]), ["uq", "ull"], ["urs"])

    def tiles(b): quant(T.eq[:, 128 * b:128 * b + 128], T.es[:, 128 * b:128 * b + 128], T.eb[:, 3 - b:515 - b], ["eb"], ["eq%d" % b])

    def parents():
        for b in range(4): vts(T.parl[:, 20 * b:20 * b + 20], T.ai[:, :], 4.0, float(b), A.mult, A.add, ["ai"], ["par%d" % b])

    def pair(at, y, r, n):
        vts(T.wv[:, at:at + 2 * n:2], y, 2.0, None, A.mult, None, r, ["wv%da" % at])
        vts(T.wv[:, at + 1:at + 2 * n:2], y, 2.0, 1.0, A.mult, A.add, r, ["wv%db" % at])

    side.update({
        "qu": (quant, T.uq[:, :], T.us[:, :], T.ub[:, :], ["ub"], ["uq"]),
        "pu": (pick_u,),
        "ai": (vts, T.ai[:, :], T.sei[:, :], 1, None, A.arith_shift_right, None, ["sei"], ["ai"]), "par": (parents,),
        "up1": (vts, T.up[:, 0:6], T.wo[:, 0:12:2], ln["x1"], 0.5, A.subtract, A.mult, ["wo1", "wo2.0", "wo2.1", "x1"], ["up1"]),
        "up3": (vts, T.up[:, 6:14], T.wo[:, 68:76], ln["x1"], 0.5, A.subtract, A.mult, WO3 + ["x1"], ["up3"]),
        "one": (vts, T.one[:, :], T.it[:, 0:15], ln["subl"], T.fs[:, 143:144], A.add, A.is_equal, ["it0", "subl", "fs"], ["one"]),
        "upm": (vtt, T.upm[:, :], T.up[:, :], T.one[:, :], A.mult, ["up0", "up1", "up3", "one"], ["upm"]), "top": (vred, T.yt[:, 1:2], T.upm[:, :], ["upm"], ["top"]),
        "cl0": (vcp, T.cl[:, 0:1], T.yt[:, 1:2], ["top"], ["cl0"]), "wu": (pair, 16, T.yt[:, 1:2], ["top"], 1),
        "clab": (vts, T.cl[:, 16:18], T.gs[:, 239:256:16], ln["some"], None, A.mult, None, ["gs4", "some"], ["clab"]),
        "m4": (vts, T.m4[:, :], T.it[:, 0:128], ln["way"], None, A.is_equal, None, ["it0", "way"], ["m4"]),
        "mk": (vts, T.mk[:, 16:336], T.i16[:, :], ln["x15"], None, A.is_equal, None, ["i16", "x15"], ["mk"]),
        "d0a": (vts, T.d0a[:, 0:16], T.it[:, 0:16], ln["x15"], -4096.0, A.is_equal, A.mult, ["it0", "x15"], ["d0a"]),
        "d0b": (vts, T.d0a[:, 16:32], T.it[:, 0:16], ln["next"], 1024.0, A.is_equal, A.mult, ["it0", "next"], ["d0b"]),
        "d0l": (vtt, T.d0l[:, 0:16], T.d0a[:, 0:16], T.d0a[:, 16:32], A.add, ["d0a", "d0b"], ["d0l0"]),
        **{"d%d%s" % (n, e): (copy, e, T.d0l[:, n:min(2 * n, C)], T.d0l[:, 0:min(n, C - n)], ["d0l%d" % i for i in range(j + 1)], ["d0l%d" % (j + 1)]) for j, n in enumerate((16, 32, 64, 128, 256)) for e in "SV"},
        "last": (vts, ln["last"], T.xi[:, 0:1], 15.0, None, A.is_equal, None, ["xi15"], ["last"]), "small": (vts, ln["small"], ln["last"], 1.0 / BIG, None, A.max, None, ["last"], ["small"]),
        "s0a": (vts, T.d0a[:, 32:48], T.it[:, 0:16], ln["next"], BIG, A.is_equal, A.mult, ["it0", "next"], ["s0a"]),
        "s0b": (vts, T.d0a[:, 48:64], T.it[:, 0:16], ln["x15"], None, A.not_equal, None, ["it0", "x15"], ["s0b"]),
        "d0s": (vtt, T.d0s[:, 0:16], T.d0a[:, 32:48], T.d0a[:, 48:64], A.max, ["s0a", "s0b"], ["d0s0"]),
        **{"s%d%s" % (16 << j, e): (copy, e, T.d0s[:, 16 << j:32 << j], T.d0s[:, 0:16 << j], ["d0s%d" % i for i in range(j + 1)], ["d0s%d" % (j + 1)]) for j in range(4) for e in "SV"},
        "an": (vtt, T.an[:, :], T.ad[:, :], T.zz[:, :], A.is_lt, ["ad"] + ZZ, ["an"]), "w1": (vtt, T.w1[:, :], T.sg[:, :], T.zz[:, :], A.mult, ["sg"] + ZZ, ["w1"]),
        "down": (vtt, T.e0[:, 0:16], T.w1[:, :], T.an[:, :], A.mult, ["w1", "an"], [E0[6]]),
        "cl1": (vts, T.cl[:, 1:8], T.wv[:, 2:16:2], 0.5, None, A.mult, None, ["wv2a", "wv4a", "wv8a"], ["cl1"]),
        "zl": (vtt, T.zl[:, :], T.zz[:, :], T.mk[:, 16:32], A.mult, ZZ + ["mk"], ["zl"]), "zr": (vred, T.zr[:, :], T.zl[:, :], ["zl"], ["zr"]),
        "tm": (vts, T.tm[:, :], T.zz[:, :], T.zr[:, 0:1], -1.0, A.is_lt, A.mult, ZZ + ["zr"], ["tm"]),
        "back": (vtt, T.e0[:, 16:32], T.e0[:, 0:16], T.tm[:, :], A.mult, [E0[6], "tm"], [E0[7]]),
        "own": (vts, T.e0[:, 32:48], T.zl[:, :], -2.0, -256.0, A.mult, A.max, ["zl"], [E0[8]]),
        "s1": (vts, T.s1[:, :], T.sei[:, :], 1, None, A.bitwise_and, None, ["sei"], ["s1"]),
        "st": (vts, T.st[:, 1:20], T.s1[:, 1:20], 16.0, ln["subl0"], A.mult, A.subtract, ["s1", "subl0"], ["st"]),
        "st0": (vts, T.st[:, 0:1], T.s1[:, 0:1], 16.0, ln["subl1"], A.mult, A.subtract, ["s1", "subl1"], ["st0"]),
        "lc": (vts, T.lc[:, :], T.cj[:, 2:34], -C / 2, None, A.add, None, ["cj"], ["lc"]), "lt": (op, "V", lambda e: e.transpose(T.lt[:, :], T.lc[:, :]), ["lc"], ["lt"]),
        "rows": (rows,), "out1": (laid_out, 1), "out2": (laid_out, 2),
        "ci": (vcp, T.ci[:, :], T.cl[:, :], ["cl0", "cl1", "cl8", "cl16", "clab"], ["ci"]), "cj": (vts, T.cj[:, :], T.ci[:, :], OWN - 1, None, A.bitwise_and, None, ["ci"], ["cj"]),
        "ls": (vcp, T.ls[:, :], T.cj[:, 0:16], ["cj"], ["ls"]),
        "fs": (latch, T.fs[:, :], T.fc[:, :], 144, FC, ["fs"]), "tl": (listed, T.tl[:, :], T.fs[:, 15:128:16], ["fs"], ["tl"])})
    side.update({"t%d" % b: (tiles, b) for b in range(4)})

    def tree():
        vts(T.wo[:, 0:4:2], T.kid[:, 2 * OWN:2 * OWN + 2], 2.0, ln["x1"], A.mult, A.add, ["kid0", "kid1", "x1"], ["wo1"])
        yield vts(T.kid[:, 0:2 * C], T.kid[:, 2 * OWN:2 * OWN + 2 * C], OWN - 1, None, A.bitwise_and, None, ["kid0", "kid1"], ["kid2"])
        for c in range(2): vts(T.wo[:, 4 + 2 * c:68:4], kid.indirect(T.wo[:, 2 * c:2 * c + 1]), 2.0, ln["x1"], A.mult, A.add, KID + ["wo1", "x1"], ["wo2.%d" % c])
        yield
        for c in range(4): vts(T.wo[:, 68 + c:132:4], kid.indirect(T.wo[:, 4 + 2 * c:5 + 2 * c]), 2.0, ln["x1"], A.mult, A.add, KID + ["wo2.%d" % (c % 2), "x1"], ["wo3.%d" % c])
        yield
        yield vtt(T.g4[:, :], kid.indirect(T.wo[:, 68:76]), T.m4[:, :], A.mult, KID + WO3 + ["m4"], ["g4"])
        yield vscan(T.g5[:, :], T.g4[:, :], T.g4[:, :], 0.0, A.max, A.max, ["g4"], ["yt"])
        yield pair(2, T.g5[:, 127:128], ["yt"], 1)
        for n in (1, 2, 4, 8): yield from below(n)

    def below(n):
        a, b = {1: (2, 4), 2: (4, 8), 4: (8, 18), 8: (18, 34)}[n]
        h, k = 16 * a - 32, 16 * (b - a)
        if n == 8 and LEAVES == "S":
            yield act(T.lg[:, :], kid.indirect(T.wv[:, a:b]), KID + ["wv18a", "wv18b"], ["gg8"])
            yield latch(T.lf[:, :], T.lg[:, :], k, ["gg8"], ["gs8"])
            yield listed(T.cl[:, 18:34], T.lf[:, 15:k:16], ["gs8"], ["cl16"])
        yield vtt(T.gg[:, h:h + k], kid.indirect(T.wv[:, a:b]), T.mk[:, 16:16 + k], A.mult, KID + ["wv%d%s" % (j, c) for j in (a, b - 2 * (n == 4)) for c in "ab"] + ["mk"], ["gg%d" % n])
        yield vscan(T.gs[:, h:h + k], T.d0r[:, 0:k], T.gg[:, h:h + k], 0.0, A.mult, A.add, ["gg%d" % n, "d0r"], ["gs%d" % n])
        y = T.gs[:, h + 15:h + 32 * n:16]
        if n < 8: pair(b, y, ["gs%d" % n], 2 * n)
        if n >= 4: vcp(T.cl[:, 2 * n:4 * n], y, ["gs%d" % n], ["cl%d" % (2 * n)])
        yield

    side.update({
        "*": (next, tree()), "lab0": (labels, 0), "lab3": (leaves,), "kr": (firsts,), **{"sg2" + e: (copy, e, T.tb[:, OWN:OWN + C], T.tb[:, 0:C], ["tb0"], ["tb1"]) for e in "SV"}, "lab1": (labels, 1), "lab2": (labels, 2),
        "yf": (vts, T.yf[:, :], T.cl[:, 0:16], 4.0, None, A.mult, None, ["cl0", "cl1", "cl8"], ["yf"]),
        "o16": (vtt, T.o16[:, :], T.yf[:, :], T.ji[:, :], A.max, ["yf", "ji"], ["o16"]), "ol": (vcp, T.ol[:, :], T.o16[:, :], ["o16"], ["ol"]),
        "at": (vcp, T.at[:, :].indirect(T.ol[:, 0:16]), T.kr[:, :], ["ol", "kr0", "kr1", "kr2"], ["at"]),
        "als": (latch, T.als[:, :], T.ar[:, :], C, ["ar0", "ar1"], ["als"]),
        "af": (vtt, T.af[:, :], T.als[:, 15:C:16], T.st[:, :], A.add, ["als", "st", "st0"], ["af"]), "al": (vcp, T.al[:, :], T.af[:, :], ["af"], ["al"]),
        "vq": (quant, T.vq[:, :], T.vs[:, :], T.vb[:, :], ["vb"], ["vq"])})

    def beside(e, h): copy(e, T.ar[:, 160 * h:160 * h + 160], T.at[:, 4 * OWN:4 * (OWN + C)].indirect(T.parl[:, 10 * h:10 * h + 10]), ["at", "par0"], ["ar%d" % h])

    def out(i, e):
        (c0, c1), t = runs(3)[i], "q1.%d" % i
        mm(4 + i, T.vq[:, 0:128], T.vs[:, 0:128], T.q1[:, c0:c1], T.qs1[:, c0:c1], [t, "vq"], c1 - c0)
        copy(e, T.ysb[:, c0:c1], bank(4 + i, c1 - c0), ["bank%d" % (4 + i)], ["ysb%d" % i])
        store("S", T.y[:, c0:c1], T.ysb[:, c0:c1], ["ysb%d" % i])

    def out_codes(i):
        c0, c1 = runs(3)[i]
        store("Y", T.oc[:, 4 * c0:4 * c1], T.q1[:, c0:c1].bitcast(dt.uint8), ["q1.%d" % i])

    def out_scales():
        for k in range(4): store("Y", T.osc[4 * k:4 * k + 4, :], T.qs1[32 * k:32 * k + 4, :], ["q1.0", "q1.1"])

    for r in range(4):
        step = {"pos": (next, positions(r)), "tnS": (turned, "S", r, 1), "tnV": (turned, "V", r, 1), **{"step%d%s" % (h, e): (stepped, e, h) for h in range(3) for e in "SV"}, "pq0": (requant, 0), "pq1": (requant, 1), "oc0": (out_codes, 0), "oc1": (out_codes, 1), "osc": (out_scales,), "above": (above, r), "zt": (zt, r), "bsc": (placed,), "bl": (listed, T.bl[:, :], T.bsc[:, 15:C:16], ["bsc"], ["bl"], 256.0),
                "im": (store, "Y", T.im[:, :], T.mf[0:128:16, :], ["mf"]), **{"mf" + e: (shifted, e, T.mf[:, :], T.mr[:, :], C / 2, ["mr0", "mr1"], ["mf"]) for e in "SV"}}
        for i in range(2):
            step.update({"q%d" % i: (made_q, r, i), "layer%d" % i: (layer, r, i), "sc%d" % i: (scores, r, i), "sg%d" % i: (signs, r, i), "pack%d" % i: (pack, r, i), "post%d" % i: (post, r, i),
                         "un%d" % i: (arrived, r, i), "msc%d" % i: (mapped, r, i, 1), "ml%d" % i: (mapped, r, i, 2)})
            step.update({"x%d%d" % (i, b): (summed, r - 1, i, b) for b in range(4)})
            for e in "SV":
                step.update({"lr%d%s" % (i, e): (spread, e, r, i), "next%d%s" % (i, e): (spread, e, r + 1, i), "prep%d%s" % (i, e): (prep, e, r, i), "brep%d%s" % (i, e): (brep, e, i),
                             "ar%d%s" % (i, e): (beside, e, i), "mr%d%s" % (i, e): (mapped, r, i, 0, e), "met%d%s" % (i, e): (met, e, i), "k%d%s" % (i, e): (kept, e, r, i),
                             "out%d%s" % (i, e): (out, i, e)})
                for b in range(4):
                    step.update({"h%d%d%s" % (i, b, e): (scaled, e, r, i, b), "g%d%d%s" % (i, b, e): (halved, e, i, b), "xp%d%d%s" % (b, i, e): (laid, e, r, b, i), "aw%d%d%s" % (i, b, e): (taken, e, r, i, b), "ag%d%d%s" % (i, b, e): (picked, e, r - 1, i, b)})
        for n in ROUNDS[r if r in (0, 3) else 1 if relay[r] is None else 2].split():
            f = step.get(n) or side[n]
            f[0](*f[1:])
    for k in ("V", "S", "T", "G"):
        wait("G", ("c" + k, cnt[k]))
    g.wait_ge(T.sem.stored, stores[0])
    g.wait_ge(T.sem.sent, sent[0])
